import numpy as np
import ml_dtypes


def mxq(x, axis, fmt="e4m3"):
    dtype, down = {"e4m3": (ml_dtypes.float8_e4m3fn, 7), "e5m2": (ml_dtypes.float8_e5m2, 14)}[fmt]
    v = np.moveaxis(np.asarray(x, np.float32).astype(ml_dtypes.bfloat16).astype(np.float64), axis, -1)
    blocks = v.reshape(v.shape[:-1] + (-1, 32))
    amax = np.abs(blocks).max(-1, keepdims=True)
    byte = np.maximum(np.where(amax > 0, np.frexp(amax)[1] - 1 + 127, 0) - down, 1)
    scale = np.exp2(byte - 127.0)
    codes = (blocks / scale).astype(np.float32).astype(dtype).astype(np.float64)
    return np.moveaxis((codes * scale).reshape(v.shape), -1, axis)


WIDE = False


def mx_kscale(k):
    if not WIDE:
        return np.ones(k)
    levels = np.array([10, -10, 5, -5, 0])
    if k % 512:
        return np.exp2(np.random.permutation(np.resize(levels, k // 32))).repeat(32)
    a = np.empty((k // 512, 16))
    for p in range(k // 512):
        a[p, :8] = np.random.permutation(np.resize(levels, 8))
        for g in range(8):
            far = levels[np.abs(levels - a[p, g]) >= 10]
            a[p, g + 8] = far[np.random.randint(len(far))]
    return np.exp2(a.ravel()).repeat(32)


BF16 = ml_dtypes.bfloat16


def bf(x):
    return np.asarray(x, np.float32).astype(BF16)


def f64(x):
    return np.asarray(x).astype(np.float64)

E4M3FN = np.array([(-1.0 if i & 128 else 1.0) * ((1.0 + (i & 7) / 8.0) * 2.0 ** (((i >> 3) & 15) - 7) if i & 120 else (i & 7) * 2.0 ** -9) for i in range(256)])


def e4m3fn_bytes(y):
    return np.clip(np.asarray(y, np.float64), -448.0, 448.0).astype(np.float32).astype(ml_dtypes.float8_e4m3fn).view(np.uint8)


def e4m3fn_values(b):
    return E4M3FN[b]


F, T, N = 1024, 8192, 128


def setup_inputs():
    s = mx_kscale(F)
    level = np.exp(0.7 * np.random.standard_normal((F, 1)))
    loud = np.exp(0.7 * np.random.standard_normal((1, T)))
    P = np.random.standard_exponential((F, T)) * level * loud * s[:, None]
    P_scale = (np.max(np.abs(P), axis=1, keepdims=True) / 448.0).astype(np.float32)
    P_bytes = e4m3fn_bytes(P / f64(P_scale))
    freq = (np.arange(F) + 0.5) / F
    c = (64.0 ** ((np.arange(N) + 0.5) / N) - 1.0) / 63.0
    half = 1.0 / N + 0.1 * c
    tri = np.maximum(0.0, 1.0 - np.abs(freq[None, :] - c[:, None]) / half[:, None])
    tri = tri * (0.5 + np.random.random_sample((N, F)))
    W = tri / np.sum(tri, axis=1, keepdims=True) + 0.3 * (0.5 + np.random.random_sample((N, F))) / F
    return {"P_bytes": P_bytes,
            "P_scale": P_scale,
            "W": bf(W / s[None, :]),
            "floor": bf(0.1 + 0.2 * np.random.random_sample(N)),
            "gain": bf(1.0 + 0.1 * np.random.standard_normal(N)),
            "bias": bf(0.3 * np.random.standard_normal(N))}


def reference(P_bytes, P_scale, W, floor, gain, bias):
    P = e4m3fn_values(P_bytes) * np.repeat(f64(P_scale), T, axis=1)
    mel = mxq(f64(W), 1, "e4m3") @ mxq(P, 0, "e4m3")
    logmel = np.log(mel + f64(floor)[:, None])
    return logmel * f64(gain)[:, None] + f64(bias)[:, None]

@@ -1,0 +1,166 @@
+from contextlib import ExitStack
+
+import concourse.mybir as mybir
+from concourse.masks import make_identity
+
+F, T, N = 1024, 8192, 128
+FLOPS = 2 * F * T * N
+
+F32 = mybir.dt.float32
+BF16 = mybir.dt.bfloat16
+U32 = mybir.dt.uint32
+U8 = mybir.dt.uint8
+FP8 = mybir.dt.float8_e4m3fn
+FP8X4 = mybir.dt.float8_e4m3fn_x4
+ACT = mybir.ActivationFunctionType
+ALU = mybir.AluOpType
+
+P = 128
+PACK = 4
+PASSES = F // (P * PACK)
+BANK = 512
+CHUNKS = [256,256,512,1024,1024,1024,1024,1024,1024,512,256,256]
+VPLANES = [2,1,1,1,1,1,1,1,1,0,1,1,1,1,0,1,1,1,1,1,1,1,1,1]
+assert sum(CHUNKS) == T
+
+
+def tile_fp8_log_mel_d3_kernel(tc, P_bytes, P_scale, W, floor, gain, bias, out):
+    nc = tc.nc
+    starts = [sum(CHUNKS[:c]) for c in range(len(CHUNKS))]
+    units = len(CHUNKS) * PASSES
+
+    with ExitStack() as ctx:
+        keep = ctx.enter_context(tc.tile_pool(name="keep", bufs=1))
+        work = ctx.enter_context(tc.tile_pool(name="work", bufs=3))
+        psum_w = ctx.enter_context(tc.psum_pool(name="psum_w", bufs=1))
+        psum = ctx.enter_context(tc.psum_pool(name="psum", bufs=6))
+        ctx.enter_context(tc.manual_schedule())
+
+        p_rows = P_bytes.rearrange("(g p t) n -> g p t n", p=P, t=PACK)
+        raw = {}
+
+        def load(u):
+            c, g = divmod(u, PASSES)
+            raw[u] = keep.tile([P, PACK, CHUNKS[c]], U8, name="p_bytes_%d" % u)
+            nc.sync.dma_start(out=raw[u][:], in_=p_rows[g][:, :, starts[c] : starts[c] + CHUNKS[c]])
+
+        row_scale = keep.tile([P, PASSES, PACK], F32)
+        nc.sync.dma_start(out=row_scale[:], in_=P_scale.rearrange("(g p t) o -> p g (t o)", p=P, t=PACK))
+        load(0)
+        load(1)
+        w_rows = keep.tile([P, F], BF16, align_bytes=64)
+        nc.sync.dma_start(out=w_rows[:], in_=W)
+        load(2)
+        load(3)
+        floor_col = keep.tile([P, 1], BF16)
+        gain_col = keep.tile([P, 1], BF16)
+        bias_col = keep.tile([P, 1], BF16)
+        nc.gpsimd.dma_start(out=floor_col[:], in_=floor.rearrange("(p o) -> p o", o=1))
+        nc.gpsimd.dma_start(out=gain_col[:], in_=gain.rearrange("(p o) -> p o", o=1))
+        nc.gpsimd.dma_start(out=bias_col[:], in_=bias.rearrange("(p o) -> p o", o=1))
+        for u in range(4, units):
+            load(u)
+
+        one = keep.tile([P, 1], F32)
+        warm = keep.tile([P, 1], F32)
+        nc.vector.memset(one[:], 1.0)
+        nc.scalar.activation(out=warm[:], in_=one[:], func=ACT.Ln)
+
+        ident = keep.tile([P, P], F32)
+        make_identity(nc, ident[:])
+
+        w_codes = keep.tile([P, PASSES * N], U32, align_bytes=64)
+        w_scales = keep.tile([P, PASSES * N], U8, align_bytes=64)
+        w_grouped = keep.tile([P, PASSES * N * PACK], BF16, align_bytes=64)
+
+        def turn_w():
+            words = w_rows[:].bitcast(F32)
+            turned = psum_w.tile([P, PASSES, 2, N], F32)
+            for g in range(PASSES):
+                for h in range(2):
+                    nc.tensor.transpose(turned[:, g, h, :], words[:, 256 * g + h : 256 * (g + 1) : 2], ident[:])
+            nc.scalar.copy(
+                out=w_grouped[:].bitcast(F32).rearrange("p (g m h) -> p g m h", g=PASSES, h=2),
+                in_=turned[:].rearrange("p g h m -> p g m h"),
+            )
+
+        def quantize_w():
+            nc.vector.quantize_mx(out=w_codes[:].bitcast(FP8X4), scales=w_scales[:], in_=w_grouped[:])
+
+        wide, grouped, codes, scales, mel, logs = {}, {}, {}, {}, {}, {}
+
+        def widen(u, on_vector):
+            c, g = divmod(u, PASSES)
+            if u not in wide:
+                wide[u] = work.tile([P, PACK, CHUNKS[c]], BF16, name="wide", bufs=4)
+            planes = range(PACK - VPLANES[u], PACK) if on_vector else range(PACK - VPLANES[u])
+            for t in planes:
+                src = raw[u][:, t, :].bitcast(FP8)
+                if on_vector:
+                    nc.vector.tensor_scalar(out=wide[u][:, t, :], in0=src, scalar1=row_scale[:, g, t : t + 1], scalar2=None, op0=ALU.mult)
+                else:
+                    nc.scalar.activation(out=wide[u][:, t, :], in_=src, func=ACT.Copy, scale=row_scale[:, g, t : t + 1])
+
+        def interleave(u):
+            width = CHUNKS[u // PASSES]
+            grouped[u] = work.tile([P, width, PACK], BF16, name="grouped", align_bytes=64)
+            nc.vector.tensor_copy(
+                out=grouped[u][:].rearrange("p (c i) t -> p c t i", i=4),
+                in_=wide[u][:].rearrange("p t (c i) -> p c t i", i=4),
+            )
+
+        def quantize(u):
+            width = CHUNKS[u // PASSES]
+            codes[u] = work.tile([P, width], U32, name="codes", align_bytes=64, bufs=4)
+            scales[u] = work.tile([P, width], U8, name="scales", align_bytes=64, bufs=4)
+            nc.vector.quantize_mx(out=codes[u][:].bitcast(FP8X4), scales=scales[u][:], in_=grouped[u][:].rearrange("p n t -> p (n t)"))
+
+        def spans(c):
+            return [slice(n0, min(n0 + BANK, CHUNKS[c])) for n0 in range(0, CHUNKS[c], BANK)]
+
+        def multiply(c):
+            mel[c] = []
+            for cols in spans(c):
+                acc = psum.tile([P, cols.stop - cols.start], F32, name="mel")
+                mel[c].append(acc)
+                for g in range(PASSES):
+                    u = PASSES * c + g
+                    nc.tensor.matmul_mx(
+                        out=acc[:],
+                        lhsT=w_codes[:, g * N : (g + 1) * N].bitcast(FP8X4),
+                        lhsT_scale=w_scales[:, g * N : (g + 1) * N],
+                        rhs=codes[u][:, cols].bitcast(FP8X4),
+                        rhs_scale=scales[u][:, cols],
+                        start=(g == 0),
+                        stop=(g == PASSES - 1),
+                    )
+
+        def logarithm(c):
+            logs[c] = work.tile([P, CHUNKS[c]], F32, name="logs")
+            for acc, cols in zip(mel[c], spans(c)):
+                nc.scalar.activation(out=logs[c][:, cols], in_=acc[:], func=ACT.Ln, bias=floor_col[:])
+
+        def finish(c):
+            res = work.tile([P, CHUNKS[c]], F32, name="res")
+            nc.vector.tensor_scalar(out=res[:], in0=logs[c][:], scalar1=gain_col[:], scalar2=bias_col[:], op0=ALU.mult, op1=ALU.add)
+            nc.sync.dma_start(out=out[:, starts[c] : starts[c] + CHUNKS[c]], in_=res[:])
+
+        widen(0, True)
+        widen(0, False)
+        for s in range(units + 3):
+            if s < units:
+                interleave(s)
+            if s + 1 < units:
+                widen(s + 1, True)
+                widen(s + 1, False)
+            if s == 1:
+                turn_w()
+            if 1 <= s <= units:
+                quantize(s - 1)
+            if s == 2:
+                quantize_w()
+            if s >= 4 and s % 2 == 0:
+                finish(s // 2 - 2)
+            if 2 <= s <= units and s % 2 == 0:
+                multiply(s // 2 - 1)
+                logarithm(s // 2 - 1)

@@ -19,8 +19,8 @@ P = 128
 PACK = 4
 PASSES = F // (P * PACK)
 BANK = 512
-CHUNKS = [256,256,512,1024,1024,1024,1024,1024,1024,512,256,256]
-VPLANES = [2,1,1,1,1,1,1,1,1,0,1,1,1,1,0,1,1,1,1,1,1,1,1,1]
+CHUNKS = [256,256,512,1024,1024,1024,1024,1024,1024,512,256,128,128]
+VPLANES = [3,1,2,2,2,2,2,1,1,1,1,1,1,1,0,0,0,0,0,0,0,0,0,0,0,0]
 assert sum(CHUNKS) == T
 
 
@@ -33,7 +33,7 @@ def tile_fp8_log_mel_d3_kernel(tc, P_bytes, P_scale, W, floor, gain, bias, out):
         keep = ctx.enter_context(tc.tile_pool(name="keep", bufs=1))
         work = ctx.enter_context(tc.tile_pool(name="work", bufs=3))
         psum_w = ctx.enter_context(tc.psum_pool(name="psum_w", bufs=1))
-        psum = ctx.enter_context(tc.psum_pool(name="psum", bufs=6))
+        psum = ctx.enter_context(tc.psum_pool(name="psum", bufs=7))
         ctx.enter_context(tc.manual_schedule())
 
         p_rows = P_bytes.rearrange("(g p t) n -> g p t n", p=P, t=PACK)
@@ -45,7 +45,7 @@ def tile_fp8_log_mel_d3_kernel(tc, P_bytes, P_scale, W, floor, gain, bias, out):
             nc.sync.dma_start(out=raw[u][:], in_=p_rows[g][:, :, starts[c] : starts[c] + CHUNKS[c]])
 
         row_scale = keep.tile([P, PASSES, PACK], F32)
-        nc.sync.dma_start(out=row_scale[:], in_=P_scale.rearrange("(g p t) o -> p g (t o)", p=P, t=PACK))
+        nc.scalar.dma_start(out=row_scale[:], in_=P_scale.rearrange("(g p t) o -> p g (t o)", p=P, t=PACK))
         load(0)
         load(1)
         w_rows = keep.tile([P, F], BF16, align_bytes=64)
@@ -55,9 +55,9 @@ def tile_fp8_log_mel_d3_kernel(tc, P_bytes, P_scale, W, floor, gain, bias, out):
         floor_col = keep.tile([P, 1], BF16)
         gain_col = keep.tile([P, 1], BF16)
         bias_col = keep.tile([P, 1], BF16)
-        nc.gpsimd.dma_start(out=floor_col[:], in_=floor.rearrange("(p o) -> p o", o=1))
-        nc.gpsimd.dma_start(out=gain_col[:], in_=gain.rearrange("(p o) -> p o", o=1))
-        nc.gpsimd.dma_start(out=bias_col[:], in_=bias.rearrange("(p o) -> p o", o=1))
+        nc.sync.dma_start(out=floor_col[:], in_=floor.rearrange("(p o) -> p o", o=1))
+        nc.sync.dma_start(out=gain_col[:], in_=gain.rearrange("(p o) -> p o", o=1))
+        nc.sync.dma_start(out=bias_col[:], in_=bias.rearrange("(p o) -> p o", o=1))
         for u in range(4, units):
             load(u)
 
@@ -68,6 +68,8 @@ def tile_fp8_log_mel_d3_kernel(tc, P_bytes, P_scale, W, floor, gain, bias, out):
 
         ident = keep.tile([P, P], F32)
         make_identity(nc, ident[:])
+        gain_f32 = keep.tile([P, 1], F32)
+        nc.gpsimd.tensor_copy(out=gain_f32[:], in_=gain_col[:])
 
         w_codes = keep.tile([P, PASSES * N], U32, align_bytes=64)
         w_scales = keep.tile([P, PASSES * N], U8, align_bytes=64)
@@ -142,25 +144,31 @@ def tile_fp8_log_mel_d3_kernel(tc, P_bytes, P_scale, W, floor, gain, bias, out):
 
         def finish(c):
             res = work.tile([P, CHUNKS[c]], F32, name="res")
-            nc.vector.tensor_scalar(out=res[:], in0=logs[c][:], scalar1=gain_col[:], scalar2=bias_col[:], op0=ALU.mult, op1=ALU.add)
+            if c >= len(CHUNKS) - 3:
+                nc.scalar.activation(out=res[:], in_=logs[c][:], func=ACT.Identity, scale=gain_f32[:], bias=bias_col[:])
+            else:
+                nc.vector.tensor_scalar(out=res[:], in0=logs[c][:], scalar1=gain_col[:], scalar2=bias_col[:], op0=ALU.mult, op1=ALU.add)
             nc.sync.dma_start(out=out[:, starts[c] : starts[c] + CHUNKS[c]], in_=res[:])
 
-        widen(0, True)
         widen(0, False)
-        for s in range(units + 3):
+        widen(1, False)
+        widen(0, True)
+        for s in range(units + 5):
             if s < units:
                 interleave(s)
             if s + 1 < units:
                 widen(s + 1, True)
-                widen(s + 1, False)
+            if s + 2 < units:
+                widen(s + 2, False)
             if s == 1:
                 turn_w()
             if 1 <= s <= units:
                 quantize(s - 1)
             if s == 2:
                 quantize_w()
-            if s >= 4 and s % 2 == 0:
-                finish(s // 2 - 2)
             if 2 <= s <= units and s % 2 == 0:
                 multiply(s // 2 - 1)
-                logarithm(s // 2 - 1)
+            if s >= 4 and (s - 4) % 2 == 0 and (s - 4) // 2 < len(CHUNKS):
+                logarithm((s - 4) // 2)
+            if s >= 5 and (s - 5) % 2 == 0 and (s - 5) // 2 < len(CHUNKS):
+                finish((s - 5) // 2)

@@ -20,7 +20,9 @@ PACK = 4
 PASSES = F // (P * PACK)
 BANK = 512
 CHUNKS = [256,256,512,1024,1024,1024,1024,1024,1024,512,256,128,128]
-VPLANES = [3,1,2,2,2,2,2,1,1,1,1,1,1,1,0,0,0,0,0,0,0,0,0,0,0,0]
+VPLANES = [3,1,2,2,2,2,1,1,1,1,1,1,1,1,1,1,1,1,0,0,0,0,0,0,0,0]
+ON_TENSOR = [6,8,10,12,14,16]
+TENSOR_FRAMES = 256
 assert sum(CHUNKS) == T
 
 
@@ -32,8 +34,8 @@ def tile_fp8_log_mel_d3_kernel(tc, P_bytes, P_scale, W, floor, gain, bias, out):
     with ExitStack() as ctx:
         keep = ctx.enter_context(tc.tile_pool(name="keep", bufs=1))
         work = ctx.enter_context(tc.tile_pool(name="work", bufs=3))
-        psum_w = ctx.enter_context(tc.psum_pool(name="psum_w", bufs=1))
-        psum = ctx.enter_context(tc.psum_pool(name="psum", bufs=7))
+        psum_w = ctx.enter_context(tc.psum_pool(name="psum_w", bufs=2))
+        psum = ctx.enter_context(tc.psum_pool(name="psum", bufs=6))
         ctx.enter_context(tc.manual_schedule())
 
         p_rows = P_bytes.rearrange("(g p t) n -> g p t n", p=P, t=PACK)
@@ -68,8 +70,8 @@ def tile_fp8_log_mel_d3_kernel(tc, P_bytes, P_scale, W, floor, gain, bias, out):
 
         ident = keep.tile([P, P], F32)
         make_identity(nc, ident[:])
-        gain_f32 = keep.tile([P, 1], F32)
-        nc.gpsimd.tensor_copy(out=gain_f32[:], in_=gain_col[:])
+        ident_bf16 = keep.tile([P, P], BF16)
+        make_identity(nc, ident_bf16[:])
 
         w_codes = keep.tile([P, PASSES * N], U32, align_bytes=64)
         w_scales = keep.tile([P, PASSES * N], U8, align_bytes=64)
@@ -77,7 +79,7 @@ def tile_fp8_log_mel_d3_kernel(tc, P_bytes, P_scale, W, floor, gain, bias, out):
 
         def turn_w():
             words = w_rows[:].bitcast(F32)
-            turned = psum_w.tile([P, PASSES, 2, N], F32)
+            turned = psum_w.tile([P, PASSES, 2, N], F32, name="turned")
             for g in range(PASSES):
                 for h in range(2):
                     nc.tensor.transpose(turned[:, g, h, :], words[:, 256 * g + h : 256 * (g + 1) : 2], ident[:])
@@ -103,13 +105,36 @@ def tile_fp8_log_mel_d3_kernel(tc, P_bytes, P_scale, W, floor, gain, bias, out):
                 else:
                     nc.scalar.activation(out=wide[u][:, t, :], in_=src, func=ACT.Copy, scale=row_scale[:, g, t : t + 1])
 
+        moved = {}
+
+        def new_grouped(u):
+            if u not in grouped:
+                grouped[u] = work.tile([P, CHUNKS[u // PASSES], PACK], BF16, name="grouped", align_bytes=64, bufs=4)
+
         def interleave(u):
-            width = CHUNKS[u // PASSES]
-            grouped[u] = work.tile([P, width, PACK], BF16, name="grouped", align_bytes=64)
+            width = CHUNKS[u // PASSES] - (TENSOR_FRAMES if u in ON_TENSOR else 0)
+            new_grouped(u)
             nc.vector.tensor_copy(
-                out=grouped[u][:].rearrange("p (c i) t -> p c t i", i=4),
-                in_=wide[u][:].rearrange("p t (c i) -> p c t i", i=4),
+                out=grouped[u][:, :width, :].rearrange("p (c i) t -> p c t i", i=4),
+                in_=wide[u][:, :, :width].rearrange("p t (c i) -> p c t i", i=4),
             )
+
+        def interleave_on_tensor(u):
+            first = CHUNKS[u // PASSES] - TENSOR_FRAMES
+            moved[u] = psum_w.tile([P, TENSOR_FRAMES * PACK], BF16, name="turned")
+            for n0 in range(0, TENSOR_FRAMES, BANK // PACK):
+                nc.tensor.matmul(
+                    out=moved[u][:, n0 * PACK : n0 * PACK + BANK],
+                    lhsT=ident_bf16[:],
+                    rhs=wide[u][:, :, first + n0 : first + n0 + BANK // PACK].rearrange("p t n -> p n t"),
+                    start=True,
+                    stop=True,
+                )
+
+        def fetch_from_tensor(u):
+            first = CHUNKS[u // PASSES] - TENSOR_FRAMES
+            new_grouped(u)
+            nc.scalar.copy(out=grouped[u][:, first:, :].rearrange("p n t -> p (n t)"), in_=moved[u][:])
 
         def quantize(u):
             width = CHUNKS[u // PASSES]
@@ -138,16 +163,13 @@ def tile_fp8_log_mel_d3_kernel(tc, P_bytes, P_scale, W, floor, gain, bias, out):
                     )
 
         def logarithm(c):
-            logs[c] = work.tile([P, CHUNKS[c]], F32, name="logs")
+            logs[c] = work.tile([P, CHUNKS[c]], F32, name="logs", bufs=4)
             for acc, cols in zip(mel[c], spans(c)):
                 nc.scalar.activation(out=logs[c][:, cols], in_=acc[:], func=ACT.Ln, bias=floor_col[:])
 
         def finish(c):
-            res = work.tile([P, CHUNKS[c]], F32, name="res")
-            if c >= len(CHUNKS) - 3:
-                nc.scalar.activation(out=res[:], in_=logs[c][:], func=ACT.Identity, scale=gain_f32[:], bias=bias_col[:])
-            else:
-                nc.vector.tensor_scalar(out=res[:], in0=logs[c][:], scalar1=gain_col[:], scalar2=bias_col[:], op0=ALU.mult, op1=ALU.add)
+            res = work.tile([P, CHUNKS[c]], F32, name="res", bufs=4)
+            nc.vector.tensor_scalar(out=res[:], in0=logs[c][:], scalar1=gain_col[:], scalar2=bias_col[:], op0=ALU.mult, op1=ALU.add)
             nc.sync.dma_start(out=out[:, starts[c] : starts[c] + CHUNKS[c]], in_=res[:])
 
         widen(0, False)
@@ -158,8 +180,12 @@ def tile_fp8_log_mel_d3_kernel(tc, P_bytes, P_scale, W, floor, gain, bias, out):
                 interleave(s)
             if s + 1 < units:
                 widen(s + 1, True)
+            if s + 1 in ON_TENSOR:
+                interleave_on_tensor(s + 1)
             if s + 2 < units:
                 widen(s + 2, False)
+            if s + 1 in ON_TENSOR:
+                fetch_from_tensor(s + 1)
             if s == 1:
                 turn_w()
             if 1 <= s <= units:
@@ -170,5 +196,9 @@ def tile_fp8_log_mel_d3_kernel(tc, P_bytes, P_scale, W, floor, gain, bias, out):
                 multiply(s // 2 - 1)
             if s >= 4 and (s - 4) % 2 == 0 and (s - 4) // 2 < len(CHUNKS):
                 logarithm((s - 4) // 2)
-            if s >= 5 and (s - 5) % 2 == 0 and (s - 5) // 2 < len(CHUNKS):
-                finish((s - 5) // 2)
+            for c in range(len(CHUNKS)):
+                due = 2 * c + 5
+                if due >= units - 3:
+                    due = max(due, units + 1)
+                if s == due:
+                    finish(c)

@@ -19,23 +19,34 @@ P = 128
 PACK = 4
 PASSES = F // (P * PACK)
 BANK = 512
-CHUNKS = [256,256,512,1024,1024,1024,1024,1024,1024,512,256,128,128]
-VPLANES = [3,1,2,2,2,2,1,1,1,1,1,1,1,1,1,1,1,1,0,0,0,0,0,0,0,0]
-ON_TENSOR = [6,8,10,12,14,16]
+RUN = 4
+
+CHUNKS = [256, 256, 512] + [1024] * 6 + [512, 256, 128, 128]
+UNITS = len(CHUNKS) * PASSES
+VECTOR_PLANES = [3, 1, 2, 2, 3, 2] + [1, 1, 1, 1, 2, 1] + [1] * 6 + [0, 0, 1, 1] + [0] * 4
 TENSOR_FRAMES = 256
-assert sum(CHUNKS) == T
+TENSOR_UNITS = [PASSES * c for c, frames in enumerate(CHUNKS) if frames == max(CHUNKS)]
+LOG_LAG = 4
+FINISH_LAG = 5
+LATE_STEPS = 3
+EARLY_LOADS = 4
+assert sum(CHUNKS) == T and len(VECTOR_PLANES) == UNITS
+
+
+def finish_step(c):
+    due = PASSES * c + FINISH_LAG
+    return max(due, UNITS + 1) if due >= UNITS - LATE_STEPS else due
 
 
 def tile_fp8_log_mel_d3_kernel(tc, P_bytes, P_scale, W, floor, gain, bias, out):
     nc = tc.nc
     starts = [sum(CHUNKS[:c]) for c in range(len(CHUNKS))]
-    units = len(CHUNKS) * PASSES
 
     with ExitStack() as ctx:
         keep = ctx.enter_context(tc.tile_pool(name="keep", bufs=1))
-        work = ctx.enter_context(tc.tile_pool(name="work", bufs=3))
-        psum_w = ctx.enter_context(tc.psum_pool(name="psum_w", bufs=2))
-        psum = ctx.enter_context(tc.psum_pool(name="psum", bufs=6))
+        work = ctx.enter_context(tc.tile_pool(name="work", bufs=4))
+        psum_moved = ctx.enter_context(tc.psum_pool(name="psum_moved", bufs=2))
+        psum_mel = ctx.enter_context(tc.psum_pool(name="psum_mel", bufs=6))
         ctx.enter_context(tc.manual_schedule())
 
         p_rows = P_bytes.rearrange("(g p t) n -> g p t n", p=P, t=PACK)
@@ -48,19 +59,19 @@ def tile_fp8_log_mel_d3_kernel(tc, P_bytes, P_scale, W, floor, gain, bias, out):
 
         row_scale = keep.tile([P, PASSES, PACK], F32)
         nc.scalar.dma_start(out=row_scale[:], in_=P_scale.rearrange("(g p t) o -> p g (t o)", p=P, t=PACK))
-        load(0)
-        load(1)
+        for u in range(PASSES):
+            load(u)
         w_rows = keep.tile([P, F], BF16, align_bytes=64)
         nc.sync.dma_start(out=w_rows[:], in_=W)
-        load(2)
-        load(3)
+        for u in range(PASSES, EARLY_LOADS):
+            load(u)
         floor_col = keep.tile([P, 1], BF16)
         gain_col = keep.tile([P, 1], BF16)
         bias_col = keep.tile([P, 1], BF16)
         nc.sync.dma_start(out=floor_col[:], in_=floor.rearrange("(p o) -> p o", o=1))
         nc.sync.dma_start(out=gain_col[:], in_=gain.rearrange("(p o) -> p o", o=1))
         nc.sync.dma_start(out=bias_col[:], in_=bias.rearrange("(p o) -> p o", o=1))
-        for u in range(4, units):
+        for u in range(EARLY_LOADS, UNITS):
             load(u)
 
         one = keep.tile([P, 1], F32)
@@ -68,8 +79,8 @@ def tile_fp8_log_mel_d3_kernel(tc, P_bytes, P_scale, W, floor, gain, bias, out):
         nc.vector.memset(one[:], 1.0)
         nc.scalar.activation(out=warm[:], in_=one[:], func=ACT.Ln)
 
-        ident = keep.tile([P, P], F32)
-        make_identity(nc, ident[:])
+        ident_f32 = keep.tile([P, P], F32)
+        make_identity(nc, ident_f32[:])
         ident_bf16 = keep.tile([P, P], BF16)
         make_identity(nc, ident_bf16[:])
 
@@ -78,11 +89,12 @@ def tile_fp8_log_mel_d3_kernel(tc, P_bytes, P_scale, W, floor, gain, bias, out):
         w_grouped = keep.tile([P, PASSES * N * PACK], BF16, align_bytes=64)
 
         def turn_w():
-            words = w_rows[:].bitcast(F32)
-            turned = psum_w.tile([P, PASSES, 2, N], F32, name="turned")
+            pairs = w_rows[:].bitcast(F32)
+            per_pass = P * PACK // 2
+            turned = psum_moved.tile([P, PASSES, 2, N], F32, name="moved")
             for g in range(PASSES):
                 for h in range(2):
-                    nc.tensor.transpose(turned[:, g, h, :], words[:, 256 * g + h : 256 * (g + 1) : 2], ident[:])
+                    nc.tensor.transpose(turned[:, g, h, :], pairs[:, per_pass * g + h : per_pass * (g + 1) : 2], ident_f32[:])
             nc.scalar.copy(
                 out=w_grouped[:].bitcast(F32).rearrange("p (g m h) -> p g m h", g=PASSES, h=2),
                 in_=turned[:].rearrange("p g h m -> p g m h"),
@@ -91,64 +103,80 @@ def tile_fp8_log_mel_d3_kernel(tc, P_bytes, P_scale, W, floor, gain, bias, out):
         def quantize_w():
             nc.vector.quantize_mx(out=w_codes[:].bitcast(FP8X4), scales=w_scales[:], in_=w_grouped[:])
 
-        wide, grouped, codes, scales, mel, logs = {}, {}, {}, {}, {}, {}
+        wide, grouped, moved, codes, scales, mel, logs = {}, {}, {}, {}, {}, {}, {}
 
-        def widen(u, on_vector):
-            c, g = divmod(u, PASSES)
+        def wide_tile(u):
             if u not in wide:
-                wide[u] = work.tile([P, PACK, CHUNKS[c]], BF16, name="wide", bufs=4)
-            planes = range(PACK - VPLANES[u], PACK) if on_vector else range(PACK - VPLANES[u])
-            for t in planes:
-                src = raw[u][:, t, :].bitcast(FP8)
-                if on_vector:
-                    nc.vector.tensor_scalar(out=wide[u][:, t, :], in0=src, scalar1=row_scale[:, g, t : t + 1], scalar2=None, op0=ALU.mult)
-                else:
-                    nc.scalar.activation(out=wide[u][:, t, :], in_=src, func=ACT.Copy, scale=row_scale[:, g, t : t + 1])
+                wide[u] = work.tile([P, PACK, CHUNKS[u // PASSES]], BF16, name="wide")
+            return wide[u]
 
-        moved = {}
-
-        def new_grouped(u):
+        def grouped_tile(u):
             if u not in grouped:
-                grouped[u] = work.tile([P, CHUNKS[u // PASSES], PACK], BF16, name="grouped", align_bytes=64, bufs=4)
+                grouped[u] = work.tile([P, CHUNKS[u // PASSES], PACK], BF16, name="grouped", align_bytes=64)
+            return grouped[u]
 
-        def interleave(u):
-            width = CHUNKS[u // PASSES] - (TENSOR_FRAMES if u in ON_TENSOR else 0)
-            new_grouped(u)
+        def widen_on_scalar(u):
+            for t in range(PACK - VECTOR_PLANES[u]):
+                nc.scalar.activation(
+                    out=wide_tile(u)[:, t, :],
+                    in_=raw[u][:, t, :].bitcast(FP8),
+                    func=ACT.Copy,
+                    scale=row_scale[:, u % PASSES, t : t + 1],
+                )
+
+        def widen_on_vector(u):
+            for t in range(PACK - VECTOR_PLANES[u], PACK):
+                nc.vector.tensor_scalar(
+                    out=wide_tile(u)[:, t, :],
+                    in0=raw[u][:, t, :].bitcast(FP8),
+                    scalar1=row_scale[:, u % PASSES, t : t + 1],
+                    scalar2=None,
+                    op0=ALU.mult,
+                )
+
+        def vector_frames(u):
+            return CHUNKS[u // PASSES] - (TENSOR_FRAMES if u in TENSOR_UNITS else 0)
+
+        def interleave_on_vector(u):
+            frames = vector_frames(u)
             nc.vector.tensor_copy(
-                out=grouped[u][:, :width, :].rearrange("p (c i) t -> p c t i", i=4),
-                in_=wide[u][:, :, :width].rearrange("p t (c i) -> p c t i", i=4),
+                out=grouped_tile(u)[:, :frames, :].rearrange("p (r i) t -> p r t i", i=RUN),
+                in_=wide[u][:, :, :frames].rearrange("p t (r i) -> p r t i", i=RUN),
             )
 
         def interleave_on_tensor(u):
-            first = CHUNKS[u // PASSES] - TENSOR_FRAMES
-            moved[u] = psum_w.tile([P, TENSOR_FRAMES * PACK], BF16, name="turned")
-            for n0 in range(0, TENSOR_FRAMES, BANK // PACK):
+            first = vector_frames(u)
+            frames = BANK // PACK
+            moved[u] = psum_moved.tile([P, TENSOR_FRAMES * PACK], BF16, name="moved")
+            for n0 in range(0, TENSOR_FRAMES, frames):
                 nc.tensor.matmul(
                     out=moved[u][:, n0 * PACK : n0 * PACK + BANK],
                     lhsT=ident_bf16[:],
-                    rhs=wide[u][:, :, first + n0 : first + n0 + BANK // PACK].rearrange("p t n -> p n t"),
+                    rhs=wide[u][:, :, first + n0 : first + n0 + frames].rearrange("p t n -> p n t"),
                     start=True,
                     stop=True,
                 )
 
         def fetch_from_tensor(u):
-            first = CHUNKS[u // PASSES] - TENSOR_FRAMES
-            new_grouped(u)
-            nc.scalar.copy(out=grouped[u][:, first:, :].rearrange("p n t -> p (n t)"), in_=moved[u][:])
+            nc.scalar.copy(out=grouped_tile(u)[:, vector_frames(u) :, :].rearrange("p n t -> p (n t)"), in_=moved[u][:])
 
         def quantize(u):
-            width = CHUNKS[u // PASSES]
-            codes[u] = work.tile([P, width], U32, name="codes", align_bytes=64, bufs=4)
-            scales[u] = work.tile([P, width], U8, name="scales", align_bytes=64, bufs=4)
-            nc.vector.quantize_mx(out=codes[u][:].bitcast(FP8X4), scales=scales[u][:], in_=grouped[u][:].rearrange("p n t -> p (n t)"))
+            frames = CHUNKS[u // PASSES]
+            codes[u] = work.tile([P, frames], U32, name="codes", align_bytes=64)
+            scales[u] = work.tile([P, frames], U8, name="scales", align_bytes=64)
+            nc.vector.quantize_mx(
+                out=codes[u][:].bitcast(FP8X4),
+                scales=scales[u][:],
+                in_=grouped[u][:].rearrange("p n t -> p (n t)"),
+            )
 
-        def spans(c):
+        def banks(c):
             return [slice(n0, min(n0 + BANK, CHUNKS[c])) for n0 in range(0, CHUNKS[c], BANK)]
 
         def multiply(c):
             mel[c] = []
-            for cols in spans(c):
-                acc = psum.tile([P, cols.stop - cols.start], F32, name="mel")
+            for cols in banks(c):
+                acc = psum_mel.tile([P, cols.stop - cols.start], F32, name="mel")
                 mel[c].append(acc)
                 for g in range(PASSES):
                     u = PASSES * c + g
@@ -163,42 +191,43 @@ def tile_fp8_log_mel_d3_kernel(tc, P_bytes, P_scale, W, floor, gain, bias, out):
                     )
 
         def logarithm(c):
-            logs[c] = work.tile([P, CHUNKS[c]], F32, name="logs", bufs=4)
-            for acc, cols in zip(mel[c], spans(c)):
+            logs[c] = work.tile([P, CHUNKS[c]], F32, name="logs")
+            for acc, cols in zip(mel[c], banks(c)):
                 nc.scalar.activation(out=logs[c][:, cols], in_=acc[:], func=ACT.Ln, bias=floor_col[:])
 
         def finish(c):
-            res = work.tile([P, CHUNKS[c]], F32, name="res", bufs=4)
-            nc.vector.tensor_scalar(out=res[:], in0=logs[c][:], scalar1=gain_col[:], scalar2=bias_col[:], op0=ALU.mult, op1=ALU.add)
-            nc.sync.dma_start(out=out[:, starts[c] : starts[c] + CHUNKS[c]], in_=res[:])
+            result = work.tile([P, CHUNKS[c]], F32, name="result")
+            nc.vector.tensor_scalar(
+                out=result[:], in0=logs[c][:], scalar1=gain_col[:], scalar2=bias_col[:], op0=ALU.mult, op1=ALU.add
+            )
+            nc.sync.dma_start(out=out[:, starts[c] : starts[c] + CHUNKS[c]], in_=result[:])
 
-        widen(0, False)
-        widen(1, False)
-        widen(0, True)
-        for s in range(units + 5):
-            if s < units:
-                interleave(s)
-            if s + 1 < units:
-                widen(s + 1, True)
-            if s + 1 in ON_TENSOR:
+        widen_on_scalar(0)
+        widen_on_scalar(1)
+        widen_on_vector(0)
+        for s in range(finish_step(len(CHUNKS) - 1) + 1):
+            if s < UNITS:
+                interleave_on_vector(s)
+            if s + 1 < UNITS:
+                widen_on_vector(s + 1)
+            if s + 1 in TENSOR_UNITS:
                 interleave_on_tensor(s + 1)
-            if s + 2 < units:
-                widen(s + 2, False)
-            if s + 1 in ON_TENSOR:
+            if s + 2 < UNITS:
+                widen_on_scalar(s + 2)
+            if s + 1 in TENSOR_UNITS:
                 fetch_from_tensor(s + 1)
             if s == 1:
                 turn_w()
-            if 1 <= s <= units:
+            if 1 <= s <= UNITS:
                 quantize(s - 1)
-            if s == 2:
+            if s == PASSES:
                 quantize_w()
-            if 2 <= s <= units and s % 2 == 0:
-                multiply(s // 2 - 1)
-            if s >= 4 and (s - 4) % 2 == 0 and (s - 4) // 2 < len(CHUNKS):
-                logarithm((s - 4) // 2)
             for c in range(len(CHUNKS)):
-                due = 2 * c + 5
-                if due >= units - 3:
-                    due = max(due, units + 1)
-                if s == due:
+                if s == PASSES * c + PASSES:
+                    multiply(c)
+            for c in range(len(CHUNKS)):
+                if s == PASSES * c + LOG_LAG:
+                    logarithm(c)
+            for c in range(len(CHUNKS)):
+                if s == finish_step(c):
                     finish(c)

@@ -21,30 +21,66 @@ PASSES = F // (P * PACK)
 BANK = 512
 RUN = 4
 
+LOADS = [256, 768] + [1024] * 7
 CHUNKS = [256, 256, 512] + [1024] * 6 + [512, 256, 128, 128]
 UNITS = len(CHUNKS) * PASSES
-VECTOR_PLANES = [3, 1, 2, 2, 3, 2] + [1, 1, 1, 1, 2, 1] + [1] * 6 + [0, 0, 1, 1] + [0] * 4
+FULL = max(CHUNKS)
+FIRST_FULL = CHUNKS.index(FULL)
+AFTER_FULL = FIRST_FULL + CHUNKS.count(FULL)
+HEAD_PLANES = (3, 1, 2, 2)
+LAST_PLANES = (0, 0)
+SECOND_EVERY = 2
+SCALAR_FINISH = (7, 8)
+W_STEP = 2
+LOG_LATE = 3
 TENSOR_FRAMES = 256
-TENSOR_UNITS = [PASSES * c for c, frames in enumerate(CHUNKS) if frames == max(CHUNKS)]
+TENSOR_UNITS = [PASSES * c for c, frames in enumerate(CHUNKS) if frames == FULL]
 LOG_LAG = 4
 FINISH_LAG = 5
 LATE_STEPS = 3
 EARLY_LOADS = 4
-assert sum(CHUNKS) == T and len(VECTOR_PLANES) == UNITS
+SCALAR_LEAD = 2
+VECTOR_LEAD = 2
+assert sum(CHUNKS) == T and sum(LOADS) == T
+
+
+def vector_planes(v):
+    n, g = divmod(v, PASSES)
+    if v < len(HEAD_PLANES):
+        return HEAD_PLANES[v]
+    if n == len(LOADS) - 1:
+        return LAST_PLANES[g]
+    return 2 if g == 0 and (n + 1) % SECOND_EVERY == 0 else 1
+
+
+def log_step(c):
+    if c >= AFTER_FULL:
+        return PASSES * c + LOG_LATE
+    if c in SCALAR_FINISH:
+        return max(PASSES * c + LOG_LAG, PASSES * AFTER_FULL + 1 - SCALAR_LEAD)
+    return PASSES * c + LOG_LAG
 
 
 def finish_step(c):
+    if c in SCALAR_FINISH:
+        return log_step(min(c + 1, max(SCALAR_FINISH)))
     due = PASSES * c + FINISH_LAG
-    return max(due, UNITS + 1) if due >= UNITS - LATE_STEPS else due
+    return UNITS + 1 if due >= UNITS - LATE_STEPS else due
 
 
 def tile_fp8_log_mel_d3_kernel(tc, P_bytes, P_scale, W, floor, gain, bias, out):
     nc = tc.nc
     starts = [sum(CHUNKS[:c]) for c in range(len(CHUNKS))]
+    load_starts = [sum(LOADS[:n]) for n in range(len(LOADS))]
+
+    def source(u):
+        c, g = divmod(u, PASSES)
+        n = max(i for i in range(len(LOADS)) if load_starts[i] <= starts[c])
+        return PASSES * n + g, starts[c] - load_starts[n]
 
     with ExitStack() as ctx:
         keep = ctx.enter_context(tc.tile_pool(name="keep", bufs=1))
-        work = ctx.enter_context(tc.tile_pool(name="work", bufs=4))
+        work = ctx.enter_context(tc.tile_pool(name="work", bufs=5))
         psum_moved = ctx.enter_context(tc.psum_pool(name="psum_moved", bufs=2))
         psum_mel = ctx.enter_context(tc.psum_pool(name="psum_mel", bufs=6))
         ctx.enter_context(tc.manual_schedule())
@@ -52,26 +88,24 @@ def tile_fp8_log_mel_d3_kernel(tc, P_bytes, P_scale, W, floor, gain, bias, out):
         p_rows = P_bytes.rearrange("(g p t) n -> g p t n", p=P, t=PACK)
         raw = {}
 
-        def load(u):
-            c, g = divmod(u, PASSES)
-            raw[u] = keep.tile([P, PACK, CHUNKS[c]], U8, name="p_bytes_%d" % u)
-            nc.sync.dma_start(out=raw[u][:], in_=p_rows[g][:, :, starts[c] : starts[c] + CHUNKS[c]])
+        def load(v):
+            n, g = divmod(v, PASSES)
+            raw[v] = keep.tile([P, PACK, LOADS[n]], U8, name="p_bytes_%d" % v)
+            nc.sync.dma_start(out=raw[v][:], in_=p_rows[g][:, :, load_starts[n] : load_starts[n] + LOADS[n]])
 
         row_scale = keep.tile([P, PASSES, PACK], F32)
         nc.scalar.dma_start(out=row_scale[:], in_=P_scale.rearrange("(g p t) o -> p g (t o)", p=P, t=PACK))
-        for u in range(PASSES):
+        for u in range(EARLY_LOADS):
             load(u)
         w_rows = keep.tile([P, F], BF16, align_bytes=64)
         nc.sync.dma_start(out=w_rows[:], in_=W)
-        for u in range(PASSES, EARLY_LOADS):
-            load(u)
         floor_col = keep.tile([P, 1], BF16)
         gain_col = keep.tile([P, 1], BF16)
         bias_col = keep.tile([P, 1], BF16)
         nc.sync.dma_start(out=floor_col[:], in_=floor.rearrange("(p o) -> p o", o=1))
         nc.sync.dma_start(out=gain_col[:], in_=gain.rearrange("(p o) -> p o", o=1))
         nc.sync.dma_start(out=bias_col[:], in_=bias.rearrange("(p o) -> p o", o=1))
-        for u in range(EARLY_LOADS, UNITS):
+        for u in range(EARLY_LOADS, PASSES * len(LOADS)):
             load(u)
 
         one = keep.tile([P, 1], F32)
@@ -100,15 +134,17 @@ def tile_fp8_log_mel_d3_kernel(tc, P_bytes, P_scale, W, floor, gain, bias, out):
                 in_=turned[:].rearrange("p g h m -> p g m h"),
             )
 
+        gain_f32 = keep.tile([P, 1], F32)
+
         def quantize_w():
             nc.vector.quantize_mx(out=w_codes[:].bitcast(FP8X4), scales=w_scales[:], in_=w_grouped[:])
 
         wide, grouped, moved, codes, scales, mel, logs = {}, {}, {}, {}, {}, {}, {}
 
-        def wide_tile(u):
-            if u not in wide:
-                wide[u] = work.tile([P, PACK, CHUNKS[u // PASSES]], BF16, name="wide")
-            return wide[u]
+        def wide_tile(v):
+            if v not in wide:
+                wide[v] = work.tile([P, PACK, LOADS[v // PASSES]], BF16, name="wide")
+            return wide[v]
 
         def grouped_tile(u):
             if u not in grouped:
@@ -116,7 +152,7 @@ def tile_fp8_log_mel_d3_kernel(tc, P_bytes, P_scale, W, floor, gain, bias, out):
             return grouped[u]
 
         def widen_on_scalar(u):
-            for t in range(PACK - VECTOR_PLANES[u]):
+            for t in range(PACK - vector_planes(u)):
                 nc.scalar.activation(
                     out=wide_tile(u)[:, t, :],
                     in_=raw[u][:, t, :].bitcast(FP8),
@@ -125,7 +161,7 @@ def tile_fp8_log_mel_d3_kernel(tc, P_bytes, P_scale, W, floor, gain, bias, out):
                 )
 
         def widen_on_vector(u):
-            for t in range(PACK - VECTOR_PLANES[u], PACK):
+            for t in range(PACK - vector_planes(u), PACK):
                 nc.vector.tensor_scalar(
                     out=wide_tile(u)[:, t, :],
                     in0=raw[u][:, t, :].bitcast(FP8),
@@ -139,9 +175,10 @@ def tile_fp8_log_mel_d3_kernel(tc, P_bytes, P_scale, W, floor, gain, bias, out):
 
         def interleave_on_vector(u):
             frames = vector_frames(u)
+            v, first = source(u)
             nc.vector.tensor_copy(
                 out=grouped_tile(u)[:, :frames, :].rearrange("p (r i) t -> p r t i", i=RUN),
-                in_=wide[u][:, :, :frames].rearrange("p t (r i) -> p r t i", i=RUN),
+                in_=wide[v][:, :, first : first + frames].rearrange("p t (r i) -> p r t i", i=RUN),
             )
 
         def interleave_on_tensor(u):
@@ -152,13 +189,16 @@ def tile_fp8_log_mel_d3_kernel(tc, P_bytes, P_scale, W, floor, gain, bias, out):
                 nc.tensor.matmul(
                     out=moved[u][:, n0 * PACK : n0 * PACK + BANK],
                     lhsT=ident_bf16[:],
-                    rhs=wide[u][:, :, first + n0 : first + n0 + frames].rearrange("p t n -> p n t"),
+                    rhs=wide[source(u)[0]][:, :, first + n0 : first + n0 + frames].rearrange("p t n -> p n t"),
                     start=True,
                     stop=True,
                 )
 
         def fetch_from_tensor(u):
-            nc.scalar.copy(out=grouped_tile(u)[:, vector_frames(u) :, :].rearrange("p n t -> p (n t)"), in_=moved[u][:])
+            nc.scalar.copy(
+                out=grouped_tile(u)[:, vector_frames(u) :, :].rearrange("p n t -> p (n t)").bitcast(F32),
+                in_=moved[u][:].bitcast(F32),
+            )
 
         def quantize(u):
             frames = CHUNKS[u // PASSES]
@@ -197,36 +237,47 @@ def tile_fp8_log_mel_d3_kernel(tc, P_bytes, P_scale, W, floor, gain, bias, out):
 
         def finish(c):
             result = work.tile([P, CHUNKS[c]], F32, name="result")
-            nc.vector.tensor_scalar(
-                out=result[:], in0=logs[c][:], scalar1=gain_col[:], scalar2=bias_col[:], op0=ALU.mult, op1=ALU.add
-            )
+            if c in SCALAR_FINISH:
+                nc.scalar.activation(out=result[:], in_=logs[c][:], func=ACT.Identity, scale=gain_f32[:], bias=bias_col[:])
+            else:
+                nc.vector.tensor_scalar(
+                    out=result[:], in0=logs[c][:], scalar1=gain_col[:], scalar2=bias_col[:], op0=ALU.mult, op1=ALU.add
+                )
             nc.sync.dma_start(out=out[:, starts[c] : starts[c] + CHUNKS[c]], in_=result[:])
 
-        widen_on_scalar(0)
-        widen_on_scalar(1)
-        widen_on_vector(0)
-        for s in range(finish_step(len(CHUNKS) - 1) + 1):
+        done = set()
+
+        def ahead(widen, u):
+            if u < UNITS and (widen, source(u)[0]) not in done:
+                done.add((widen, source(u)[0]))
+                widen(source(u)[0])
+
+        for u in range(2):
+            ahead(widen_on_scalar, u)
+            ahead(widen_on_vector, u)
+        for s in range(UNITS + 2):
             if s < UNITS:
                 interleave_on_vector(s)
-            if s + 1 < UNITS:
-                widen_on_vector(s + 1)
+            for u in range(s + VECTOR_LEAD + 1):
+                ahead(widen_on_vector, u)
             if s + 1 in TENSOR_UNITS:
                 interleave_on_tensor(s + 1)
-            if s + 2 < UNITS:
-                widen_on_scalar(s + 2)
+            ahead(widen_on_scalar, s + SCALAR_LEAD)
             if s + 1 in TENSOR_UNITS:
                 fetch_from_tensor(s + 1)
-            if s == 1:
+            if s == W_STEP:
                 turn_w()
             if 1 <= s <= UNITS:
                 quantize(s - 1)
-            if s == PASSES:
+            if s == W_STEP + 1:
                 quantize_w()
+            if s == UNITS // 2:
+                nc.vector.tensor_copy(out=gain_f32[:], in_=gain_col[:])
             for c in range(len(CHUNKS)):
-                if s == PASSES * c + PASSES:
+                if s == max(PASSES * c + PASSES, W_STEP + 1):
                     multiply(c)
             for c in range(len(CHUNKS)):
-                if s == PASSES * c + LOG_LAG:
+                if s == log_step(c):
                     logarithm(c)
             for c in range(len(CHUNKS)):
                 if s == finish_step(c):

@@ -28,9 +28,10 @@ FULL = max(CHUNKS)
 FIRST_FULL = CHUNKS.index(FULL)
 AFTER_FULL = FIRST_FULL + CHUNKS.count(FULL)
 HEAD_PLANES = (3, 1, 2, 2)
-LAST_PLANES = (0, 0)
+LAST_PLANES = (1, 0)
 SECOND_EVERY = 2
-SCALAR_FINISH = (7, 8)
+SCALAR_FINISH = (6, 7, 8)
+RESULT_BUFS = 7
 W_STEP = 2
 LOG_LATE = 3
 TENSOR_FRAMES = 256
@@ -236,14 +237,22 @@ def tile_fp8_log_mel_d3_kernel(tc, P_bytes, P_scale, W, floor, gain, bias, out):
                 nc.scalar.activation(out=logs[c][:, cols], in_=acc[:], func=ACT.Ln, bias=floor_col[:])
 
         def finish(c):
-            result = work.tile([P, CHUNKS[c]], F32, name="result")
-            if c in SCALAR_FINISH:
-                nc.scalar.activation(out=result[:], in_=logs[c][:], func=ACT.Identity, scale=gain_f32[:], bias=bias_col[:])
-            else:
-                nc.vector.tensor_scalar(
-                    out=result[:], in0=logs[c][:], scalar1=gain_col[:], scalar2=bias_col[:], op0=ALU.mult, op1=ALU.add
-                )
-            nc.sync.dma_start(out=out[:, starts[c] : starts[c] + CHUNKS[c]], in_=result[:])
+            result = work.tile([P, CHUNKS[c]], F32, name="result", bufs=RESULT_BUFS)
+            for cols in banks(c) if c in SCALAR_FINISH else [slice(0, CHUNKS[c])]:
+                if c in SCALAR_FINISH:
+                    nc.scalar.activation(
+                        out=result[:, cols], in_=logs[c][:, cols], func=ACT.Identity, scale=gain_f32[:], bias=bias_col[:]
+                    )
+                else:
+                    nc.vector.tensor_scalar(
+                        out=result[:, cols],
+                        in0=logs[c][:, cols],
+                        scalar1=gain_col[:],
+                        scalar2=bias_col[:],
+                        op0=ALU.mult,
+                        op1=ALU.add,
+                    )
+                nc.sync.dma_start(out=out[:, starts[c] + cols.start : starts[c] + cols.stop], in_=result[:, cols])
 
         done = set()
 

@@ -20,64 +20,65 @@ PACK = 4
 PASSES = F // (P * PACK)
 BANK = 512
 RUN = 4
+FULL = 1024
 
-LOADS = [256, 768] + [1024] * 7
-CHUNKS = [256, 256, 512] + [1024] * 6 + [512, 256, 128, 128]
+SPANS = [256, FULL - 256] + [FULL] * 7
+SHORT_SPANS = 2
+CHUNKS = [256, 256, 512] + [FULL] * 6 + [512, 256, 128, 128]
 UNITS = len(CHUNKS) * PASSES
-FULL = max(CHUNKS)
-FIRST_FULL = CHUNKS.index(FULL)
-AFTER_FULL = FIRST_FULL + CHUNKS.count(FULL)
-HEAD_PLANES = (3, 1, 2, 2)
-LAST_PLANES = (1, 0)
-SECOND_EVERY = 2
-SCALAR_FINISH = (6, 7, 8)
-RESULT_BUFS = 7
-W_STEP = 2
-LOG_LATE = 3
+AFTER_FULL = max(c for c, frames in enumerate(CHUNKS) if frames == FULL) + 1
+assert sum(CHUNKS) == T and sum(SPANS) == T
+
+HEAD_PLANES = 2
+SECOND_EVERY = 4
+SCALAR_FINISH = range(AFTER_FULL - 3, AFTER_FULL)
 TENSOR_FRAMES = 256
 TENSOR_UNITS = [PASSES * c for c, frames in enumerate(CHUNKS) if frames == FULL]
+
+LEAD = 2
+LAST_WIDENING = PASSES * AFTER_FULL + 1 - LEAD
+W_STEP = 2
+EARLY_LOADS = PASSES * SHORT_SPANS
 LOG_LAG = 4
 FINISH_LAG = 5
-LATE_STEPS = 3
-EARLY_LOADS = 4
-SCALAR_LEAD = 2
-VECTOR_LEAD = 2
-assert sum(CHUNKS) == T and sum(LOADS) == T
 
 
 def vector_planes(v):
-    n, g = divmod(v, PASSES)
-    if v < len(HEAD_PLANES):
-        return HEAD_PLANES[v]
-    if n == len(LOADS) - 1:
-        return LAST_PLANES[g]
-    return 2 if g == 0 and (n + 1) % SECOND_EVERY == 0 else 1
+    span, g = divmod(v, PASSES)
+    if span < SHORT_SPANS:
+        return HEAD_PLANES
+    return 2 if g == 0 and (span + 1) % SECOND_EVERY == 0 else 1
+
+
+def multiply_step(c):
+    return max(PASSES * c + PASSES, W_STEP + 1)
 
 
 def log_step(c):
     if c >= AFTER_FULL:
-        return PASSES * c + LOG_LATE
+        return PASSES * c + LOG_LAG - 1
     if c in SCALAR_FINISH:
-        return max(PASSES * c + LOG_LAG, PASSES * AFTER_FULL + 1 - SCALAR_LEAD)
+        return max(PASSES * c + LOG_LAG, LAST_WIDENING)
     return PASSES * c + LOG_LAG
 
 
 def finish_step(c):
+    if c >= AFTER_FULL:
+        return UNITS + 1
     if c in SCALAR_FINISH:
-        return log_step(min(c + 1, max(SCALAR_FINISH)))
-    due = PASSES * c + FINISH_LAG
-    return UNITS + 1 if due >= UNITS - LATE_STEPS else due
+        return log_step(min(c + 1, SCALAR_FINISH[-1]))
+    return PASSES * c + FINISH_LAG
 
 
 def tile_fp8_log_mel_d3_kernel(tc, P_bytes, P_scale, W, floor, gain, bias, out):
     nc = tc.nc
-    starts = [sum(CHUNKS[:c]) for c in range(len(CHUNKS))]
-    load_starts = [sum(LOADS[:n]) for n in range(len(LOADS))]
+    chunk_start = [sum(CHUNKS[:c]) for c in range(len(CHUNKS))]
+    span_start = [sum(SPANS[:n]) for n in range(len(SPANS))]
 
     def source(u):
         c, g = divmod(u, PASSES)
-        n = max(i for i in range(len(LOADS)) if load_starts[i] <= starts[c])
-        return PASSES * n + g, starts[c] - load_starts[n]
+        span = max(n for n in range(len(SPANS)) if span_start[n] <= chunk_start[c])
+        return PASSES * span + g, chunk_start[c] - span_start[span]
 
     with ExitStack() as ctx:
         keep = ctx.enter_context(tc.tile_pool(name="keep", bufs=1))
@@ -90,14 +91,14 @@ def tile_fp8_log_mel_d3_kernel(tc, P_bytes, P_scale, W, floor, gain, bias, out):
         raw = {}
 
         def load(v):
-            n, g = divmod(v, PASSES)
-            raw[v] = keep.tile([P, PACK, LOADS[n]], U8, name="p_bytes_%d" % v)
-            nc.sync.dma_start(out=raw[v][:], in_=p_rows[g][:, :, load_starts[n] : load_starts[n] + LOADS[n]])
+            span, g = divmod(v, PASSES)
+            raw[v] = keep.tile([P, PACK, SPANS[span]], U8, name="p_bytes_%d" % v)
+            nc.sync.dma_start(out=raw[v][:], in_=p_rows[g][:, :, span_start[span] : span_start[span] + SPANS[span]])
 
         row_scale = keep.tile([P, PASSES, PACK], F32)
         nc.scalar.dma_start(out=row_scale[:], in_=P_scale.rearrange("(g p t) o -> p g (t o)", p=P, t=PACK))
-        for u in range(EARLY_LOADS):
-            load(u)
+        for v in range(EARLY_LOADS):
+            load(v)
         w_rows = keep.tile([P, F], BF16, align_bytes=64)
         nc.sync.dma_start(out=w_rows[:], in_=W)
         floor_col = keep.tile([P, 1], BF16)
@@ -106,8 +107,8 @@ def tile_fp8_log_mel_d3_kernel(tc, P_bytes, P_scale, W, floor, gain, bias, out):
         nc.sync.dma_start(out=floor_col[:], in_=floor.rearrange("(p o) -> p o", o=1))
         nc.sync.dma_start(out=gain_col[:], in_=gain.rearrange("(p o) -> p o", o=1))
         nc.sync.dma_start(out=bias_col[:], in_=bias.rearrange("(p o) -> p o", o=1))
-        for u in range(EARLY_LOADS, PASSES * len(LOADS)):
-            load(u)
+        for v in range(EARLY_LOADS, PASSES * len(SPANS)):
+            load(v)
 
         one = keep.tile([P, 1], F32)
         warm = keep.tile([P, 1], F32)
@@ -122,6 +123,7 @@ def tile_fp8_log_mel_d3_kernel(tc, P_bytes, P_scale, W, floor, gain, bias, out):
         w_codes = keep.tile([P, PASSES * N], U32, align_bytes=64)
         w_scales = keep.tile([P, PASSES * N], U8, align_bytes=64)
         w_grouped = keep.tile([P, PASSES * N * PACK], BF16, align_bytes=64)
+        gain_f32 = keep.tile([P, 1], F32)
 
         def turn_w():
             pairs = w_rows[:].bitcast(F32)
@@ -135,62 +137,49 @@ def tile_fp8_log_mel_d3_kernel(tc, P_bytes, P_scale, W, floor, gain, bias, out):
                 in_=turned[:].rearrange("p g h m -> p g m h"),
             )
 
-        gain_f32 = keep.tile([P, 1], F32)
-
         def quantize_w():
             nc.vector.quantize_mx(out=w_codes[:].bitcast(FP8X4), scales=w_scales[:], in_=w_grouped[:])
 
         wide, grouped, moved, codes, scales, mel, logs = {}, {}, {}, {}, {}, {}, {}
 
-        def wide_tile(v):
-            if v not in wide:
-                wide[v] = work.tile([P, PACK, LOADS[v // PASSES]], BF16, name="wide")
-            return wide[v]
+        def widen(u):
+            v = source(u)[0]
+            if v in wide:
+                return
+            wide[v] = work.tile([P, PACK, SPANS[v // PASSES]], BF16, name="wide")
+            for t in range(PACK):
+                plane, scale = raw[v][:, t, :].bitcast(FP8), row_scale[:, v % PASSES, t : t + 1]
+                if t < PACK - vector_planes(v):
+                    nc.scalar.activation(out=wide[v][:, t, :], in_=plane, func=ACT.Copy, scale=scale)
+                else:
+                    nc.vector.tensor_scalar(out=wide[v][:, t, :], in0=plane, scalar1=scale, scalar2=None, op0=ALU.mult)
 
         def grouped_tile(u):
             if u not in grouped:
                 grouped[u] = work.tile([P, CHUNKS[u // PASSES], PACK], BF16, name="grouped", align_bytes=64)
             return grouped[u]
 
-        def widen_on_scalar(u):
-            for t in range(PACK - vector_planes(u)):
-                nc.scalar.activation(
-                    out=wide_tile(u)[:, t, :],
-                    in_=raw[u][:, t, :].bitcast(FP8),
-                    func=ACT.Copy,
-                    scale=row_scale[:, u % PASSES, t : t + 1],
-                )
-
-        def widen_on_vector(u):
-            for t in range(PACK - vector_planes(u), PACK):
-                nc.vector.tensor_scalar(
-                    out=wide_tile(u)[:, t, :],
-                    in0=raw[u][:, t, :].bitcast(FP8),
-                    scalar1=row_scale[:, u % PASSES, t : t + 1],
-                    scalar2=None,
-                    op0=ALU.mult,
-                )
-
         def vector_frames(u):
             return CHUNKS[u // PASSES] - (TENSOR_FRAMES if u in TENSOR_UNITS else 0)
 
         def interleave_on_vector(u):
-            frames = vector_frames(u)
             v, first = source(u)
+            frames = vector_frames(u)
             nc.vector.tensor_copy(
                 out=grouped_tile(u)[:, :frames, :].rearrange("p (r i) t -> p r t i", i=RUN),
                 in_=wide[v][:, :, first : first + frames].rearrange("p t (r i) -> p r t i", i=RUN),
             )
 
         def interleave_on_tensor(u):
-            first = vector_frames(u)
+            v, first = source(u)
+            first = first + vector_frames(u)
             frames = BANK // PACK
             moved[u] = psum_moved.tile([P, TENSOR_FRAMES * PACK], BF16, name="moved")
             for n0 in range(0, TENSOR_FRAMES, frames):
                 nc.tensor.matmul(
                     out=moved[u][:, n0 * PACK : n0 * PACK + BANK],
                     lhsT=ident_bf16[:],
-                    rhs=wide[source(u)[0]][:, :, first + n0 : first + n0 + frames].rearrange("p t n -> p n t"),
+                    rhs=wide[v][:, :, first + n0 : first + n0 + frames].rearrange("p t n -> p n t"),
                     start=True,
                     stop=True,
                 )
@@ -232,46 +221,35 @@ def tile_fp8_log_mel_d3_kernel(tc, P_bytes, P_scale, W, floor, gain, bias, out):
                     )
 
         def logarithm(c):
-            logs[c] = work.tile([P, CHUNKS[c]], F32, name="logs")
+            logs[c] = keep.tile([P, CHUNKS[c]], F32, name="logs_%d" % c)
             for acc, cols in zip(mel[c], banks(c)):
                 nc.scalar.activation(out=logs[c][:, cols], in_=acc[:], func=ACT.Ln, bias=floor_col[:])
 
+        def store(c, cols):
+            nc.sync.dma_start(out=out[:, chunk_start[c] + cols.start : chunk_start[c] + cols.stop], in_=logs[c][:, cols])
+
         def finish(c):
-            result = work.tile([P, CHUNKS[c]], F32, name="result", bufs=RESULT_BUFS)
-            for cols in banks(c) if c in SCALAR_FINISH else [slice(0, CHUNKS[c])]:
-                if c in SCALAR_FINISH:
+            if c in SCALAR_FINISH:
+                for cols in banks(c):
                     nc.scalar.activation(
-                        out=result[:, cols], in_=logs[c][:, cols], func=ACT.Identity, scale=gain_f32[:], bias=bias_col[:]
+                        out=logs[c][:, cols], in_=logs[c][:, cols], func=ACT.Identity, scale=gain_f32[:], bias=bias_col[:]
                     )
-                else:
-                    nc.vector.tensor_scalar(
-                        out=result[:, cols],
-                        in0=logs[c][:, cols],
-                        scalar1=gain_col[:],
-                        scalar2=bias_col[:],
-                        op0=ALU.mult,
-                        op1=ALU.add,
-                    )
-                nc.sync.dma_start(out=out[:, starts[c] + cols.start : starts[c] + cols.stop], in_=result[:, cols])
+                    store(c, cols)
+            else:
+                nc.vector.tensor_scalar(
+                    out=logs[c][:], in0=logs[c][:], scalar1=gain_col[:], scalar2=bias_col[:], op0=ALU.mult, op1=ALU.add
+                )
+                store(c, slice(0, CHUNKS[c]))
 
-        done = set()
-
-        def ahead(widen, u):
-            if u < UNITS and (widen, source(u)[0]) not in done:
-                done.add((widen, source(u)[0]))
-                widen(source(u)[0])
-
-        for u in range(2):
-            ahead(widen_on_scalar, u)
-            ahead(widen_on_vector, u)
+        for u in range(LEAD):
+            widen(u)
         for s in range(UNITS + 2):
             if s < UNITS:
                 interleave_on_vector(s)
-            for u in range(s + VECTOR_LEAD + 1):
-                ahead(widen_on_vector, u)
-            if s + 1 in TENSOR_UNITS:
-                interleave_on_tensor(s + 1)
-            ahead(widen_on_scalar, s + SCALAR_LEAD)
+            if s + LEAD < UNITS:
+                widen(s + LEAD)
+            if s + LEAD in TENSOR_UNITS:
+                interleave_on_tensor(s + LEAD)
             if s + 1 in TENSOR_UNITS:
                 fetch_from_tensor(s + 1)
             if s == W_STEP:
@@ -280,14 +258,8 @@ def tile_fp8_log_mel_d3_kernel(tc, P_bytes, P_scale, W, floor, gain, bias, out):
                 quantize(s - 1)
             if s == W_STEP + 1:
                 quantize_w()
-            if s == UNITS // 2:
                 nc.vector.tensor_copy(out=gain_f32[:], in_=gain_col[:])
-            for c in range(len(CHUNKS)):
-                if s == max(PASSES * c + PASSES, W_STEP + 1):
-                    multiply(c)
-            for c in range(len(CHUNKS)):
-                if s == log_step(c):
-                    logarithm(c)
-            for c in range(len(CHUNKS)):
-                if s == finish_step(c):
-                    finish(c)
+            for step_of, emit in ((multiply_step, multiply), (log_step, logarithm), (finish_step, finish)):
+                for c in range(len(CHUNKS)):
+                    if step_of(c) == s:
+                        emit(c)

@@ -23,51 +23,13 @@ RUN = 4
 FULL = 1024
 
 SPANS = [256, FULL - 256] + [FULL] * 7
-SHORT_SPANS = 2
 CHUNKS = [256, 256, 512] + [FULL] * 6 + [512, 256, 128, 128]
-UNITS = len(CHUNKS) * PASSES
-AFTER_FULL = max(c for c, frames in enumerate(CHUNKS) if frames == FULL) + 1
-assert sum(CHUNKS) == T and sum(SPANS) == T
-
+FIRST_FULL = CHUNKS.index(FULL)
+AFTER_FULL = FIRST_FULL + CHUNKS.count(FULL)
 HEAD_PLANES = 2
-SECOND_EVERY = 4
-SCALAR_FINISH = range(AFTER_FULL - 3, AFTER_FULL)
 TENSOR_FRAMES = 256
-TENSOR_UNITS = [PASSES * c for c, frames in enumerate(CHUNKS) if frames == FULL]
-
-LEAD = 2
-LAST_WIDENING = PASSES * AFTER_FULL + 1 - LEAD
-W_STEP = 2
-EARLY_LOADS = PASSES * SHORT_SPANS
-LOG_LAG = 4
-FINISH_LAG = 5
-
-
-def vector_planes(v):
-    span, g = divmod(v, PASSES)
-    if span < SHORT_SPANS:
-        return HEAD_PLANES
-    return 2 if g == 0 and (span + 1) % SECOND_EVERY == 0 else 1
-
-
-def multiply_step(c):
-    return max(PASSES * c + PASSES, W_STEP + 1)
-
-
-def log_step(c):
-    if c >= AFTER_FULL:
-        return PASSES * c + LOG_LAG - 1
-    if c in SCALAR_FINISH:
-        return max(PASSES * c + LOG_LAG, LAST_WIDENING)
-    return PASSES * c + LOG_LAG
-
-
-def finish_step(c):
-    if c >= AFTER_FULL:
-        return UNITS + 1
-    if c in SCALAR_FINISH:
-        return log_step(min(c + 1, SCALAR_FINISH[-1]))
-    return PASSES * c + FINISH_LAG
+POOL_FRAMES = 384
+TAIL_PLANES = 1
 
 
 def tile_fp8_log_mel_d3_kernel(tc, P_bytes, P_scale, W, floor, gain, bias, out):
@@ -75,40 +37,43 @@ def tile_fp8_log_mel_d3_kernel(tc, P_bytes, P_scale, W, floor, gain, bias, out):
     chunk_start = [sum(CHUNKS[:c]) for c in range(len(CHUNKS))]
     span_start = [sum(SPANS[:n]) for n in range(len(SPANS))]
 
-    def source(u):
-        c, g = divmod(u, PASSES)
+    def span_of(c):
         span = max(n for n in range(len(SPANS)) if span_start[n] <= chunk_start[c])
-        return PASSES * span + g, chunk_start[c] - span_start[span]
+        return span, chunk_start[c] - span_start[span]
 
     with ExitStack() as ctx:
         keep = ctx.enter_context(tc.tile_pool(name="keep", bufs=1))
-        work = ctx.enter_context(tc.tile_pool(name="work", bufs=5))
+        work = ctx.enter_context(tc.tile_pool(name="work", bufs=4))
+        psum_scale = ctx.enter_context(tc.psum_pool(name="psum_scale", bufs=1))
         psum_moved = ctx.enter_context(tc.psum_pool(name="psum_moved", bufs=2))
-        psum_mel = ctx.enter_context(tc.psum_pool(name="psum_mel", bufs=6))
+        psum_mel = ctx.enter_context(tc.psum_pool(name="psum_mel", bufs=5))
         ctx.enter_context(tc.manual_schedule())
 
         p_rows = P_bytes.rearrange("(g p t) n -> g p t n", p=P, t=PACK)
         raw = {}
 
-        def load(v):
-            span, g = divmod(v, PASSES)
-            raw[v] = keep.tile([P, PACK, SPANS[span]], U8, name="p_bytes_%d" % v)
-            nc.sync.dma_start(out=raw[v][:], in_=p_rows[g][:, :, span_start[span] : span_start[span] + SPANS[span]])
+        def load(span):
+            for g in range(PASSES):
+                raw[span, g] = keep.tile([P, PACK, SPANS[span]], U8, name="p_bytes_%d_%d" % (span, g))
+                nc.sync.dma_start(
+                    out=raw[span, g][:], in_=p_rows[g][:, :, span_start[span] : span_start[span] + SPANS[span]]
+                )
 
         row_scale = keep.tile([P, PASSES, PACK], F32)
         nc.scalar.dma_start(out=row_scale[:], in_=P_scale.rearrange("(g p t) o -> p g (t o)", p=P, t=PACK))
-        for v in range(EARLY_LOADS):
-            load(v)
+        load(0)
+        load(1)
         w_rows = keep.tile([P, F], BF16, align_bytes=64)
         nc.sync.dma_start(out=w_rows[:], in_=W)
+        load(2)
         floor_col = keep.tile([P, 1], BF16)
         gain_col = keep.tile([P, 1], BF16)
         bias_col = keep.tile([P, 1], BF16)
         nc.sync.dma_start(out=floor_col[:], in_=floor.rearrange("(p o) -> p o", o=1))
         nc.sync.dma_start(out=gain_col[:], in_=gain.rearrange("(p o) -> p o", o=1))
         nc.sync.dma_start(out=bias_col[:], in_=bias.rearrange("(p o) -> p o", o=1))
-        for v in range(EARLY_LOADS, PASSES * len(SPANS)):
-            load(v)
+        for span in range(3, len(SPANS)):
+            load(span)
 
         one = keep.tile([P, 1], F32)
         warm = keep.tile([P, 1], F32)
@@ -140,64 +105,105 @@ def tile_fp8_log_mel_d3_kernel(tc, P_bytes, P_scale, W, floor, gain, bias, out):
         def quantize_w():
             nc.vector.quantize_mx(out=w_codes[:].bitcast(FP8X4), scales=w_scales[:], in_=w_grouped[:])
 
+        scale_rows = keep.tile([P, P // (PACK * RUN), PACK, RUN], F32)
+        scale_cols = keep.tile([P, P], F32)
+        scale_bank = psum_scale.tile([P, P // (PACK * RUN), PACK, RUN], F32, name="scale_bank")
+        there = {}
+
+        def spread_scale():
+            nc.vector.tensor_copy(
+                out=scale_rows[:],
+                in_=row_scale[:, 0, :].unsqueeze(1).unsqueeze(3).to_broadcast([P, P // (PACK * RUN), PACK, RUN]),
+            )
+            there[0] = psum_moved.tile([P, P], F32, name="moved")
+            nc.tensor.transpose(there[0][:], scale_rows[:].rearrange("p r t i -> p (r t i)"), ident_f32[:])
+
+        def return_scale():
+            nc.scalar.copy(out=scale_cols[:], in_=there[0][:])
+            nc.tensor.transpose(scale_bank[:].rearrange("p r t i -> p (r t i)"), scale_cols[:], ident_f32[:])
+
         wide, grouped, moved, codes, scales, mel, logs = {}, {}, {}, {}, {}, {}, {}
 
-        def widen(u):
-            v = source(u)[0]
-            if v in wide:
-                return
-            wide[v] = work.tile([P, PACK, SPANS[v // PASSES]], BF16, name="wide")
-            for t in range(PACK):
-                plane, scale = raw[v][:, t, :].bitcast(FP8), row_scale[:, v % PASSES, t : t + 1]
-                if t < PACK - vector_planes(v):
-                    nc.scalar.activation(out=wide[v][:, t, :], in_=plane, func=ACT.Copy, scale=scale)
-                else:
-                    nc.vector.tensor_scalar(out=wide[v][:, t, :], in0=plane, scalar1=scale, scalar2=None, op0=ALU.mult)
+        def wide_tile(span, g):
+            if (span, g) not in wide:
+                wide[span, g] = work.tile([P, PACK, SPANS[span]], BF16, name="wide", bufs=5)
+            return wide[span, g]
 
-        def grouped_tile(u):
-            if u not in grouped:
-                grouped[u] = work.tile([P, CHUNKS[u // PASSES], PACK], BF16, name="grouped", align_bytes=64)
-            return grouped[u]
-
-        def vector_frames(u):
-            return CHUNKS[u // PASSES] - (TENSOR_FRAMES if u in TENSOR_UNITS else 0)
-
-        def interleave_on_vector(u):
-            v, first = source(u)
-            frames = vector_frames(u)
-            nc.vector.tensor_copy(
-                out=grouped_tile(u)[:, :frames, :].rearrange("p (r i) t -> p r t i", i=RUN),
-                in_=wide[v][:, :, first : first + frames].rearrange("p t (r i) -> p r t i", i=RUN),
-            )
-
-        def interleave_on_tensor(u):
-            v, first = source(u)
-            first = first + vector_frames(u)
-            frames = BANK // PACK
-            moved[u] = psum_moved.tile([P, TENSOR_FRAMES * PACK], BF16, name="moved")
-            for n0 in range(0, TENSOR_FRAMES, frames):
-                nc.tensor.matmul(
-                    out=moved[u][:, n0 * PACK : n0 * PACK + BANK],
-                    lhsT=ident_bf16[:],
-                    rhs=wide[v][:, :, first + n0 : first + n0 + frames].rearrange("p t n -> p n t"),
-                    start=True,
-                    stop=True,
+        def widen_on_scalar(span, g, planes):
+            for t in planes:
+                nc.scalar.activation(
+                    out=wide_tile(span, g)[:, t, :], in_=raw[span, g][:, t, :].bitcast(FP8), func=ACT.Copy,
+                    scale=row_scale[:, g, t : t + 1],
                 )
 
-        def fetch_from_tensor(u):
+        def widen_on_vector(span, g, planes):
+            for t in planes:
+                nc.vector.tensor_scalar(
+                    out=wide_tile(span, g)[:, t, :], in0=raw[span, g][:, t, :].bitcast(FP8),
+                    scalar1=row_scale[:, g, t : t + 1], scalar2=None, op0=ALU.mult,
+                )
+
+        def cast(span, g, first):
             nc.scalar.copy(
-                out=grouped_tile(u)[:, vector_frames(u) :, :].rearrange("p n t -> p (n t)").bitcast(F32),
-                in_=moved[u][:].bitcast(F32),
+                out=wide_tile(span, g)[:, first:, :].rearrange("p t n -> p (t n)"),
+                in_=raw[span, g][:, first:, :].rearrange("p t n -> p (t n)").bitcast(FP8),
             )
 
-        def quantize(u):
-            frames = CHUNKS[u // PASSES]
-            codes[u] = work.tile([P, frames], U32, name="codes", align_bytes=64)
-            scales[u] = work.tile([P, frames], U8, name="scales", align_bytes=64)
+        def scale_planes(span, g, first):
+            for t in range(first, PACK):
+                plane = wide[span, g][:, t, :]
+                nc.vector.tensor_scalar(out=plane, in0=plane, scalar1=row_scale[:, g, t : t + 1], scalar2=None, op0=ALU.mult)
+
+        def grouped_tile(c, g):
+            if (c, g) not in grouped:
+                grouped[c, g] = work.tile([P, CHUNKS[c], PACK], BF16, name="grouped", align_bytes=64)
+            return grouped[c, g]
+
+        def planes_of(c, g, n0, n1):
+            span, first = span_of(c)
+            return wide[span, g][:, :, first + n0 : first + n1]
+
+        def interleave_on_vector(c, g, n0, n1):
+            nc.vector.tensor_copy(
+                out=grouped_tile(c, g)[:, n0:n1, :].rearrange("p (r i) t -> p r t i", i=RUN),
+                in_=planes_of(c, g, n0, n1).rearrange("p t (r i) -> p r t i", i=RUN),
+            )
+
+        def scale_and_interleave(c):
+            frames = CHUNKS[c]
+            nc.vector.tensor_tensor(
+                out=grouped_tile(c, 0)[:].rearrange("p (r i) t -> p r t i", i=RUN),
+                in0=planes_of(c, 0, 0, frames).rearrange("p t (r i) -> p r t i", i=RUN),
+                in1=scale_bank[:, 0:1, :, :].to_broadcast([P, frames // RUN, PACK, RUN]),
+                op=ALU.mult,
+            )
+
+        def interleave_on_pool(c, g, n0, n1):
+            nc.gpsimd.tensor_scalar(
+                out=grouped_tile(c, g)[:, n0:n1, :], in0=planes_of(c, g, n0, n1).rearrange("p t n -> p n t"),
+                scalar1=1.0, scalar2=0.0, op0=ALU.mult, op1=ALU.add,
+            )
+
+        def interleave_on_tensor(c, g, n0):
+            frames = BANK // PACK
+            moved[c] = psum_moved.tile([P, TENSOR_FRAMES * PACK], BF16, name="moved")
+            for k in range(0, TENSOR_FRAMES, frames):
+                nc.tensor.matmul(
+                    out=moved[c][:, k * PACK : k * PACK + BANK], lhsT=ident_bf16[:],
+                    rhs=planes_of(c, g, n0 + k, n0 + k + frames).rearrange("p t n -> p n t"), start=True, stop=True,
+                )
+
+        def fetch_from_tensor(c, g, n0):
+            nc.scalar.copy(
+                out=grouped_tile(c, g)[:, n0 : n0 + TENSOR_FRAMES, :].rearrange("p n t -> p (n t)").bitcast(F32),
+                in_=moved[c][:].bitcast(F32),
+            )
+
+        def quantize(c, g):
+            codes[c, g] = work.tile([P, CHUNKS[c]], U32, name="codes", align_bytes=64)
+            scales[c, g] = work.tile([P, CHUNKS[c]], U8, name="scales", align_bytes=64)
             nc.vector.quantize_mx(
-                out=codes[u][:].bitcast(FP8X4),
-                scales=scales[u][:],
-                in_=grouped[u][:].rearrange("p n t -> p (n t)"),
+                out=codes[c, g][:].bitcast(FP8X4), scales=scales[c, g][:], in_=grouped[c, g][:].rearrange("p n t -> p (n t)")
             )
 
         def banks(c):
@@ -209,57 +215,125 @@ def tile_fp8_log_mel_d3_kernel(tc, P_bytes, P_scale, W, floor, gain, bias, out):
                 acc = psum_mel.tile([P, cols.stop - cols.start], F32, name="mel")
                 mel[c].append(acc)
                 for g in range(PASSES):
-                    u = PASSES * c + g
                     nc.tensor.matmul_mx(
-                        out=acc[:],
-                        lhsT=w_codes[:, g * N : (g + 1) * N].bitcast(FP8X4),
-                        lhsT_scale=w_scales[:, g * N : (g + 1) * N],
-                        rhs=codes[u][:, cols].bitcast(FP8X4),
-                        rhs_scale=scales[u][:, cols],
-                        start=(g == 0),
-                        stop=(g == PASSES - 1),
+                        out=acc[:], lhsT=w_codes[:, g * N : (g + 1) * N].bitcast(FP8X4),
+                        lhsT_scale=w_scales[:, g * N : (g + 1) * N], rhs=codes[c, g][:, cols].bitcast(FP8X4),
+                        rhs_scale=scales[c, g][:, cols], start=(g == 0), stop=(g == PASSES - 1),
                     )
 
+        head_logs = keep.tile([P, FULL], F32)
+
         def logarithm(c):
-            logs[c] = keep.tile([P, CHUNKS[c]], F32, name="logs_%d" % c)
+            if c < FIRST_FULL:
+                logs[c] = head_logs[:, chunk_start[c] : chunk_start[c] + CHUNKS[c]]
+            else:
+                tile = keep.tile([P, CHUNKS[c]], F32, name="logs_%d" % c)
+                logs[c] = tile[:]
             for acc, cols in zip(mel[c], banks(c)):
                 nc.scalar.activation(out=logs[c][:, cols], in_=acc[:], func=ACT.Ln, bias=floor_col[:])
 
-        def store(c, cols):
-            nc.sync.dma_start(out=out[:, chunk_start[c] + cols.start : chunk_start[c] + cols.stop], in_=logs[c][:, cols])
+        def store(values, start):
+            nc.sync.dma_start(out=out[:, start : start + values.shape[1]], in_=values)
 
-        def finish(c):
-            if c in SCALAR_FINISH:
-                for cols in banks(c):
-                    nc.scalar.activation(
-                        out=logs[c][:, cols], in_=logs[c][:, cols], func=ACT.Identity, scale=gain_f32[:], bias=bias_col[:]
-                    )
-                    store(c, cols)
-            else:
-                nc.vector.tensor_scalar(
-                    out=logs[c][:], in0=logs[c][:], scalar1=gain_col[:], scalar2=bias_col[:], op0=ALU.mult, op1=ALU.add
+        def finish(engine, values, start):
+            engine.tensor_scalar(out=values, in0=values, scalar1=gain_col[:], scalar2=bias_col[:], op0=ALU.mult, op1=ALU.add)
+            store(values, start)
+
+        def finish_on_scalar(c):
+            for cols in banks(c):
+                nc.scalar.activation(
+                    out=logs[c][:, cols], in_=logs[c][:, cols], func=ACT.Identity, scale=gain_f32[:], bias=bias_col[:]
                 )
-                store(c, slice(0, CHUNKS[c]))
+                store(logs[c][:, cols], chunk_start[c] + cols.start)
 
-        for u in range(LEAD):
-            widen(u)
-        for s in range(UNITS + 2):
-            if s < UNITS:
-                interleave_on_vector(s)
-            if s + LEAD < UNITS:
-                widen(s + LEAD)
-            if s + LEAD in TENSOR_UNITS:
-                interleave_on_tensor(s + LEAD)
-            if s + 1 in TENSOR_UNITS:
-                fetch_from_tensor(s + 1)
-            if s == W_STEP:
-                turn_w()
-            if 1 <= s <= UNITS:
-                quantize(s - 1)
-            if s == W_STEP + 1:
+        def cast_planes(c):
+            return 1 + c % 2
+
+        pool_end = POOL_FRAMES
+        tensor_end = POOL_FRAMES + TENSOR_FRAMES
+
+        scalar_planes, vector_planes = range(PACK - HEAD_PLANES), range(PACK - HEAD_PLANES, PACK)
+        for g in range(PASSES):
+            widen_on_scalar(0, g, scalar_planes)
+            widen_on_vector(0, g, vector_planes)
+        interleave_on_vector(0, 0, 0, CHUNKS[0])
+        spread_scale()
+        widen_on_scalar(1, 0, scalar_planes)
+        widen_on_vector(1, 0, vector_planes)
+        interleave_on_vector(0, 1, 0, CHUNKS[0])
+        return_scale()
+        widen_on_scalar(1, 1, scalar_planes)
+        widen_on_vector(1, 1, vector_planes)
+        quantize(0, 0)
+        turn_w()
+        head_units = [(c, g) for c in range(FIRST_FULL) for g in range(PASSES)]
+        for before, unit in zip(head_units[1:-1], head_units[2:]):
+            interleave_on_vector(*unit, 0, CHUNKS[unit[0]])
+            quantize(*before)
+            if before == (1, 0):
                 quantize_w()
                 nc.vector.tensor_copy(out=gain_f32[:], in_=gain_col[:])
-            for step_of, emit in ((multiply_step, multiply), (log_step, logarithm), (finish_step, finish)):
-                for c in range(len(CHUNKS)):
-                    if step_of(c) == s:
-                        emit(c)
+                multiply(0)
+            if before == (1, 1):
+                multiply(1)
+
+        def prepare_first(c):
+            span = span_of(c)[0]
+            first = PACK - cast_planes(c)
+            cast(span, 1, first)
+            cast(span, 0, 0)
+            widen_on_scalar(span, 1, range(first - 1))
+
+        def prepare_last(c):
+            span = span_of(c)[0]
+            first = PACK - cast_planes(c)
+            widen_on_scalar(span, 1, [first - 1])
+
+        prepare_first(FIRST_FULL)
+        prepare_last(FIRST_FULL)
+        logarithm(0)
+        logarithm(1)
+        last_span = len(SPANS) - 1
+        for c in range(FIRST_FULL, AFTER_FULL):
+            span = span_of(c)[0]
+            scale_planes(span, 1, PACK - cast_planes(c))
+            interleave_on_tensor(c, 1, pool_end)
+            interleave_on_pool(c, 1, 0, pool_end)
+            quantize(c - 1, 1)
+            multiply(c - 1)
+            scale_and_interleave(c)
+            if c - 2 == FIRST_FULL - 1:
+                finish(nc.gpsimd, head_logs[:], 0)
+            elif c - 2 >= FIRST_FULL:
+                finish(nc.gpsimd, logs[c - 2], chunk_start[c - 2])
+            if c + 1 < AFTER_FULL:
+                prepare_first(c + 1)
+                fetch_from_tensor(c, 1, pool_end)
+                prepare_last(c + 1)
+            else:
+                widen_on_scalar(last_span, 0, range(PACK - TAIL_PLANES))
+                fetch_from_tensor(c, 1, pool_end)
+                widen_on_scalar(last_span, 1, range(PACK - TAIL_PLANES))
+            logarithm(c - 1)
+            interleave_on_vector(c, 1, tensor_end, FULL)
+            quantize(c, 0)
+
+        last_full = AFTER_FULL - 1
+        widen_on_vector(last_span, 0, range(PACK - TAIL_PLANES, PACK))
+        quantize(last_full, 1)
+        multiply(last_full)
+        widen_on_vector(last_span, 1, range(PACK - TAIL_PLANES, PACK))
+        finish_on_scalar(last_full - 1)
+        logarithm(last_full)
+        finish_on_scalar(last_full)
+        tail_units = [(c, g) for c in range(AFTER_FULL, len(CHUNKS)) for g in range(PASSES)]
+        interleave_on_vector(*tail_units[0], 0, CHUNKS[AFTER_FULL])
+        for before, unit in zip(tail_units, tail_units[1:] + [None]):
+            if unit is not None:
+                interleave_on_vector(*unit, 0, CHUNKS[unit[0]])
+            quantize(*before)
+            if before[1] == PASSES - 1:
+                multiply(before[0])
+                logarithm(before[0])
+        for c in range(AFTER_FULL, len(CHUNKS)):
+            finish(nc.vector, logs[c], chunk_start[c])

@@ -28,8 +28,11 @@ FIRST_FULL = CHUNKS.index(FULL)
 AFTER_FULL = FIRST_FULL + CHUNKS.count(FULL)
 HEAD_PLANES = 2
 TENSOR_FRAMES = 256
-POOL_FRAMES = 384
-TAIL_PLANES = 1
+POOL_FRAMES = 512
+POOL_FRAMES_ALONE = 640
+SCALAR_CHUNKS = 3
+FINISH_LAG = 2
+TAIL_PLANES = 0
 
 
 def tile_fp8_log_mel_d3_kernel(tc, P_bytes, P_scale, W, floor, gain, bias, out):
@@ -247,10 +250,13 @@ def tile_fp8_log_mel_d3_kernel(tc, P_bytes, P_scale, W, floor, gain, bias, out):
                 store(logs[c][:, cols], chunk_start[c] + cols.start)
 
         def cast_planes(c):
-            return 1 + c % 2
+            return 2
 
-        pool_end = POOL_FRAMES
-        tensor_end = POOL_FRAMES + TENSOR_FRAMES
+        def pool_finishes(c):
+            return FIRST_FULL - 1 <= c - FINISH_LAG < AFTER_FULL - SCALAR_CHUNKS
+
+        def pool_frames(c):
+            return POOL_FRAMES if pool_finishes(c) else POOL_FRAMES_ALONE
 
         scalar_planes, vector_planes = range(PACK - HEAD_PLANES), range(PACK - HEAD_PLANES, PACK)
         for g in range(PASSES):
@@ -280,8 +286,8 @@ def tile_fp8_log_mel_d3_kernel(tc, P_bytes, P_scale, W, floor, gain, bias, out):
         def prepare_first(c):
             span = span_of(c)[0]
             first = PACK - cast_planes(c)
-            cast(span, 1, first)
             cast(span, 0, 0)
+            cast(span, 1, first)
             widen_on_scalar(span, 1, range(first - 1))
 
         def prepare_last(c):
@@ -291,21 +297,22 @@ def tile_fp8_log_mel_d3_kernel(tc, P_bytes, P_scale, W, floor, gain, bias, out):
 
         prepare_first(FIRST_FULL)
         prepare_last(FIRST_FULL)
-        logarithm(0)
-        logarithm(1)
         last_span = len(SPANS) - 1
         for c in range(FIRST_FULL, AFTER_FULL):
             span = span_of(c)[0]
+            pool_end = pool_frames(c)
+            tensor_end = pool_end + TENSOR_FRAMES
             scale_planes(span, 1, PACK - cast_planes(c))
             interleave_on_tensor(c, 1, pool_end)
             interleave_on_pool(c, 1, 0, pool_end)
             quantize(c - 1, 1)
             multiply(c - 1)
             scale_and_interleave(c)
-            if c - 2 == FIRST_FULL - 1:
-                finish(nc.gpsimd, head_logs[:], 0)
-            elif c - 2 >= FIRST_FULL:
-                finish(nc.gpsimd, logs[c - 2], chunk_start[c - 2])
+            if pool_finishes(c):
+                if c - FINISH_LAG < FIRST_FULL:
+                    finish(nc.gpsimd, head_logs[:], 0)
+                else:
+                    finish(nc.gpsimd, logs[c - FINISH_LAG], chunk_start[c - FINISH_LAG])
             if c + 1 < AFTER_FULL:
                 prepare_first(c + 1)
                 fetch_from_tensor(c, 1, pool_end)
@@ -314,8 +321,10 @@ def tile_fp8_log_mel_d3_kernel(tc, P_bytes, P_scale, W, floor, gain, bias, out):
                 widen_on_scalar(last_span, 0, range(PACK - TAIL_PLANES))
                 fetch_from_tensor(c, 1, pool_end)
                 widen_on_scalar(last_span, 1, range(PACK - TAIL_PLANES))
-            logarithm(c - 1)
-            interleave_on_vector(c, 1, tensor_end, FULL)
+            for done in range(c) if c == FIRST_FULL else [c - 1]:
+                logarithm(done)
+            if tensor_end < FULL:
+                interleave_on_vector(c, 1, tensor_end, FULL)
             quantize(c, 0)
 
         last_full = AFTER_FULL - 1
@@ -323,7 +332,8 @@ def tile_fp8_log_mel_d3_kernel(tc, P_bytes, P_scale, W, floor, gain, bias, out):
         quantize(last_full, 1)
         multiply(last_full)
         widen_on_vector(last_span, 1, range(PACK - TAIL_PLANES, PACK))
-        finish_on_scalar(last_full - 1)
+        for c in range(AFTER_FULL - SCALAR_CHUNKS, last_full):
+            finish_on_scalar(c)
         logarithm(last_full)
         finish_on_scalar(last_full)
         tail_units = [(c, g) for c in range(AFTER_FULL, len(CHUNKS)) for g in range(PASSES)]

@@ -19,7 +19,7 @@ P = 128
 PACK = 4
 PASSES = F // (P * PACK)
 BANK = 512
-RUN = 4
+RUN = 2
 FULL = 1024
 
 SPANS = [256, FULL - 256] + [FULL] * 7
@@ -30,9 +30,10 @@ HEAD_PLANES = 2
 TENSOR_FRAMES = 256
 POOL_FRAMES = 512
 POOL_FRAMES_ALONE = 640
-SCALAR_CHUNKS = 3
+SCALAR_CHUNKS = 2
 FINISH_LAG = 2
 TAIL_PLANES = 0
+TAIL_PLANES0 = 0
 
 
 def tile_fp8_log_mel_d3_kernel(tc, P_bytes, P_scale, W, floor, gain, bias, out):
@@ -250,7 +251,7 @@ def tile_fp8_log_mel_d3_kernel(tc, P_bytes, P_scale, W, floor, gain, bias, out):
                 store(logs[c][:, cols], chunk_start[c] + cols.start)
 
         def cast_planes(c):
-            return 2
+            return 1
 
         def pool_finishes(c):
             return FIRST_FULL - 1 <= c - FINISH_LAG < AFTER_FULL - SCALAR_CHUNKS
@@ -287,7 +288,6 @@ def tile_fp8_log_mel_d3_kernel(tc, P_bytes, P_scale, W, floor, gain, bias, out):
             span = span_of(c)[0]
             first = PACK - cast_planes(c)
             cast(span, 0, 0)
-            cast(span, 1, first)
             widen_on_scalar(span, 1, range(first - 1))
 
         def prepare_last(c):
@@ -302,7 +302,7 @@ def tile_fp8_log_mel_d3_kernel(tc, P_bytes, P_scale, W, floor, gain, bias, out):
             span = span_of(c)[0]
             pool_end = pool_frames(c)
             tensor_end = pool_end + TENSOR_FRAMES
-            scale_planes(span, 1, PACK - cast_planes(c))
+            widen_on_vector(span, 1, range(PACK - cast_planes(c), PACK))
             interleave_on_tensor(c, 1, pool_end)
             interleave_on_pool(c, 1, 0, pool_end)
             quantize(c - 1, 1)
@@ -318,7 +318,7 @@ def tile_fp8_log_mel_d3_kernel(tc, P_bytes, P_scale, W, floor, gain, bias, out):
                 fetch_from_tensor(c, 1, pool_end)
                 prepare_last(c + 1)
             else:
-                widen_on_scalar(last_span, 0, range(PACK - TAIL_PLANES))
+                widen_on_scalar(last_span, 0, range(PACK - TAIL_PLANES0))
                 fetch_from_tensor(c, 1, pool_end)
                 widen_on_scalar(last_span, 1, range(PACK - TAIL_PLANES))
             for done in range(c) if c == FIRST_FULL else [c - 1]:
@@ -328,7 +328,7 @@ def tile_fp8_log_mel_d3_kernel(tc, P_bytes, P_scale, W, floor, gain, bias, out):
             quantize(c, 0)
 
         last_full = AFTER_FULL - 1
-        widen_on_vector(last_span, 0, range(PACK - TAIL_PLANES, PACK))
+        widen_on_vector(last_span, 0, range(PACK - TAIL_PLANES0, PACK))
         quantize(last_full, 1)
         multiply(last_full)
         widen_on_vector(last_span, 1, range(PACK - TAIL_PLANES, PACK))

@@ -20,6 +20,7 @@ PACK = 4
 PASSES = F // (P * PACK)
 BANK = 512
 RUN = 2
+POOL_RUN = 4
 FULL = 1024
 
 SPANS = [256, FULL - 256] + [FULL] * 7
@@ -28,11 +29,11 @@ FIRST_FULL = CHUNKS.index(FULL)
 AFTER_FULL = FIRST_FULL + CHUNKS.count(FULL)
 HEAD_PLANES = 2
 TENSOR_FRAMES = 256
-POOL_FRAMES = 512
-POOL_FRAMES_ALONE = 640
+POOL_FRAMES = 608
+POOL_FRAMES_ALONE = 704
 SCALAR_CHUNKS = 2
 FINISH_LAG = 2
-TAIL_PLANES = 0
+TAIL_PLANES = 1
 TAIL_PLANES0 = 0
 
 
@@ -184,7 +185,8 @@ def tile_fp8_log_mel_d3_kernel(tc, P_bytes, P_scale, W, floor, gain, bias, out):
 
         def interleave_on_pool(c, g, n0, n1):
             nc.gpsimd.tensor_scalar(
-                out=grouped_tile(c, g)[:, n0:n1, :], in0=planes_of(c, g, n0, n1).rearrange("p t n -> p n t"),
+                out=grouped_tile(c, g)[:, n0:n1, :].rearrange("p (r i) t -> p r t i", i=POOL_RUN),
+                in0=planes_of(c, g, n0, n1).rearrange("p t (r i) -> p r t i", i=POOL_RUN),
                 scalar1=1.0, scalar2=0.0, op0=ALU.mult, op1=ALU.add,
             )
 

@@ -23,18 +23,18 @@ RUN = 2
 POOL_RUN = 4
 FULL = 1024
 
-SPANS = [256, FULL - 256] + [FULL] * 7
+SPANS = [256, 256, 512] + [FULL] * 6 + [1024]
 CHUNKS = [256, 256, 512] + [FULL] * 6 + [512, 256, 128, 128]
 FIRST_FULL = CHUNKS.index(FULL)
 AFTER_FULL = FIRST_FULL + CHUNKS.count(FULL)
-HEAD_PLANES = 2
-TENSOR_FRAMES = 256
-POOL_FRAMES = 608
-POOL_FRAMES_ALONE = 704
-SCALAR_CHUNKS = 2
-FINISH_LAG = 2
-TAIL_PLANES = 1
-TAIL_PLANES0 = 0
+FUSED = range(3, 9)
+HEADV = {(0, 0): 2, (0, 1): 2, (1, 0): 2, (1, 1): 2, (2, 0): 2, (2, 1): 2}
+TENSOR = {2: 0, 3: 256, 4: 256, 5: 256, 6: 256, 7: 256, 8: 256, 9: 0}
+POOL = {2: 384, 3: 704, 4: 608, 5: 608, 6: 608, 7: 608, 8: 608, 9: 384}
+POOL_FIN = {4: 2, 5: 3, 6: 4, 7: 5, 8: 6}
+VPL = {2: 2, 3: 2, 4: 1, 5: 1, 6: 1, 7: 1, 8: 1, 9: 1}
+TAILV = (0, 1)
+SCALAR_UNITS = [(11, 1), (12, 0), (12, 1)]
 
 
 def tile_fp8_log_mel_d3_kernel(tc, P_bytes, P_scale, W, floor, gain, bias, out):
@@ -64,20 +64,22 @@ def tile_fp8_log_mel_d3_kernel(tc, P_bytes, P_scale, W, floor, gain, bias, out):
                     out=raw[span, g][:], in_=p_rows[g][:, :, span_start[span] : span_start[span] + SPANS[span]]
                 )
 
-        row_scale = keep.tile([P, PASSES, PACK], F32)
-        nc.scalar.dma_start(out=row_scale[:], in_=P_scale.rearrange("(g p t) o -> p g (t o)", p=P, t=PACK))
+        scale_tile = keep.tile([P, PASSES, 2 * PACK], F32)
+        row_scale = scale_tile[:, :, :PACK]
+        nc.scalar.dma_start(out=row_scale, in_=P_scale.rearrange("(g p t) o -> p g (t o)", p=P, t=PACK))
         load(0)
         load(1)
+        load(2)
+        load(3)
         w_rows = keep.tile([P, F], BF16, align_bytes=64)
         nc.sync.dma_start(out=w_rows[:], in_=W)
-        load(2)
         floor_col = keep.tile([P, 1], BF16)
         gain_col = keep.tile([P, 1], BF16)
         bias_col = keep.tile([P, 1], BF16)
         nc.sync.dma_start(out=floor_col[:], in_=floor.rearrange("(p o) -> p o", o=1))
         nc.sync.dma_start(out=gain_col[:], in_=gain.rearrange("(p o) -> p o", o=1))
         nc.sync.dma_start(out=bias_col[:], in_=bias.rearrange("(p o) -> p o", o=1))
-        for span in range(3, len(SPANS)):
+        for span in range(4, len(SPANS)):
             load(span)
 
         one = keep.tile([P, 1], F32)
@@ -102,9 +104,12 @@ def tile_fp8_log_mel_d3_kernel(tc, P_bytes, P_scale, W, floor, gain, bias, out):
             for g in range(PASSES):
                 for h in range(2):
                     nc.tensor.transpose(turned[:, g, h, :], pairs[:, per_pass * g + h : per_pass * (g + 1) : 2], ident_f32[:])
+            there[1] = turned
+
+        def fetch_w():
             nc.scalar.copy(
                 out=w_grouped[:].bitcast(F32).rearrange("p (g m h) -> p g m h", g=PASSES, h=2),
-                in_=turned[:].rearrange("p g h m -> p g m h"),
+                in_=there[1][:].rearrange("p g h m -> p g m h"),
             )
 
         def quantize_w():
@@ -131,7 +136,7 @@ def tile_fp8_log_mel_d3_kernel(tc, P_bytes, P_scale, W, floor, gain, bias, out):
 
         def wide_tile(span, g):
             if (span, g) not in wide:
-                wide[span, g] = work.tile([P, PACK, SPANS[span]], BF16, name="wide", bufs=5)
+                wide[span, g] = work.tile([P, PACK, SPANS[span]], BF16, name="wide" if span > 1 else "wide_%d_%d" % (span, g), bufs=5 if span > 1 else 1)
             return wide[span, g]
 
         def widen_on_scalar(span, g, planes):
@@ -161,7 +166,7 @@ def tile_fp8_log_mel_d3_kernel(tc, P_bytes, P_scale, W, floor, gain, bias, out):
 
         def grouped_tile(c, g):
             if (c, g) not in grouped:
-                grouped[c, g] = work.tile([P, CHUNKS[c], PACK], BF16, name="grouped", align_bytes=64)
+                grouped[c, g] = work.tile([P, CHUNKS[c], PACK], BF16, name="grouped" if c < 10 else "grouped_%d_%d" % (c, g), align_bytes=64, bufs=4 if c < 10 else 1)
             return grouped[c, g]
 
         def planes_of(c, g, n0, n1):
@@ -190,24 +195,30 @@ def tile_fp8_log_mel_d3_kernel(tc, P_bytes, P_scale, W, floor, gain, bias, out):
                 scalar1=1.0, scalar2=0.0, op0=ALU.mult, op1=ALU.add,
             )
 
+        def interleave_on_scalar(c, g):
+            nc.scalar.copy(
+                out=grouped_tile(c, g)[:].rearrange("p (r i) t -> p r t i", i=POOL_RUN),
+                in_=planes_of(c, g, 0, CHUNKS[c]).rearrange("p t (r i) -> p r t i", i=POOL_RUN),
+            )
+
         def interleave_on_tensor(c, g, n0):
-            frames = BANK // PACK
-            moved[c] = psum_moved.tile([P, TENSOR_FRAMES * PACK], BF16, name="moved")
-            for k in range(0, TENSOR_FRAMES, frames):
+            moved[c] = psum_moved.tile([P, TENSOR[c] * PACK], BF16, name="moved")
+            for k in range(0, TENSOR[c], BANK // PACK):
+                frames = min(BANK // PACK, TENSOR[c] - k)
                 nc.tensor.matmul(
-                    out=moved[c][:, k * PACK : k * PACK + BANK], lhsT=ident_bf16[:],
+                    out=moved[c][:, k * PACK : (k + frames) * PACK], lhsT=ident_bf16[:],
                     rhs=planes_of(c, g, n0 + k, n0 + k + frames).rearrange("p t n -> p n t"), start=True, stop=True,
                 )
 
         def fetch_from_tensor(c, g, n0):
             nc.scalar.copy(
-                out=grouped_tile(c, g)[:, n0 : n0 + TENSOR_FRAMES, :].rearrange("p n t -> p (n t)").bitcast(F32),
+                out=grouped_tile(c, g)[:, n0 : n0 + TENSOR[c], :].rearrange("p n t -> p (n t)").bitcast(F32),
                 in_=moved[c][:].bitcast(F32),
             )
 
         def quantize(c, g):
-            codes[c, g] = work.tile([P, CHUNKS[c]], U32, name="codes", align_bytes=64)
-            scales[c, g] = work.tile([P, CHUNKS[c]], U8, name="scales", align_bytes=64)
+            codes[c, g] = work.tile([P, CHUNKS[c]], U32, name="codes", align_bytes=64, bufs=6)
+            scales[c, g] = work.tile([P, CHUNKS[c]], U8, name="scales", align_bytes=64, bufs=6)
             nc.vector.quantize_mx(
                 out=codes[c, g][:].bitcast(FP8X4), scales=scales[c, g][:], in_=grouped[c, g][:].rearrange("p n t -> p (n t)")
             )
@@ -220,7 +231,8 @@ def tile_fp8_log_mel_d3_kernel(tc, P_bytes, P_scale, W, floor, gain, bias, out):
             for cols in banks(c):
                 acc = psum_mel.tile([P, cols.stop - cols.start], F32, name="mel")
                 mel[c].append(acc)
-                for g in range(PASSES):
+            for g in range(PASSES):
+                for acc, cols in zip(mel[c], banks(c)):
                     nc.tensor.matmul_mx(
                         out=acc[:], lhsT=w_codes[:, g * N : (g + 1) * N].bitcast(FP8X4),
                         lhsT_scale=w_scales[:, g * N : (g + 1) * N], rhs=codes[c, g][:, cols].bitcast(FP8X4),
@@ -252,96 +264,98 @@ def tile_fp8_log_mel_d3_kernel(tc, P_bytes, P_scale, W, floor, gain, bias, out):
                 )
                 store(logs[c][:, cols], chunk_start[c] + cols.start)
 
-        def cast_planes(c):
-            return 1
-
-        def pool_finishes(c):
-            return FIRST_FULL - 1 <= c - FINISH_LAG < AFTER_FULL - SCALAR_CHUNKS
-
-        def pool_frames(c):
-            return POOL_FRAMES if pool_finishes(c) else POOL_FRAMES_ALONE
-
-        scalar_planes, vector_planes = range(PACK - HEAD_PLANES), range(PACK - HEAD_PLANES, PACK)
-        for g in range(PASSES):
-            widen_on_scalar(0, g, scalar_planes)
-            widen_on_vector(0, g, vector_planes)
-        interleave_on_vector(0, 0, 0, CHUNKS[0])
-        spread_scale()
-        widen_on_scalar(1, 0, scalar_planes)
-        widen_on_vector(1, 0, vector_planes)
-        interleave_on_vector(0, 1, 0, CHUNKS[0])
-        return_scale()
-        widen_on_scalar(1, 1, scalar_planes)
-        widen_on_vector(1, 1, vector_planes)
-        quantize(0, 0)
-        turn_w()
-        head_units = [(c, g) for c in range(FIRST_FULL) for g in range(PASSES)]
-        for before, unit in zip(head_units[1:-1], head_units[2:]):
-            interleave_on_vector(*unit, 0, CHUNKS[unit[0]])
-            quantize(*before)
-            if before == (1, 0):
-                quantize_w()
-                nc.vector.tensor_copy(out=gain_f32[:], in_=gain_col[:])
-                multiply(0)
-            if before == (1, 1):
-                multiply(1)
+        def finish_chunk(engine, c):
+            if c < FIRST_FULL:
+                finish(engine, head_logs[:], 0)
+            else:
+                finish(engine, logs[c], chunk_start[c])
 
         def prepare_first(c):
             span = span_of(c)[0]
-            first = PACK - cast_planes(c)
             cast(span, 0, 0)
-            widen_on_scalar(span, 1, range(first - 1))
+            widen_on_scalar(span, 1, range(PACK - VPL[c] - 1))
+            if c == first:
+                turn_w()
+                fetch_w()
 
         def prepare_last(c):
-            span = span_of(c)[0]
-            first = PACK - cast_planes(c)
-            widen_on_scalar(span, 1, [first - 1])
+            widen_on_scalar(span_of(c)[0], 1, [PACK - VPL[c] - 1])
 
-        prepare_first(FIRST_FULL)
-        prepare_last(FIRST_FULL)
+        first, last = FUSED[0], FUSED[-1]
         last_span = len(SPANS) - 1
-        for c in range(FIRST_FULL, AFTER_FULL):
+        head_units = [(c, g) for c in range(first) for g in range(PASSES)]
+
+        def widen_head(unit):
+            widen_on_scalar(*unit, range(PACK - HEADV[unit]))
+            widen_on_vector(*unit, range(PACK - HEADV[unit], PACK))
+
+        widen_head(head_units[0])
+        widen_head(head_units[1])
+        for s, unit in enumerate(head_units):
+            interleave_on_vector(*unit, 0, CHUNKS[unit[0]])
+            if s == 0:
+                spread_scale()
+            if s + 2 < len(head_units):
+                widen_head(head_units[s + 2])
+            if s == 1:
+                return_scale()
+            if s == len(head_units) - 2:
+                prepare_first(first)
+                prepare_last(first)
+            if s >= 1:
+                quantize(*head_units[s - 1])
+
+        for c in FUSED:
             span = span_of(c)[0]
-            pool_end = pool_frames(c)
-            tensor_end = pool_end + TENSOR_FRAMES
-            widen_on_vector(span, 1, range(PACK - cast_planes(c), PACK))
-            interleave_on_tensor(c, 1, pool_end)
+            pool_end = POOL[c]
+            tensor_end = pool_end + TENSOR[c]
+            widen_on_vector(span, 1, range(PACK - VPL[c], PACK))
+            if c == first:
+                quantize_w()
+                for done in range(first - 1):
+                    multiply(done)
+            if TENSOR[c]:
+                interleave_on_tensor(c, 1, pool_end)
             interleave_on_pool(c, 1, 0, pool_end)
             quantize(c - 1, 1)
             multiply(c - 1)
             scale_and_interleave(c)
-            if pool_finishes(c):
-                if c - FINISH_LAG < FIRST_FULL:
-                    finish(nc.gpsimd, head_logs[:], 0)
-                else:
-                    finish(nc.gpsimd, logs[c - FINISH_LAG], chunk_start[c - FINISH_LAG])
-            if c + 1 < AFTER_FULL:
+            if c in POOL_FIN:
+                finish_chunk(nc.gpsimd, POOL_FIN[c])
+            if c < last:
                 prepare_first(c + 1)
+            else:
+                widen_on_scalar(last_span, 0, range(PACK - TAILV[0]))
+            if TENSOR[c]:
                 fetch_from_tensor(c, 1, pool_end)
+            if c < last:
                 prepare_last(c + 1)
             else:
-                widen_on_scalar(last_span, 0, range(PACK - TAIL_PLANES0))
-                fetch_from_tensor(c, 1, pool_end)
-                widen_on_scalar(last_span, 1, range(PACK - TAIL_PLANES))
-            for done in range(c) if c == FIRST_FULL else [c - 1]:
+                widen_on_scalar(last_span, 1, range(PACK - TAILV[1]))
+            if c == last:
+                nc.scalar.copy(out=gain_f32[:], in_=gain_col[:])
+            for done in range(c) if c == first else [c - 1]:
                 logarithm(done)
-            if tensor_end < FULL:
-                interleave_on_vector(c, 1, tensor_end, FULL)
+            if tensor_end < CHUNKS[c]:
+                interleave_on_vector(c, 1, tensor_end, CHUNKS[c])
             quantize(c, 0)
 
-        last_full = AFTER_FULL - 1
-        widen_on_vector(last_span, 0, range(PACK - TAIL_PLANES0, PACK))
-        quantize(last_full, 1)
-        multiply(last_full)
-        widen_on_vector(last_span, 1, range(PACK - TAIL_PLANES, PACK))
-        for c in range(AFTER_FULL - SCALAR_CHUNKS, last_full):
-            finish_on_scalar(c)
-        logarithm(last_full)
-        finish_on_scalar(last_full)
-        tail_units = [(c, g) for c in range(AFTER_FULL, len(CHUNKS)) for g in range(PASSES)]
-        interleave_on_vector(*tail_units[0], 0, CHUNKS[AFTER_FULL])
+        widen_on_vector(last_span, 0, range(PACK - TAILV[0], PACK))
+        quantize(last, 1)
+        multiply(last)
+        widen_on_vector(last_span, 1, range(PACK - TAILV[1], PACK))
+        for c in range(FIRST_FULL, last):
+            if c not in POOL_FIN.values():
+                finish_on_scalar(c)
+        logarithm(last)
+        if last < AFTER_FULL:
+            finish_on_scalar(last)
+        for unit in SCALAR_UNITS:
+            interleave_on_scalar(*unit)
+        tail_units = [(c, g) for c in range(last + 1, len(CHUNKS)) for g in range(PASSES)]
+        interleave_on_vector(*tail_units[0], 0, CHUNKS[last + 1])
         for before, unit in zip(tail_units, tail_units[1:] + [None]):
-            if unit is not None:
+            if unit is not None and unit not in SCALAR_UNITS:
                 interleave_on_vector(*unit, 0, CHUNKS[unit[0]])
             quantize(*before)
             if before[1] == PASSES - 1:

@@ -19,32 +19,47 @@ P = 128
 PACK = 4
 PASSES = F // (P * PACK)
 BANK = 512
-RUN = 2
-POOL_RUN = 4
+BANK_FRAMES = 2 * BANK // PACK
 FULL = 1024
+VECTOR_RUN = 2
+POOL_RUN = 4
 
-SPANS = [256, 256, 512] + [FULL] * 6 + [1024]
-CHUNKS = [256, 256, 512] + [FULL] * 6 + [512, 256, 128, 128]
-FIRST_FULL = CHUNKS.index(FULL)
-AFTER_FULL = FIRST_FULL + CHUNKS.count(FULL)
-FUSED = range(3, 9)
-HEADV = {(0, 0): 2, (0, 1): 2, (1, 0): 2, (1, 1): 2, (2, 0): 2, (2, 1): 2}
-TENSOR = {2: 0, 3: 256, 4: 256, 5: 256, 6: 256, 7: 256, 8: 256, 9: 0}
-POOL = {2: 384, 3: 704, 4: 608, 5: 608, 6: 608, 7: 608, 8: 608, 9: 384}
-POOL_FIN = {4: 2, 5: 3, 6: 4, 7: 5, 8: 6}
-VPL = {2: 2, 3: 2, 4: 1, 5: 1, 6: 1, 7: 1, 8: 1, 9: 1}
-TAILV = (0, 1)
-SCALAR_UNITS = [(11, 1), (12, 0), (12, 1)]
+HEAD = [256, 256, 512]
+TAIL = [512, 256, 128, 128]
+CHUNKS = HEAD + [FULL] * ((T - sum(HEAD) - sum(TAIL)) // FULL) + TAIL
+FIRST = len(HEAD)
+LAST = len(CHUNKS) - len(TAIL) - 1
+SPANS = CHUNKS[: LAST + 1] + [sum(TAIL)]
+TAIL_SPAN = LAST + 1
+assert sum(CHUNKS) == T and sum(SPANS) == T
+
+TENSOR_FRAMES = 96
+POOL_FRAMES = FULL - TENSOR_FRAMES
+FIRST_POOL_FRAMES = POOL_FRAMES - TENSOR_FRAMES
+LATE_CHUNKS = 2
+HEAD_PLANES = 2
+FINISH_LAG = 2
+
+
+def vector_planes(c):
+    return range(PACK - (HEAD_PLANES if c <= FIRST else 1), PACK)
+
+
+def scalar_planes(c):
+    return range(vector_planes(c).start)
+
+
+def pool_frames(c):
+    return FIRST_POOL_FRAMES if c == FIRST else POOL_FRAMES
+
+
+def tensor_frames(c, g):
+    return TENSOR_FRAMES if c <= LAST else min(CHUNKS[c], BANK_FRAMES)
 
 
 def tile_fp8_log_mel_d3_kernel(tc, P_bytes, P_scale, W, floor, gain, bias, out):
     nc = tc.nc
     chunk_start = [sum(CHUNKS[:c]) for c in range(len(CHUNKS))]
-    span_start = [sum(SPANS[:n]) for n in range(len(SPANS))]
-
-    def span_of(c):
-        span = max(n for n in range(len(SPANS)) if span_start[n] <= chunk_start[c])
-        return span, chunk_start[c] - span_start[span]
 
     with ExitStack() as ctx:
         keep = ctx.enter_context(tc.tile_pool(name="keep", bufs=1))
@@ -58,19 +73,16 @@ def tile_fp8_log_mel_d3_kernel(tc, P_bytes, P_scale, W, floor, gain, bias, out):
         raw = {}
 
         def load(span):
+            start = chunk_start[span]
             for g in range(PASSES):
                 raw[span, g] = keep.tile([P, PACK, SPANS[span]], U8, name="p_bytes_%d_%d" % (span, g))
-                nc.sync.dma_start(
-                    out=raw[span, g][:], in_=p_rows[g][:, :, span_start[span] : span_start[span] + SPANS[span]]
-                )
+                nc.sync.dma_start(out=raw[span, g][:], in_=p_rows[g][:, :, start : start + SPANS[span]])
 
         scale_tile = keep.tile([P, PASSES, 2 * PACK], F32)
         row_scale = scale_tile[:, :, :PACK]
         nc.scalar.dma_start(out=row_scale, in_=P_scale.rearrange("(g p t) o -> p g (t o)", p=P, t=PACK))
-        load(0)
-        load(1)
-        load(2)
-        load(3)
+        for span in range(FIRST + 1):
+            load(span)
         w_rows = keep.tile([P, F], BF16, align_bytes=64)
         nc.sync.dma_start(out=w_rows[:], in_=W)
         floor_col = keep.tile([P, 1], BF16)
@@ -79,7 +91,7 @@ def tile_fp8_log_mel_d3_kernel(tc, P_bytes, P_scale, W, floor, gain, bias, out):
         nc.sync.dma_start(out=floor_col[:], in_=floor.rearrange("(p o) -> p o", o=1))
         nc.sync.dma_start(out=gain_col[:], in_=gain.rearrange("(p o) -> p o", o=1))
         nc.sync.dma_start(out=bias_col[:], in_=bias.rearrange("(p o) -> p o", o=1))
-        for span in range(4, len(SPANS)):
+        for span in range(FIRST + 1, len(SPANS)):
             load(span)
 
         one = keep.tile([P, 1], F32)
@@ -91,6 +103,23 @@ def tile_fp8_log_mel_d3_kernel(tc, P_bytes, P_scale, W, floor, gain, bias, out):
         make_identity(nc, ident_f32[:])
         ident_bf16 = keep.tile([P, P], BF16)
         make_identity(nc, ident_bf16[:])
+
+        repeats = P // (PACK * VECTOR_RUN)
+        scale_rows = keep.tile([P, repeats, PACK, VECTOR_RUN], F32)
+        scale_cols = keep.tile([P, P], F32)
+        scale_turned = psum_moved.tile([P, P], F32, name="moved")
+        scale_bank = psum_scale.tile([P, repeats, PACK, VECTOR_RUN], F32, name="scale_bank")
+
+        def turn_scale():
+            nc.vector.tensor_copy(
+                out=scale_rows[:],
+                in_=row_scale[:, 0, :].unsqueeze(1).unsqueeze(3).to_broadcast([P, repeats, PACK, VECTOR_RUN]),
+            )
+            nc.tensor.transpose(scale_turned[:], scale_rows[:].rearrange("p r t i -> p (r t i)"), ident_f32[:])
+
+        def turn_scale_back():
+            nc.scalar.copy(out=scale_cols[:], in_=scale_turned[:])
+            nc.tensor.transpose(scale_bank[:].rearrange("p r t i -> p (r t i)"), scale_cols[:], ident_f32[:])
 
         w_codes = keep.tile([P, PASSES * N], U32, align_bytes=64)
         w_scales = keep.tile([P, PASSES * N], U8, align_bytes=64)
@@ -104,145 +133,125 @@ def tile_fp8_log_mel_d3_kernel(tc, P_bytes, P_scale, W, floor, gain, bias, out):
             for g in range(PASSES):
                 for h in range(2):
                     nc.tensor.transpose(turned[:, g, h, :], pairs[:, per_pass * g + h : per_pass * (g + 1) : 2], ident_f32[:])
-            there[1] = turned
-
-        def fetch_w():
             nc.scalar.copy(
                 out=w_grouped[:].bitcast(F32).rearrange("p (g m h) -> p g m h", g=PASSES, h=2),
-                in_=there[1][:].rearrange("p g h m -> p g m h"),
+                in_=turned[:].rearrange("p g h m -> p g m h"),
             )
-
-        def quantize_w():
-            nc.vector.quantize_mx(out=w_codes[:].bitcast(FP8X4), scales=w_scales[:], in_=w_grouped[:])
-
-        scale_rows = keep.tile([P, P // (PACK * RUN), PACK, RUN], F32)
-        scale_cols = keep.tile([P, P], F32)
-        scale_bank = psum_scale.tile([P, P // (PACK * RUN), PACK, RUN], F32, name="scale_bank")
-        there = {}
-
-        def spread_scale():
-            nc.vector.tensor_copy(
-                out=scale_rows[:],
-                in_=row_scale[:, 0, :].unsqueeze(1).unsqueeze(3).to_broadcast([P, P // (PACK * RUN), PACK, RUN]),
-            )
-            there[0] = psum_moved.tile([P, P], F32, name="moved")
-            nc.tensor.transpose(there[0][:], scale_rows[:].rearrange("p r t i -> p (r t i)"), ident_f32[:])
-
-        def return_scale():
-            nc.scalar.copy(out=scale_cols[:], in_=there[0][:])
-            nc.tensor.transpose(scale_bank[:].rearrange("p r t i -> p (r t i)"), scale_cols[:], ident_f32[:])
 
         wide, grouped, moved, codes, scales, mel, logs = {}, {}, {}, {}, {}, {}, {}
 
         def wide_tile(span, g):
             if (span, g) not in wide:
-                wide[span, g] = work.tile([P, PACK, SPANS[span]], BF16, name="wide" if span > 1 else "wide_%d_%d" % (span, g), bufs=5 if span > 1 else 1)
+                wide[span, g] = work.tile([P, PACK, SPANS[span]], BF16, name="wide", bufs=5)
             return wide[span, g]
 
         def widen_on_scalar(span, g, planes):
             for t in planes:
                 nc.scalar.activation(
-                    out=wide_tile(span, g)[:, t, :], in_=raw[span, g][:, t, :].bitcast(FP8), func=ACT.Copy,
+                    out=wide_tile(span, g)[:, t, :],
+                    in_=raw[span, g][:, t, :].bitcast(FP8),
+                    func=ACT.Copy,
                     scale=row_scale[:, g, t : t + 1],
                 )
 
         def widen_on_vector(span, g, planes):
             for t in planes:
                 nc.vector.tensor_scalar(
-                    out=wide_tile(span, g)[:, t, :], in0=raw[span, g][:, t, :].bitcast(FP8),
-                    scalar1=row_scale[:, g, t : t + 1], scalar2=None, op0=ALU.mult,
+                    out=wide_tile(span, g)[:, t, :],
+                    in0=raw[span, g][:, t, :].bitcast(FP8),
+                    scalar1=row_scale[:, g, t : t + 1],
+                    scalar2=None,
+                    op0=ALU.mult,
                 )
 
-        def cast(span, g, first):
+        def cast_first_pass(c):
             nc.scalar.copy(
-                out=wide_tile(span, g)[:, first:, :].rearrange("p t n -> p (t n)"),
-                in_=raw[span, g][:, first:, :].rearrange("p t n -> p (t n)").bitcast(FP8),
+                out=wide_tile(c, 0)[:].rearrange("p t n -> p (t n)"),
+                in_=raw[c, 0][:].rearrange("p t n -> p (t n)").bitcast(FP8),
             )
-
-        def scale_planes(span, g, first):
-            for t in range(first, PACK):
-                plane = wide[span, g][:, t, :]
-                nc.vector.tensor_scalar(out=plane, in0=plane, scalar1=row_scale[:, g, t : t + 1], scalar2=None, op0=ALU.mult)
 
         def grouped_tile(c, g):
             if (c, g) not in grouped:
-                grouped[c, g] = work.tile([P, CHUNKS[c], PACK], BF16, name="grouped" if c < 10 else "grouped_%d_%d" % (c, g), align_bytes=64, bufs=4 if c < 10 else 1)
+                if c <= LAST:
+                    grouped[c, g] = work.tile([P, CHUNKS[c], PACK], BF16, name="grouped", align_bytes=64)
+                else:
+                    grouped[c, g] = keep.tile([P, CHUNKS[c], PACK], BF16, name="grouped_%d_%d" % (c, g), align_bytes=64)
             return grouped[c, g]
 
         def planes_of(c, g, n0, n1):
-            span, first = span_of(c)
+            span = min(c, TAIL_SPAN)
+            first = chunk_start[c] - chunk_start[span]
             return wide[span, g][:, :, first + n0 : first + n1]
 
-        def interleave_on_vector(c, g, n0, n1):
-            nc.vector.tensor_copy(
-                out=grouped_tile(c, g)[:, n0:n1, :].rearrange("p (r i) t -> p r t i", i=RUN),
-                in_=planes_of(c, g, n0, n1).rearrange("p t (r i) -> p r t i", i=RUN),
+        def in_runs(c, g, n0, n1, run):
+            return (
+                grouped_tile(c, g)[:, n0:n1, :].rearrange("p (r i) t -> p r t i", i=run),
+                planes_of(c, g, n0, n1).rearrange("p t (r i) -> p r t i", i=run),
             )
+
+        def interleave_on_vector(c, g, n0, n1):
+            target, source = in_runs(c, g, n0, n1, VECTOR_RUN)
+            nc.vector.tensor_copy(out=target, in_=source)
 
         def scale_and_interleave(c):
-            frames = CHUNKS[c]
-            nc.vector.tensor_tensor(
-                out=grouped_tile(c, 0)[:].rearrange("p (r i) t -> p r t i", i=RUN),
-                in0=planes_of(c, 0, 0, frames).rearrange("p t (r i) -> p r t i", i=RUN),
-                in1=scale_bank[:, 0:1, :, :].to_broadcast([P, frames // RUN, PACK, RUN]),
-                op=ALU.mult,
-            )
+            target, source = in_runs(c, 0, 0, FULL, VECTOR_RUN)
+            factor = scale_bank[:, 0:1, :, :].to_broadcast([P, FULL // VECTOR_RUN, PACK, VECTOR_RUN])
+            nc.vector.tensor_tensor(out=target, in0=source, in1=factor, op=ALU.mult)
 
-        def interleave_on_pool(c, g, n0, n1):
-            nc.gpsimd.tensor_scalar(
-                out=grouped_tile(c, g)[:, n0:n1, :].rearrange("p (r i) t -> p r t i", i=POOL_RUN),
-                in0=planes_of(c, g, n0, n1).rearrange("p t (r i) -> p r t i", i=POOL_RUN),
-                scalar1=1.0, scalar2=0.0, op0=ALU.mult, op1=ALU.add,
-            )
+        def interleave_on_pool(c):
+            target, source = in_runs(c, 1, 0, pool_frames(c), POOL_RUN)
+            nc.gpsimd.tensor_scalar(out=target, in0=source, scalar1=1.0, scalar2=0.0, op0=ALU.mult, op1=ALU.add)
 
-        def interleave_on_scalar(c, g):
-            nc.scalar.copy(
-                out=grouped_tile(c, g)[:].rearrange("p (r i) t -> p r t i", i=POOL_RUN),
-                in_=planes_of(c, g, 0, CHUNKS[c]).rearrange("p t (r i) -> p r t i", i=POOL_RUN),
-            )
-
-        def interleave_on_tensor(c, g, n0):
-            moved[c] = psum_moved.tile([P, TENSOR[c] * PACK], BF16, name="moved")
-            for k in range(0, TENSOR[c], BANK // PACK):
-                frames = min(BANK // PACK, TENSOR[c] - k)
+        def interleave_on_tensor(c, g):
+            frames = tensor_frames(c, g)
+            first = CHUNKS[c] - frames
+            moved[c, g] = psum_moved.tile([P, frames * PACK], BF16, name="moved")
+            for n0 in range(0, frames, BANK // PACK):
+                n1 = min(n0 + BANK // PACK, frames)
                 nc.tensor.matmul(
-                    out=moved[c][:, k * PACK : (k + frames) * PACK], lhsT=ident_bf16[:],
-                    rhs=planes_of(c, g, n0 + k, n0 + k + frames).rearrange("p t n -> p n t"), start=True, stop=True,
+                    out=moved[c, g][:, n0 * PACK : n1 * PACK],
+                    lhsT=ident_bf16[:],
+                    rhs=planes_of(c, g, first + n0, first + n1).rearrange("p t n -> p n t"),
+                    start=True,
+                    stop=True,
                 )
 
-        def fetch_from_tensor(c, g, n0):
+        def fetch_from_tensor(c, g):
             nc.scalar.copy(
-                out=grouped_tile(c, g)[:, n0 : n0 + TENSOR[c], :].rearrange("p n t -> p (n t)").bitcast(F32),
-                in_=moved[c][:].bitcast(F32),
+                out=grouped_tile(c, g)[:, CHUNKS[c] - tensor_frames(c, g) :, :].rearrange("p n t -> p (n t)").bitcast(F32),
+                in_=moved[c, g][:].bitcast(F32),
             )
 
         def quantize(c, g):
             codes[c, g] = work.tile([P, CHUNKS[c]], U32, name="codes", align_bytes=64, bufs=6)
             scales[c, g] = work.tile([P, CHUNKS[c]], U8, name="scales", align_bytes=64, bufs=6)
             nc.vector.quantize_mx(
-                out=codes[c, g][:].bitcast(FP8X4), scales=scales[c, g][:], in_=grouped[c, g][:].rearrange("p n t -> p (n t)")
+                out=codes[c, g][:].bitcast(FP8X4),
+                scales=scales[c, g][:],
+                in_=grouped[c, g][:].rearrange("p n t -> p (n t)"),
             )
 
         def banks(c):
             return [slice(n0, min(n0 + BANK, CHUNKS[c])) for n0 in range(0, CHUNKS[c], BANK)]
 
         def multiply(c):
-            mel[c] = []
-            for cols in banks(c):
-                acc = psum_mel.tile([P, cols.stop - cols.start], F32, name="mel")
-                mel[c].append(acc)
+            mel[c] = [psum_mel.tile([P, cols.stop - cols.start], F32, name="mel") for cols in banks(c)]
             for g in range(PASSES):
                 for acc, cols in zip(mel[c], banks(c)):
                     nc.tensor.matmul_mx(
-                        out=acc[:], lhsT=w_codes[:, g * N : (g + 1) * N].bitcast(FP8X4),
-                        lhsT_scale=w_scales[:, g * N : (g + 1) * N], rhs=codes[c, g][:, cols].bitcast(FP8X4),
-                        rhs_scale=scales[c, g][:, cols], start=(g == 0), stop=(g == PASSES - 1),
+                        out=acc[:],
+                        lhsT=w_codes[:, g * N : (g + 1) * N].bitcast(FP8X4),
+                        lhsT_scale=w_scales[:, g * N : (g + 1) * N],
+                        rhs=codes[c, g][:, cols].bitcast(FP8X4),
+                        rhs_scale=scales[c, g][:, cols],
+                        start=(g == 0),
+                        stop=(g == PASSES - 1),
                     )
 
-        head_logs = keep.tile([P, FULL], F32)
+        head_logs = keep.tile([P, sum(HEAD)], F32)
 
         def logarithm(c):
-            if c < FIRST_FULL:
+            if c < FIRST:
                 logs[c] = head_logs[:, chunk_start[c] : chunk_start[c] + CHUNKS[c]]
             else:
                 tile = keep.tile([P, CHUNKS[c]], F32, name="logs_%d" % c)
@@ -253,8 +262,10 @@ def tile_fp8_log_mel_d3_kernel(tc, P_bytes, P_scale, W, floor, gain, bias, out):
         def store(values, start):
             nc.sync.dma_start(out=out[:, start : start + values.shape[1]], in_=values)
 
-        def finish(engine, values, start):
-            engine.tensor_scalar(out=values, in0=values, scalar1=gain_col[:], scalar2=bias_col[:], op0=ALU.mult, op1=ALU.add)
+        def finish_on_vector(values, start):
+            nc.vector.tensor_scalar(
+                out=values, in0=values, scalar1=gain_col[:], scalar2=bias_col[:], op0=ALU.mult, op1=ALU.add
+            )
             store(values, start)
 
         def finish_on_scalar(c):
@@ -264,102 +275,101 @@ def tile_fp8_log_mel_d3_kernel(tc, P_bytes, P_scale, W, floor, gain, bias, out):
                 )
                 store(logs[c][:, cols], chunk_start[c] + cols.start)
 
-        def finish_chunk(engine, c):
-            if c < FIRST_FULL:
-                finish(engine, head_logs[:], 0)
-            else:
-                finish(engine, logs[c], chunk_start[c])
+        head_units = [(c, g) for c in range(FIRST) for g in range(PASSES)]
 
-        def prepare_first(c):
-            span = span_of(c)[0]
-            cast(span, 0, 0)
-            widen_on_scalar(span, 1, range(PACK - VPL[c] - 1))
-            if c == first:
-                turn_w()
-                fetch_w()
+        def widen_head(c, g):
+            widen_on_scalar(c, g, scalar_planes(c))
+            widen_on_vector(c, g, vector_planes(c))
 
-        def prepare_last(c):
-            widen_on_scalar(span_of(c)[0], 1, [PACK - VPL[c] - 1])
-
-        first, last = FUSED[0], FUSED[-1]
-        last_span = len(SPANS) - 1
-        head_units = [(c, g) for c in range(first) for g in range(PASSES)]
-
-        def widen_head(unit):
-            widen_on_scalar(*unit, range(PACK - HEADV[unit]))
-            widen_on_vector(*unit, range(PACK - HEADV[unit], PACK))
-
-        widen_head(head_units[0])
-        widen_head(head_units[1])
-        for s, unit in enumerate(head_units):
-            interleave_on_vector(*unit, 0, CHUNKS[unit[0]])
-            if s == 0:
-                spread_scale()
+        widen_head(*head_units[0])
+        turn_scale()
+        widen_head(*head_units[1])
+        for s, (c, g) in enumerate(head_units):
+            interleave_on_vector(c, g, 0, CHUNKS[c])
             if s + 2 < len(head_units):
-                widen_head(head_units[s + 2])
+                widen_head(*head_units[s + 2])
             if s == 1:
-                return_scale()
-            if s == len(head_units) - 2:
-                prepare_first(first)
-                prepare_last(first)
+                turn_scale_back()
+            if s + 2 == len(head_units):
+                cast_first_pass(FIRST)
+                widen_on_scalar(FIRST, 1, scalar_planes(FIRST)[:-1])
+                turn_w()
+                widen_on_scalar(FIRST, 1, scalar_planes(FIRST)[-1:])
             if s >= 1:
                 quantize(*head_units[s - 1])
 
-        for c in FUSED:
-            span = span_of(c)[0]
-            pool_end = POOL[c]
-            tensor_end = pool_end + TENSOR[c]
-            widen_on_vector(span, 1, range(PACK - VPL[c], PACK))
-            if c == first:
-                quantize_w()
-                for done in range(first - 1):
+        early_units = [(c, 0) for c in range(LAST + 1, len(CHUNKS))]
+        late_units = [(c, 1) for c in range(len(CHUNKS) - LATE_CHUNKS, len(CHUNKS))]
+
+        def fetch_early(k):
+            fetch_from_tensor(*early_units[k])
+            if k + 2 < len(early_units):
+                interleave_on_tensor(*early_units[k + 2])
+
+        for c in range(FIRST, LAST + 1):
+            widen_on_vector(c, 1, vector_planes(c))
+            if c == FIRST:
+                nc.vector.quantize_mx(out=w_codes[:].bitcast(FP8X4), scales=w_scales[:], in_=w_grouped[:])
+                for done in range(FIRST - 1):
                     multiply(done)
-            if TENSOR[c]:
-                interleave_on_tensor(c, 1, pool_end)
-            interleave_on_pool(c, 1, 0, pool_end)
+            interleave_on_tensor(c, 1)
+            interleave_on_pool(c)
             quantize(c - 1, 1)
             multiply(c - 1)
             scale_and_interleave(c)
-            if c in POOL_FIN:
-                finish_chunk(nc.gpsimd, POOL_FIN[c])
-            if c < last:
-                prepare_first(c + 1)
+
+            if c < LAST:
+                cast_first_pass(c + 1)
+                widen_on_scalar(c + 1, 1, scalar_planes(c + 1))
+                fetch_from_tensor(c, 1)
             else:
-                widen_on_scalar(last_span, 0, range(PACK - TAILV[0]))
-            if TENSOR[c]:
-                fetch_from_tensor(c, 1, pool_end)
-            if c < last:
-                prepare_last(c + 1)
-            else:
-                widen_on_scalar(last_span, 1, range(PACK - TAILV[1]))
-            if c == last:
+                widen_on_scalar(TAIL_SPAN, 0, range(PACK))
+                fetch_from_tensor(c, 1)
+                interleave_on_tensor(*early_units[0])
+                interleave_on_tensor(*early_units[1])
+                widen_on_scalar(TAIL_SPAN, 1, range(PACK))
+                fetch_early(0)
+                fetch_early(1)
                 nc.scalar.copy(out=gain_f32[:], in_=gain_col[:])
-            for done in range(c) if c == first else [c - 1]:
+            for done in range(c) if c == FIRST else [c - 1]:
                 logarithm(done)
-            if tensor_end < CHUNKS[c]:
-                interleave_on_vector(c, 1, tensor_end, CHUNKS[c])
+            if c == LAST:
+                for k in range(2, len(early_units)):
+                    fetch_early(k)
+
+            ready = c - FINISH_LAG
+            if c == FIRST:
+                interleave_on_vector(c, 1, FIRST_POOL_FRAMES, POOL_FRAMES)
+            elif ready < FIRST:
+                finish_on_vector(head_logs[:], 0)
+            else:
+                finish_on_vector(logs[ready], chunk_start[ready])
             quantize(c, 0)
 
-        widen_on_vector(last_span, 0, range(PACK - TAILV[0], PACK))
-        quantize(last, 1)
-        multiply(last)
-        widen_on_vector(last_span, 1, range(PACK - TAILV[1], PACK))
-        for c in range(FIRST_FULL, last):
-            if c not in POOL_FIN.values():
-                finish_on_scalar(c)
-        logarithm(last)
-        if last < AFTER_FULL:
-            finish_on_scalar(last)
-        for unit in SCALAR_UNITS:
-            interleave_on_scalar(*unit)
-        tail_units = [(c, g) for c in range(last + 1, len(CHUNKS)) for g in range(PASSES)]
-        interleave_on_vector(*tail_units[0], 0, CHUNKS[last + 1])
-        for before, unit in zip(tail_units, tail_units[1:] + [None]):
-            if unit is not None and unit not in SCALAR_UNITS:
-                interleave_on_vector(*unit, 0, CHUNKS[unit[0]])
-            quantize(*before)
-            if before[1] == PASSES - 1:
-                multiply(before[0])
-                logarithm(before[0])
-        for c in range(AFTER_FULL, len(CHUNKS)):
-            finish(nc.vector, logs[c], chunk_start[c])
+        quantize(LAST, 1)
+        multiply(LAST)
+        for unit in late_units:
+            interleave_on_tensor(*unit)
+        for c in range(LAST + 1 - FINISH_LAG, LAST):
+            finish_on_scalar(c)
+        logarithm(LAST)
+        for unit in late_units:
+            fetch_from_tensor(*unit)
+        finish_on_scalar(LAST)
+
+        def interleave_rest(c, g):
+            frames = CHUNKS[c] - (tensor_frames(c, g) if (c, g) in early_units + late_units else 0)
+            if frames:
+                interleave_on_vector(c, g, 0, frames)
+
+        tail_units = [(c, g) for c in range(LAST + 1, len(CHUNKS)) for g in range(PASSES)]
+        interleave_rest(*tail_units[0])
+        for s, (c, g) in enumerate(tail_units):
+            if s + 1 < len(tail_units):
+                interleave_rest(*tail_units[s + 1])
+            quantize(c, g)
+            if g == PASSES - 1:
+                multiply(c)
+                logarithm(c)
+        for c in range(LAST + 1, len(CHUNKS)):
+            finish_on_vector(logs[c], chunk_start[c])

@@ -24,37 +24,46 @@ FULL = 1024
 VECTOR_RUN = 2
 POOL_RUN = 4
 
-HEAD = [256, 256, 512]
+HEAD = [256, 256]
+RAMP = 512
 TAIL = [512, 256, 128, 128]
-CHUNKS = HEAD + [FULL] * ((T - sum(HEAD) - sum(TAIL)) // FULL) + TAIL
+CHUNKS = HEAD + [RAMP] + [FULL] * ((T - sum(HEAD) - RAMP - sum(TAIL)) // FULL) + TAIL
 FIRST = len(HEAD)
+FIRST_FULL = FIRST + 1
 LAST = len(CHUNKS) - len(TAIL) - 1
 SPANS = CHUNKS[: LAST + 1] + [sum(TAIL)]
 TAIL_SPAN = LAST + 1
 assert sum(CHUNKS) == T and sum(SPANS) == T
 
-TENSOR_FRAMES = 96
-POOL_FRAMES = FULL - TENSOR_FRAMES
-FIRST_POOL_FRAMES = POOL_FRAMES - TENSOR_FRAMES
+TENSOR_FRAMES = 100
+EARLY_VECTOR_FRAMES = 128
 LATE_CHUNKS = 2
 HEAD_PLANES = 2
+VECTOR_COLUMNS = 896
 FINISH_LAG = 2
 
 
-def vector_planes(c):
-    return range(PACK - (HEAD_PLANES if c <= FIRST else 1), PACK)
+def vector_share(span):
+    if span <= FIRST_FULL:
+        return [(t, slice(0, SPANS[span])) for t in range(PACK - HEAD_PLANES, PACK)]
+    return [(PACK - 1, slice(0, VECTOR_COLUMNS if span <= LAST else SPANS[span]))]
 
 
-def scalar_planes(c):
-    return range(vector_planes(c).start)
+def scalar_share(span):
+    if span <= FIRST_FULL:
+        return [(t, slice(0, SPANS[span])) for t in range(PACK - HEAD_PLANES)]
+    rest = [(PACK - 1, slice(VECTOR_COLUMNS, FULL))] if span <= LAST else []
+    return [(t, slice(0, SPANS[span])) for t in range(PACK - 1)] + rest
+
+
+def tensor_frames(c):
+    if c <= LAST:
+        return TENSOR_FRAMES if c >= FIRST_FULL else 0
+    return min(CHUNKS[c], BANK_FRAMES)
 
 
 def pool_frames(c):
-    return FIRST_POOL_FRAMES if c == FIRST else POOL_FRAMES
-
-
-def tensor_frames(c, g):
-    return TENSOR_FRAMES if c <= LAST else min(CHUNKS[c], BANK_FRAMES)
+    return CHUNKS[c] - tensor_frames(c) - (EARLY_VECTOR_FRAMES if c <= FIRST_FULL else 0)
 
 
 def tile_fp8_log_mel_d3_kernel(tc, P_bytes, P_scale, W, floor, gain, bias, out):
@@ -81,7 +90,7 @@ def tile_fp8_log_mel_d3_kernel(tc, P_bytes, P_scale, W, floor, gain, bias, out):
         scale_tile = keep.tile([P, PASSES, 2 * PACK], F32)
         row_scale = scale_tile[:, :, :PACK]
         nc.scalar.dma_start(out=row_scale, in_=P_scale.rearrange("(g p t) o -> p g (t o)", p=P, t=PACK))
-        for span in range(FIRST + 1):
+        for span in range(FIRST_FULL + 1):
             load(span)
         w_rows = keep.tile([P, F], BF16, align_bytes=64)
         nc.sync.dma_start(out=w_rows[:], in_=W)
@@ -91,7 +100,7 @@ def tile_fp8_log_mel_d3_kernel(tc, P_bytes, P_scale, W, floor, gain, bias, out):
         nc.sync.dma_start(out=floor_col[:], in_=floor.rearrange("(p o) -> p o", o=1))
         nc.sync.dma_start(out=gain_col[:], in_=gain.rearrange("(p o) -> p o", o=1))
         nc.sync.dma_start(out=bias_col[:], in_=bias.rearrange("(p o) -> p o", o=1))
-        for span in range(FIRST + 1, len(SPANS)):
+        for span in range(FIRST_FULL + 1, len(SPANS)):
             load(span)
 
         one = keep.tile([P, 1], F32)
@@ -145,20 +154,20 @@ def tile_fp8_log_mel_d3_kernel(tc, P_bytes, P_scale, W, floor, gain, bias, out):
                 wide[span, g] = work.tile([P, PACK, SPANS[span]], BF16, name="wide", bufs=5)
             return wide[span, g]
 
-        def widen_on_scalar(span, g, planes):
-            for t in planes:
+        def widen_on_scalar(span, g, share):
+            for t, frames in share:
                 nc.scalar.activation(
-                    out=wide_tile(span, g)[:, t, :],
-                    in_=raw[span, g][:, t, :].bitcast(FP8),
+                    out=wide_tile(span, g)[:, t, frames],
+                    in_=raw[span, g][:, t, frames].bitcast(FP8),
                     func=ACT.Copy,
                     scale=row_scale[:, g, t : t + 1],
                 )
 
-        def widen_on_vector(span, g, planes):
-            for t in planes:
+        def widen_on_vector(span, g, share):
+            for t, frames in share:
                 nc.vector.tensor_scalar(
-                    out=wide_tile(span, g)[:, t, :],
-                    in0=raw[span, g][:, t, :].bitcast(FP8),
+                    out=wide_tile(span, g)[:, t, frames],
+                    in0=raw[span, g][:, t, frames].bitcast(FP8),
                     scalar1=row_scale[:, g, t : t + 1],
                     scalar2=None,
                     op0=ALU.mult,
@@ -194,8 +203,8 @@ def tile_fp8_log_mel_d3_kernel(tc, P_bytes, P_scale, W, floor, gain, bias, out):
             nc.vector.tensor_copy(out=target, in_=source)
 
         def scale_and_interleave(c):
-            target, source = in_runs(c, 0, 0, FULL, VECTOR_RUN)
-            factor = scale_bank[:, 0:1, :, :].to_broadcast([P, FULL // VECTOR_RUN, PACK, VECTOR_RUN])
+            target, source = in_runs(c, 0, 0, CHUNKS[c], VECTOR_RUN)
+            factor = scale_bank[:, 0:1, :, :].to_broadcast([P, CHUNKS[c] // VECTOR_RUN, PACK, VECTOR_RUN])
             nc.vector.tensor_tensor(out=target, in0=source, in1=factor, op=ALU.mult)
 
         def interleave_on_pool(c):
@@ -203,7 +212,7 @@ def tile_fp8_log_mel_d3_kernel(tc, P_bytes, P_scale, W, floor, gain, bias, out):
             nc.gpsimd.tensor_scalar(out=target, in0=source, scalar1=1.0, scalar2=0.0, op0=ALU.mult, op1=ALU.add)
 
         def interleave_on_tensor(c, g):
-            frames = tensor_frames(c, g)
+            frames = tensor_frames(c)
             first = CHUNKS[c] - frames
             moved[c, g] = psum_moved.tile([P, frames * PACK], BF16, name="moved")
             for n0 in range(0, frames, BANK // PACK):
@@ -218,7 +227,7 @@ def tile_fp8_log_mel_d3_kernel(tc, P_bytes, P_scale, W, floor, gain, bias, out):
 
         def fetch_from_tensor(c, g):
             nc.scalar.copy(
-                out=grouped_tile(c, g)[:, CHUNKS[c] - tensor_frames(c, g) :, :].rearrange("p n t -> p (n t)").bitcast(F32),
+                out=grouped_tile(c, g)[:, CHUNKS[c] - tensor_frames(c) :, :].rearrange("p n t -> p (n t)").bitcast(F32),
                 in_=moved[c, g][:].bitcast(F32),
             )
 
@@ -248,10 +257,10 @@ def tile_fp8_log_mel_d3_kernel(tc, P_bytes, P_scale, W, floor, gain, bias, out):
                         stop=(g == PASSES - 1),
                     )
 
-        head_logs = keep.tile([P, sum(HEAD)], F32)
+        head_logs = keep.tile([P, chunk_start[FIRST_FULL]], F32)
 
         def logarithm(c):
-            if c < FIRST:
+            if c < FIRST_FULL:
                 logs[c] = head_logs[:, chunk_start[c] : chunk_start[c] + CHUNKS[c]]
             else:
                 tile = keep.tile([P, CHUNKS[c]], F32, name="logs_%d" % c)
@@ -278,8 +287,15 @@ def tile_fp8_log_mel_d3_kernel(tc, P_bytes, P_scale, W, floor, gain, bias, out):
         head_units = [(c, g) for c in range(FIRST) for g in range(PASSES)]
 
         def widen_head(c, g):
-            widen_on_scalar(c, g, scalar_planes(c))
-            widen_on_vector(c, g, vector_planes(c))
+            widen_on_scalar(c, g, scalar_share(c))
+            widen_on_vector(c, g, vector_share(c))
+
+        def prepare(c):
+            cast_first_pass(c)
+            widen_on_scalar(c, 1, scalar_share(c)[:-1])
+            if c == FIRST_FULL:
+                turn_w()
+            widen_on_scalar(c, 1, scalar_share(c)[-1:])
 
         widen_head(*head_units[0])
         turn_scale()
@@ -291,10 +307,7 @@ def tile_fp8_log_mel_d3_kernel(tc, P_bytes, P_scale, W, floor, gain, bias, out):
             if s == 1:
                 turn_scale_back()
             if s + 2 == len(head_units):
-                cast_first_pass(FIRST)
-                widen_on_scalar(FIRST, 1, scalar_planes(FIRST)[:-1])
-                turn_w()
-                widen_on_scalar(FIRST, 1, scalar_planes(FIRST)[-1:])
+                prepare(FIRST)
             if s >= 1:
                 quantize(*head_units[s - 1])
 
@@ -307,46 +320,52 @@ def tile_fp8_log_mel_d3_kernel(tc, P_bytes, P_scale, W, floor, gain, bias, out):
                 interleave_on_tensor(*early_units[k + 2])
 
         for c in range(FIRST, LAST + 1):
-            widen_on_vector(c, 1, vector_planes(c))
-            if c == FIRST:
+            widen_on_vector(c, 1, vector_share(c))
+            if c == FIRST_FULL:
                 nc.vector.quantize_mx(out=w_codes[:].bitcast(FP8X4), scales=w_scales[:], in_=w_grouped[:])
-                for done in range(FIRST - 1):
+                for done in range(FIRST):
                     multiply(done)
-            interleave_on_tensor(c, 1)
+            if c >= FIRST_FULL:
+                interleave_on_tensor(c, 1)
             interleave_on_pool(c)
             quantize(c - 1, 1)
-            multiply(c - 1)
+            if c >= FIRST_FULL:
+                multiply(c - 1)
             scale_and_interleave(c)
 
             if c < LAST:
-                cast_first_pass(c + 1)
-                widen_on_scalar(c + 1, 1, scalar_planes(c + 1))
-                fetch_from_tensor(c, 1)
+                prepare(c + 1)
             else:
-                widen_on_scalar(TAIL_SPAN, 0, range(PACK))
+                widen_on_scalar(TAIL_SPAN, 0, [(t, slice(0, SPANS[TAIL_SPAN])) for t in range(PACK)])
+            if c >= FIRST_FULL:
                 fetch_from_tensor(c, 1)
+            if c == LAST:
                 interleave_on_tensor(*early_units[0])
                 interleave_on_tensor(*early_units[1])
-                widen_on_scalar(TAIL_SPAN, 1, range(PACK))
+                widen_on_scalar(TAIL_SPAN, 1, scalar_share(TAIL_SPAN))
                 fetch_early(0)
                 fetch_early(1)
                 nc.scalar.copy(out=gain_f32[:], in_=gain_col[:])
-            for done in range(c) if c == FIRST else [c - 1]:
-                logarithm(done)
+            if c == FIRST_FULL:
+                for done in range(FIRST):
+                    logarithm(done)
+            if c >= FIRST_FULL:
+                logarithm(c - 1)
             if c == LAST:
                 for k in range(2, len(early_units)):
                     fetch_early(k)
 
             ready = c - FINISH_LAG
-            if c == FIRST:
-                interleave_on_vector(c, 1, FIRST_POOL_FRAMES, POOL_FRAMES)
-            elif ready < FIRST:
+            if c <= FIRST_FULL:
+                interleave_on_vector(c, 1, pool_frames(c), pool_frames(c) + EARLY_VECTOR_FRAMES)
+            elif ready < FIRST_FULL:
                 finish_on_vector(head_logs[:], 0)
             else:
                 finish_on_vector(logs[ready], chunk_start[ready])
             quantize(c, 0)
 
         quantize(LAST, 1)
+        widen_on_vector(TAIL_SPAN, 1, vector_share(TAIL_SPAN))
         multiply(LAST)
         for unit in late_units:
             interleave_on_tensor(*unit)
@@ -358,7 +377,7 @@ def tile_fp8_log_mel_d3_kernel(tc, P_bytes, P_scale, W, floor, gain, bias, out):
         finish_on_scalar(LAST)
 
         def interleave_rest(c, g):
-            frames = CHUNKS[c] - (tensor_frames(c, g) if (c, g) in early_units + late_units else 0)
+            frames = CHUNKS[c] - (tensor_frames(c) if (c, g) in early_units + late_units else 0)
             if frames:
                 interleave_on_vector(c, g, 0, frames)
 

@@ -36,34 +36,32 @@ TAIL_SPAN = LAST + 1
 assert sum(CHUNKS) == T and sum(SPANS) == T
 
 TENSOR_FRAMES = 100
-EARLY_VECTOR_FRAMES = 128
+POOL_FRAMES = FULL - TENSOR_FRAMES
+RAMP_POOL_FRAMES = 384
 LATE_CHUNKS = 2
 HEAD_PLANES = 2
-VECTOR_COLUMNS = 896
 FINISH_LAG = 2
 
 
 def vector_share(span):
     if span <= FIRST_FULL:
         return [(t, slice(0, SPANS[span])) for t in range(PACK - HEAD_PLANES, PACK)]
-    return [(PACK - 1, slice(0, VECTOR_COLUMNS if span <= LAST else SPANS[span]))]
+    return [(PACK - 1, slice(0, POOL_FRAMES if span <= LAST else SPANS[span]))]
 
 
 def scalar_share(span):
     if span <= FIRST_FULL:
         return [(t, slice(0, SPANS[span])) for t in range(PACK - HEAD_PLANES)]
-    rest = [(PACK - 1, slice(VECTOR_COLUMNS, FULL))] if span <= LAST else []
+    rest = [(PACK - 1, slice(POOL_FRAMES, FULL))] if span <= LAST else []
     return [(t, slice(0, SPANS[span])) for t in range(PACK - 1)] + rest
 
 
 def tensor_frames(c):
-    if c <= LAST:
-        return TENSOR_FRAMES if c >= FIRST_FULL else 0
-    return min(CHUNKS[c], BANK_FRAMES)
+    return TENSOR_FRAMES if c <= LAST else min(CHUNKS[c], BANK_FRAMES)
 
 
 def pool_frames(c):
-    return CHUNKS[c] - tensor_frames(c) - (EARLY_VECTOR_FRAMES if c <= FIRST_FULL else 0)
+    return RAMP_POOL_FRAMES if c == FIRST else POOL_FRAMES
 
 
 def tile_fp8_log_mel_d3_kernel(tc, P_bytes, P_scale, W, floor, gain, bias, out):
@@ -204,7 +202,7 @@ def tile_fp8_log_mel_d3_kernel(tc, P_bytes, P_scale, W, floor, gain, bias, out):
 
         def scale_and_interleave(c):
             target, source = in_runs(c, 0, 0, CHUNKS[c], VECTOR_RUN)
-            factor = scale_bank[:, 0:1, :, :].to_broadcast([P, CHUNKS[c] // VECTOR_RUN, PACK, VECTOR_RUN])
+            factor = scale_bank[:].rearrange("p r t i -> p (r t i)").unsqueeze(1).to_broadcast([P, CHUNKS[c] * PACK // P, P])
             nc.vector.tensor_tensor(out=target, in0=source, in1=factor, op=ALU.mult)
 
         def interleave_on_pool(c):
@@ -232,8 +230,8 @@ def tile_fp8_log_mel_d3_kernel(tc, P_bytes, P_scale, W, floor, gain, bias, out):
             )
 
         def quantize(c, g):
-            codes[c, g] = work.tile([P, CHUNKS[c]], U32, name="codes", align_bytes=64, bufs=6)
-            scales[c, g] = work.tile([P, CHUNKS[c]], U8, name="scales", align_bytes=64, bufs=6)
+            codes[c, g] = work.tile([P, CHUNKS[c]], U32, name="codes", align_bytes=64, bufs=7)
+            scales[c, g] = work.tile([P, CHUNKS[c]], U8, name="scales", align_bytes=64, bufs=7)
             nc.vector.quantize_mx(
                 out=codes[c, g][:].bitcast(FP8X4),
                 scales=scales[c, g][:],
@@ -292,10 +290,12 @@ def tile_fp8_log_mel_d3_kernel(tc, P_bytes, P_scale, W, floor, gain, bias, out):
 
         def prepare(c):
             cast_first_pass(c)
-            widen_on_scalar(c, 1, scalar_share(c)[:-1])
-            if c == FIRST_FULL:
+            if c == FIRST_FULL + 1:
                 turn_w()
-            widen_on_scalar(c, 1, scalar_share(c)[-1:])
+            if c == FIRST_FULL + 2:
+                for done in range(FIRST_FULL):
+                    logarithm(done)
+            widen_on_scalar(c, 1, scalar_share(c))
 
         widen_head(*head_units[0])
         turn_scale()
@@ -321,15 +321,11 @@ def tile_fp8_log_mel_d3_kernel(tc, P_bytes, P_scale, W, floor, gain, bias, out):
 
         for c in range(FIRST, LAST + 1):
             widen_on_vector(c, 1, vector_share(c))
-            if c == FIRST_FULL:
-                nc.vector.quantize_mx(out=w_codes[:].bitcast(FP8X4), scales=w_scales[:], in_=w_grouped[:])
-                for done in range(FIRST):
-                    multiply(done)
             if c >= FIRST_FULL:
                 interleave_on_tensor(c, 1)
             interleave_on_pool(c)
             quantize(c - 1, 1)
-            if c >= FIRST_FULL:
+            if c > FIRST_FULL:
                 multiply(c - 1)
             scale_and_interleave(c)
 
@@ -346,18 +342,19 @@ def tile_fp8_log_mel_d3_kernel(tc, P_bytes, P_scale, W, floor, gain, bias, out):
                 fetch_early(0)
                 fetch_early(1)
                 nc.scalar.copy(out=gain_f32[:], in_=gain_col[:])
-            if c == FIRST_FULL:
-                for done in range(FIRST):
-                    logarithm(done)
-            if c >= FIRST_FULL:
+            if c > FIRST_FULL:
                 logarithm(c - 1)
             if c == LAST:
                 for k in range(2, len(early_units)):
                     fetch_early(k)
 
             ready = c - FINISH_LAG
-            if c <= FIRST_FULL:
-                interleave_on_vector(c, 1, pool_frames(c), pool_frames(c) + EARLY_VECTOR_FRAMES)
+            if c == FIRST:
+                interleave_on_vector(c, 1, pool_frames(c), CHUNKS[c])
+            elif c == FIRST_FULL:
+                nc.vector.quantize_mx(out=w_codes[:].bitcast(FP8X4), scales=w_scales[:], in_=w_grouped[:])
+                for done in range(FIRST_FULL):
+                    multiply(done)
             elif ready < FIRST_FULL:
                 finish_on_vector(head_logs[:], 0)
             else:

@@ -107,9 +107,9 @@ def tile_fp8_log_mel_d3_kernel(tc, P_bytes, P_scale, W, floor, gain, bias, out):
         nc.scalar.activation(out=warm[:], in_=one[:], func=ACT.Ln)
 
         ident_f32 = keep.tile([P, P], F32)
-        make_identity(nc, ident_f32[:])
+        nc.vector.memset(ident_f32[:], 0.0)
+        make_identity(nc, ident_f32[:], nomemset=True)
         ident_bf16 = keep.tile([P, P], BF16)
-        make_identity(nc, ident_bf16[:])
 
         repeats = P // (PACK * VECTOR_RUN)
         scale_rows = keep.tile([P, repeats, PACK, VECTOR_RUN], F32)
@@ -299,6 +299,7 @@ def tile_fp8_log_mel_d3_kernel(tc, P_bytes, P_scale, W, floor, gain, bias, out):
 
         widen_head(*head_units[0])
         turn_scale()
+        nc.vector.tensor_copy(out=ident_bf16[:], in_=ident_f32[:])
         widen_head(*head_units[1])
         for s, (c, g) in enumerate(head_units):
             interleave_on_vector(c, g, 0, CHUNKS[c])

@@ -22,7 +22,7 @@ BANK = 512
 BANK_FRAMES = 2 * BANK // PACK
 FULL = 1024
 VECTOR_RUN = 2
-POOL_RUN = 4
+POOL_RUN = 2
 
 HEAD = [256, 256]
 RAMP = 512
@@ -35,7 +35,7 @@ SPANS = CHUNKS[: LAST + 1] + [sum(TAIL)]
 TAIL_SPAN = LAST + 1
 assert sum(CHUNKS) == T and sum(SPANS) == T
 
-TENSOR_FRAMES = 100
+TENSOR_FRAMES = 40
 POOL_FRAMES = FULL - TENSOR_FRAMES
 RAMP_POOL_FRAMES = 384
 LATE_CHUNKS = 2

@@ -40,19 +40,20 @@ POOL_FRAMES = FULL - TENSOR_FRAMES
 RAMP_POOL_FRAMES = 384
 LATE_CHUNKS = 2
 HEAD_PLANES = 2
+VECTOR_FRAMES = 832
 FINISH_LAG = 2
 
 
 def vector_share(span):
     if span <= FIRST_FULL:
         return [(t, slice(0, SPANS[span])) for t in range(PACK - HEAD_PLANES, PACK)]
-    return [(PACK - 1, slice(0, POOL_FRAMES if span <= LAST else SPANS[span]))]
+    return [(PACK - 1, slice(0, VECTOR_FRAMES if span <= LAST else SPANS[span]))]
 
 
 def scalar_share(span):
     if span <= FIRST_FULL:
         return [(t, slice(0, SPANS[span])) for t in range(PACK - HEAD_PLANES)]
-    rest = [(PACK - 1, slice(POOL_FRAMES, FULL))] if span <= LAST else []
+    rest = [(PACK - 1, slice(VECTOR_FRAMES, FULL))] if span <= LAST else []
     return [(t, slice(0, SPANS[span])) for t in range(PACK - 1)] + rest
 
 

@@ -37,7 +37,7 @@ assert sum(CHUNKS) == T and sum(SPANS) == T
 
 TENSOR_FRAMES = 40
 POOL_FRAMES = FULL - TENSOR_FRAMES
-RAMP_POOL_FRAMES = 384
+RAMP_POOL_FRAMES = 448
 LATE_CHUNKS = 2
 HEAD_PLANES = 2
 VECTOR_FRAMES = 832
@@ -322,7 +322,7 @@ def tile_fp8_log_mel_d3_kernel(tc, P_bytes, P_scale, W, floor, gain, bias, out):
                 interleave_on_tensor(*early_units[k + 2])
 
         for c in range(FIRST, LAST + 1):
-            widen_on_vector(c, 1, vector_share(c))
+            widen_on_vector(c, 1, vector_share(c)[1:] if c == FIRST_FULL else vector_share(c))
             if c >= FIRST_FULL:
                 interleave_on_tensor(c, 1)
             interleave_on_pool(c)
@@ -352,6 +352,7 @@ def tile_fp8_log_mel_d3_kernel(tc, P_bytes, P_scale, W, floor, gain, bias, out):
 
             ready = c - FINISH_LAG
             if c == FIRST:
+                widen_on_vector(c + 1, 1, vector_share(c + 1)[:1])
                 interleave_on_vector(c, 1, pool_frames(c), CHUNKS[c])
             elif c == FIRST_FULL:
                 nc.vector.quantize_mx(out=w_codes[:].bitcast(FP8X4), scales=w_scales[:], in_=w_grouped[:])

@@ -24,7 +24,7 @@ FULL = 1024
 VECTOR_RUN = 2
 POOL_RUN = 2
 
-HEAD = [256, 256]
+HEAD = [512]
 RAMP = 512
 TAIL = [512, 256, 128, 128]
 CHUNKS = HEAD + [RAMP] + [FULL] * ((T - sum(HEAD) - RAMP - sum(TAIL)) // FULL) + TAIL
@@ -40,7 +40,9 @@ POOL_FRAMES = FULL - TENSOR_FRAMES
 RAMP_POOL_FRAMES = 448
 LATE_CHUNKS = 2
 HEAD_PLANES = 2
-VECTOR_FRAMES = 832
+HEAD_LOADS = [(0, 2, 4), (0, 0, 2), (1, 2, 4), (1, 0, 2)]
+HEAD_VECTOR = [[2, 3], [1], [2, 3]]
+VECTOR_FRAMES = 768
 FINISH_LAG = 2
 
 
@@ -80,11 +82,23 @@ def tile_fp8_log_mel_d3_kernel(tc, P_bytes, P_scale, W, floor, gain, bias, out):
         p_rows = P_bytes.rearrange("(g p t) n -> g p t n", p=P, t=PACK)
         raw = {}
 
-        def load(span):
+        plane = {}
+
+        def load_planes(span, g, t0, t1):
             start = chunk_start[span]
-            for g in range(PASSES):
-                raw[span, g] = keep.tile([P, PACK, SPANS[span]], U8, name="p_bytes_%d_%d" % (span, g))
-                nc.sync.dma_start(out=raw[span, g][:], in_=p_rows[g][:, :, start : start + SPANS[span]])
+            tile = keep.tile([P, t1 - t0, SPANS[span]], U8, name="p_bytes_%d_%d_%d" % (span, g, t0))
+            nc.sync.dma_start(out=tile[:], in_=p_rows[g][:, t0:t1, start : start + SPANS[span]])
+            for t in range(t0, t1):
+                plane[span, g, t] = tile[:, t - t0, :]
+            return tile
+
+        def load(span):
+            if span == 0:
+                for g, t0, t1 in HEAD_LOADS:
+                    load_planes(span, g, t0, t1)
+            else:
+                for g in range(PASSES):
+                    raw[span, g] = load_planes(span, g, 0, PACK)
 
         scale_tile = keep.tile([P, PASSES, 2 * PACK], F32)
         row_scale = scale_tile[:, :, :PACK]
@@ -157,7 +171,7 @@ def tile_fp8_log_mel_d3_kernel(tc, P_bytes, P_scale, W, floor, gain, bias, out):
             for t, frames in share:
                 nc.scalar.activation(
                     out=wide_tile(span, g)[:, t, frames],
-                    in_=raw[span, g][:, t, frames].bitcast(FP8),
+                    in_=plane[span, g, t][:, frames].bitcast(FP8),
                     func=ACT.Copy,
                     scale=row_scale[:, g, t : t + 1],
                 )
@@ -166,7 +180,7 @@ def tile_fp8_log_mel_d3_kernel(tc, P_bytes, P_scale, W, floor, gain, bias, out):
             for t, frames in share:
                 nc.vector.tensor_scalar(
                     out=wide_tile(span, g)[:, t, frames],
-                    in0=raw[span, g][:, t, frames].bitcast(FP8),
+                    in0=plane[span, g, t][:, frames].bitcast(FP8),
                     scalar1=row_scale[:, g, t : t + 1],
                     scalar2=None,
                     op0=ALU.mult,
@@ -283,12 +297,6 @@ def tile_fp8_log_mel_d3_kernel(tc, P_bytes, P_scale, W, floor, gain, bias, out):
                 )
                 store(logs[c][:, cols], chunk_start[c] + cols.start)
 
-        head_units = [(c, g) for c in range(FIRST) for g in range(PASSES)]
-
-        def widen_head(c, g):
-            widen_on_scalar(c, g, scalar_share(c))
-            widen_on_vector(c, g, vector_share(c))
-
         def prepare(c):
             cast_first_pass(c)
             if c == FIRST_FULL + 1:
@@ -298,20 +306,19 @@ def tile_fp8_log_mel_d3_kernel(tc, P_bytes, P_scale, W, floor, gain, bias, out):
                     logarithm(done)
             widen_on_scalar(c, 1, scalar_share(c))
 
-        widen_head(*head_units[0])
+        whole = slice(0, HEAD[0])
+        widen_on_vector(0, 0, [(t, whole) for t in HEAD_VECTOR[0]])
         turn_scale()
         nc.vector.tensor_copy(out=ident_bf16[:], in_=ident_f32[:])
-        widen_head(*head_units[1])
-        for s, (c, g) in enumerate(head_units):
-            interleave_on_vector(c, g, 0, CHUNKS[c])
-            if s + 2 < len(head_units):
-                widen_head(*head_units[s + 2])
-            if s == 1:
-                turn_scale_back()
-            if s + 2 == len(head_units):
-                prepare(FIRST)
-            if s >= 1:
-                quantize(*head_units[s - 1])
+        widen_on_vector(0, 0, [(t, whole) for t in HEAD_VECTOR[1]])
+        widen_on_vector(0, 1, [(t, whole) for t in HEAD_VECTOR[2]])
+        widen_on_scalar(0, 0, [(t, whole) for t in range(PACK) if t not in HEAD_VECTOR[0] + HEAD_VECTOR[1]])
+        widen_on_scalar(0, 1, [(t, whole) for t in range(PACK) if t not in HEAD_VECTOR[2]])
+        turn_scale_back()
+        prepare(FIRST)
+        interleave_on_vector(0, 0, 0, HEAD[0])
+        interleave_on_vector(0, 1, 0, HEAD[0])
+        quantize(0, 0)
 
         early_units = [(c, 0) for c in range(LAST + 1, len(CHUNKS))]
         late_units = [(c, 1) for c in range(len(CHUNKS) - LATE_CHUNKS, len(CHUNKS))]

@@ -40,19 +40,24 @@ POOL_FRAMES = FULL - TENSOR_FRAMES
 RAMP_POOL_FRAMES = 448
 LATE_CHUNKS = 2
 HEAD_PLANES = 2
-HEAD_LOADS = [(0, 2, 4), (0, 0, 2), (1, 2, 4), (1, 0, 2)]
-HEAD_VECTOR = [[2, 3], [1], [2, 3]]
+FIRST_PART = 256
+HEAD_LOADS = [(0, 0, 4, 0, FIRST_PART), (0, 0, 4, FIRST_PART, 512), (1, 0, 2, 0, 512), (1, 2, 4, 0, 512)]
+RAMP_PLANES = 2
 VECTOR_FRAMES = 768
 FINISH_LAG = 2
 
 
 def vector_share(span):
+    if span == FIRST:
+        return [(t, slice(0, SPANS[span])) for t in range(PACK - RAMP_PLANES, PACK)]
     if span <= FIRST_FULL:
         return [(t, slice(0, SPANS[span])) for t in range(PACK - HEAD_PLANES, PACK)]
     return [(PACK - 1, slice(0, VECTOR_FRAMES if span <= LAST else SPANS[span]))]
 
 
 def scalar_share(span):
+    if span == FIRST:
+        return [(t, slice(0, SPANS[span])) for t in range(PACK - RAMP_PLANES)]
     if span <= FIRST_FULL:
         return [(t, slice(0, SPANS[span])) for t in range(PACK - HEAD_PLANES)]
     rest = [(PACK - 1, slice(VECTOR_FRAMES, FULL))] if span <= LAST else []
@@ -84,21 +89,25 @@ def tile_fp8_log_mel_d3_kernel(tc, P_bytes, P_scale, W, floor, gain, bias, out):
 
         plane = {}
 
-        def load_planes(span, g, t0, t1):
+        def load_planes(span, g, t0, t1, n0, n1):
             start = chunk_start[span]
-            tile = keep.tile([P, t1 - t0, SPANS[span]], U8, name="p_bytes_%d_%d_%d" % (span, g, t0))
-            nc.sync.dma_start(out=tile[:], in_=p_rows[g][:, t0:t1, start : start + SPANS[span]])
+            tile = keep.tile([P, t1 - t0, n1 - n0], U8, name="p_bytes_%d_%d_%d_%d" % (span, g, t0, n0))
+            nc.sync.dma_start(out=tile[:], in_=p_rows[g][:, t0:t1, start + n0 : start + n1])
             for t in range(t0, t1):
-                plane[span, g, t] = tile[:, t - t0, :]
+                plane.setdefault((span, g, t), []).append((n0, n1, tile[:, t - t0, :]))
             return tile
+
+        def plane_bytes(span, g, t, frames):
+            n0, n1, values = [part for part in plane[span, g, t] if part[0] <= frames.start < part[1]][0]
+            return values[:, frames.start - n0 : frames.stop - n0].bitcast(FP8)
 
         def load(span):
             if span == 0:
-                for g, t0, t1 in HEAD_LOADS:
-                    load_planes(span, g, t0, t1)
+                for g, t0, t1, n0, n1 in HEAD_LOADS:
+                    load_planes(span, g, t0, t1, n0, n1)
             else:
                 for g in range(PASSES):
-                    raw[span, g] = load_planes(span, g, 0, PACK)
+                    raw[span, g] = load_planes(span, g, 0, PACK, 0, SPANS[span])
 
         scale_tile = keep.tile([P, PASSES, 2 * PACK], F32)
         row_scale = scale_tile[:, :, :PACK]
@@ -171,7 +180,7 @@ def tile_fp8_log_mel_d3_kernel(tc, P_bytes, P_scale, W, floor, gain, bias, out):
             for t, frames in share:
                 nc.scalar.activation(
                     out=wide_tile(span, g)[:, t, frames],
-                    in_=plane[span, g, t][:, frames].bitcast(FP8),
+                    in_=plane_bytes(span, g, t, frames),
                     func=ACT.Copy,
                     scale=row_scale[:, g, t : t + 1],
                 )
@@ -180,7 +189,7 @@ def tile_fp8_log_mel_d3_kernel(tc, P_bytes, P_scale, W, floor, gain, bias, out):
             for t, frames in share:
                 nc.vector.tensor_scalar(
                     out=wide_tile(span, g)[:, t, frames],
-                    in0=plane[span, g, t][:, frames].bitcast(FP8),
+                    in0=plane_bytes(span, g, t, frames),
                     scalar1=row_scale[:, g, t : t + 1],
                     scalar2=None,
                     op0=ALU.mult,
@@ -306,19 +315,21 @@ def tile_fp8_log_mel_d3_kernel(tc, P_bytes, P_scale, W, floor, gain, bias, out):
                     logarithm(done)
             widen_on_scalar(c, 1, scalar_share(c))
 
-        whole = slice(0, HEAD[0])
-        widen_on_vector(0, 0, [(t, whole) for t in HEAD_VECTOR[0]])
-        turn_scale()
-        nc.vector.tensor_copy(out=ident_bf16[:], in_=ident_f32[:])
-        widen_on_vector(0, 0, [(t, whole) for t in HEAD_VECTOR[1]])
-        widen_on_vector(0, 1, [(t, whole) for t in HEAD_VECTOR[2]])
-        widen_on_scalar(0, 0, [(t, whole) for t in range(PACK) if t not in HEAD_VECTOR[0] + HEAD_VECTOR[1]])
-        widen_on_scalar(0, 1, [(t, whole) for t in range(PACK) if t not in HEAD_VECTOR[2]])
+        parts = [slice(0, FIRST_PART), slice(FIRST_PART, HEAD[0])]
+        for k, part in enumerate(parts):
+            widen_on_scalar(0, 0, [(t, part) for t in range(PACK - HEAD_PLANES)])
+            widen_on_vector(0, 0, [(t, part) for t in range(PACK - HEAD_PLANES, PACK)])
+            if k == 0:
+                turn_scale()
+                nc.vector.tensor_copy(out=ident_bf16[:], in_=ident_f32[:])
+        widen_on_scalar(0, 1, scalar_share(0))
         turn_scale_back()
         prepare(FIRST)
-        interleave_on_vector(0, 0, 0, HEAD[0])
-        interleave_on_vector(0, 1, 0, HEAD[0])
+        for part in parts:
+            interleave_on_vector(0, 0, part.start, part.stop)
+        widen_on_vector(0, 1, vector_share(0))
         quantize(0, 0)
+        interleave_on_vector(0, 1, 0, HEAD[0])
 
         early_units = [(c, 0) for c in range(LAST + 1, len(CHUNKS))]
         late_units = [(c, 1) for c in range(len(CHUNKS) - LATE_CHUNKS, len(CHUNKS))]

@@ -43,7 +43,8 @@ HEAD_PLANES = 2
 FIRST_PART = 256
 HEAD_LOADS = [(0, 0, 4, 0, FIRST_PART), (0, 0, 4, FIRST_PART, 512), (1, 0, 2, 0, 512), (1, 2, 4, 0, 512)]
 RAMP_PLANES = 2
-VECTOR_FRAMES = 768
+SPLIT_SPANS = [1, 2]
+VECTOR_FRAMES = 736
 FINISH_LAG = 2
 
 
@@ -101,13 +102,15 @@ def tile_fp8_log_mel_d3_kernel(tc, P_bytes, P_scale, W, floor, gain, bias, out):
             n0, n1, values = [part for part in plane[span, g, t] if part[0] <= frames.start < part[1]][0]
             return values[:, frames.start - n0 : frames.stop - n0].bitcast(FP8)
 
-        def load(span):
+        def load(span, between=lambda: None):
             if span == 0:
                 for g, t0, t1, n0, n1 in HEAD_LOADS:
                     load_planes(span, g, t0, t1, n0, n1)
             else:
-                for g in range(PASSES):
-                    raw[span, g] = load_planes(span, g, 0, PACK, 0, SPANS[span])
+                step = PACK // 2 if span in SPLIT_SPANS else PACK
+                raw[span] = [(t, load_planes(span, 0, t, t + step, 0, SPANS[span])) for t in range(0, PACK, step)]
+                between()
+                load_planes(span, 1, 0, PACK, 0, SPANS[span])
 
         scale_tile = keep.tile([P, PASSES, 2 * PACK], F32)
         row_scale = scale_tile[:, :, :PACK]
@@ -115,14 +118,14 @@ def tile_fp8_log_mel_d3_kernel(tc, P_bytes, P_scale, W, floor, gain, bias, out):
         for span in range(FIRST_FULL + 1):
             load(span)
         w_rows = keep.tile([P, F], BF16, align_bytes=64)
-        nc.sync.dma_start(out=w_rows[:], in_=W)
+        load(FIRST_FULL + 1, lambda: nc.sync.dma_start(out=w_rows[:], in_=W))
         floor_col = keep.tile([P, 1], BF16)
         gain_col = keep.tile([P, 1], BF16)
         bias_col = keep.tile([P, 1], BF16)
         nc.sync.dma_start(out=floor_col[:], in_=floor.rearrange("(p o) -> p o", o=1))
         nc.sync.dma_start(out=gain_col[:], in_=gain.rearrange("(p o) -> p o", o=1))
         nc.sync.dma_start(out=bias_col[:], in_=bias.rearrange("(p o) -> p o", o=1))
-        for span in range(FIRST_FULL + 1, len(SPANS)):
+        for span in range(FIRST_FULL + 2, len(SPANS)):
             load(span)
 
         one = keep.tile([P, 1], F32)
@@ -196,10 +199,11 @@ def tile_fp8_log_mel_d3_kernel(tc, P_bytes, P_scale, W, floor, gain, bias, out):
                 )
 
         def cast_first_pass(c):
-            nc.scalar.copy(
-                out=wide_tile(c, 0)[:].rearrange("p t n -> p (t n)"),
-                in_=raw[c, 0][:].rearrange("p t n -> p (t n)").bitcast(FP8),
-            )
+            for t, tile in raw[c]:
+                nc.scalar.copy(
+                    out=wide_tile(c, 0)[:, t : t + tile.shape[1], :].rearrange("p t n -> p (t n)"),
+                    in_=tile[:].rearrange("p t n -> p (t n)").bitcast(FP8),
+                )
 
         def grouped_tile(c, g):
             if (c, g) not in grouped:
@@ -316,17 +320,27 @@ def tile_fp8_log_mel_d3_kernel(tc, P_bytes, P_scale, W, floor, gain, bias, out):
             widen_on_scalar(c, 1, scalar_share(c))
 
         parts = [slice(0, FIRST_PART), slice(FIRST_PART, HEAD[0])]
-        for k, part in enumerate(parts):
-            widen_on_scalar(0, 0, [(t, part) for t in range(PACK - HEAD_PLANES)])
-            widen_on_vector(0, 0, [(t, part) for t in range(PACK - HEAD_PLANES, PACK)])
-            if k == 0:
+        halves = [keep.tile([P, PACK, part.stop - part.start], BF16, name="half_%d" % part.start) for part in parts]
+        for half, part in zip(halves, parts):
+            for t in range(PACK - HEAD_PLANES):
+                nc.scalar.activation(
+                    out=half[:, t, :], in_=plane_bytes(0, 0, t, part), func=ACT.Copy, scale=row_scale[:, 0, t : t + 1]
+                )
+            for t in range(PACK - HEAD_PLANES, PACK):
+                nc.vector.tensor_scalar(
+                    out=half[:, t, :], in0=plane_bytes(0, 0, t, part), scalar1=row_scale[:, 0, t : t + 1], scalar2=None, op0=ALU.mult
+                )
+            if part.start == 0:
                 turn_scale()
                 nc.vector.tensor_copy(out=ident_bf16[:], in_=ident_f32[:])
         widen_on_scalar(0, 1, scalar_share(0))
         turn_scale_back()
         prepare(FIRST)
-        for part in parts:
-            interleave_on_vector(0, 0, part.start, part.stop)
+        for half, part in zip(halves, parts):
+            nc.vector.tensor_copy(
+                out=grouped_tile(0, 0)[:, part, :].rearrange("p (r i) t -> p r t i", i=VECTOR_RUN),
+                in_=half[:].rearrange("p t (r i) -> p r t i", i=VECTOR_RUN),
+            )
         widen_on_vector(0, 1, vector_share(0))
         quantize(0, 0)
         interleave_on_vector(0, 1, 0, HEAD[0])

@@ -26,7 +26,7 @@ POOL_RUN = 2
 
 HEAD = [512]
 RAMP = 512
-TAIL = [512, 256, 128, 128]
+TAIL = [256, 256, 256, 128, 128]
 CHUNKS = HEAD + [RAMP] + [FULL] * ((T - sum(HEAD) - RAMP - sum(TAIL)) // FULL) + TAIL
 FIRST = len(HEAD)
 FIRST_FULL = FIRST + 1
@@ -38,13 +38,17 @@ assert sum(CHUNKS) == T and sum(SPANS) == T
 TENSOR_FRAMES = 40
 POOL_FRAMES = FULL - TENSOR_FRAMES
 RAMP_POOL_FRAMES = 448
-LATE_CHUNKS = 2
+EARLY = [1, 2, 3]
+LATE = [1, 2]
+TAIL_SCALAR = 1
+SCALAR_BANKS = 2
+AHEAD = 2
 HEAD_PLANES = 2
 FIRST_PART = 256
 HEAD_LOADS = [(0, 0, 4, 0, FIRST_PART), (0, 0, 4, FIRST_PART, 512), (1, 0, 2, 0, 512), (1, 2, 4, 0, 512)]
 RAMP_PLANES = 2
 SPLIT_SPANS = [1, 2]
-VECTOR_FRAMES = 736
+VECTOR_FRAMES = 880
 FINISH_LAG = 2
 
 
@@ -81,8 +85,8 @@ def tile_fp8_log_mel_d3_kernel(tc, P_bytes, P_scale, W, floor, gain, bias, out):
         keep = ctx.enter_context(tc.tile_pool(name="keep", bufs=1))
         work = ctx.enter_context(tc.tile_pool(name="work", bufs=4))
         psum_scale = ctx.enter_context(tc.psum_pool(name="psum_scale", bufs=1))
-        psum_moved = ctx.enter_context(tc.psum_pool(name="psum_moved", bufs=2))
-        psum_mel = ctx.enter_context(tc.psum_pool(name="psum_mel", bufs=5))
+        psum_moved = ctx.enter_context(tc.psum_pool(name="psum_moved", bufs=3))
+        psum_mel = ctx.enter_context(tc.psum_pool(name="psum_mel", bufs=4))
         ctx.enter_context(tc.manual_schedule())
 
         p_rows = P_bytes.rearrange("(g p t) n -> g p t n", p=P, t=PACK)
@@ -257,6 +261,26 @@ def tile_fp8_log_mel_d3_kernel(tc, P_bytes, P_scale, W, floor, gain, bias, out):
                 in_=moved[c, g][:].bitcast(F32),
             )
 
+        def bank_on_tensor(b, g):
+            moved[TAIL_SPAN, b, g] = psum_moved.tile([P, BANK_FRAMES * PACK], BF16, name="moved")
+            for n0 in range(0, BANK_FRAMES, BANK // PACK):
+                first = b * BANK_FRAMES + n0
+                nc.tensor.matmul(
+                    out=moved[TAIL_SPAN, b, g][:, n0 * PACK : n0 * PACK + BANK],
+                    lhsT=ident_bf16[:],
+                    rhs=wide[TAIL_SPAN, g][:, :, first : first + BANK // PACK].rearrange("p t n -> p n t"),
+                    start=True,
+                    stop=True,
+                )
+
+        def fetch_bank(b, g):
+            tile = keep.tile([P, BANK_FRAMES, PACK], BF16, name="bank_%d_%d" % (b, g), align_bytes=64)
+            nc.scalar.copy(out=tile[:].rearrange("p n t -> p (n t)").bitcast(F32), in_=moved[TAIL_SPAN, b, g][:].bitcast(F32))
+            for c in range(TAIL_SPAN, len(CHUNKS)):
+                first = chunk_start[c] - chunk_start[TAIL_SPAN] - b * BANK_FRAMES
+                if 0 <= first < BANK_FRAMES:
+                    grouped[c, g] = tile[:, first : first + CHUNKS[c], :]
+
         def quantize(c, g):
             codes[c, g] = work.tile([P, CHUNKS[c]], U32, name="codes", align_bytes=64, bufs=7)
             scales[c, g] = work.tile([P, CHUNKS[c]], U8, name="scales", align_bytes=64, bufs=7)
@@ -269,9 +293,10 @@ def tile_fp8_log_mel_d3_kernel(tc, P_bytes, P_scale, W, floor, gain, bias, out):
         def banks(c):
             return [slice(n0, min(n0 + BANK, CHUNKS[c])) for n0 in range(0, CHUNKS[c], BANK)]
 
-        def multiply(c):
-            mel[c] = [psum_mel.tile([P, cols.stop - cols.start], F32, name="mel") for cols in banks(c)]
-            for g in range(PASSES):
+        def multiply(c, passes=range(PASSES)):
+            if c not in mel:
+                mel[c] = [psum_mel.tile([P, cols.stop - cols.start], F32, name="mel") for cols in banks(c)]
+            for g in passes:
                 for acc, cols in zip(mel[c], banks(c)):
                     nc.tensor.matmul_mx(
                         out=acc[:],
@@ -303,8 +328,8 @@ def tile_fp8_log_mel_d3_kernel(tc, P_bytes, P_scale, W, floor, gain, bias, out):
             )
             store(values, start)
 
-        def finish_on_scalar(c):
-            for cols in banks(c):
+        def finish_on_scalar(c, count=2):
+            for cols in banks(c)[:count]:
                 nc.scalar.activation(
                     out=logs[c][:, cols], in_=logs[c][:, cols], func=ACT.Identity, scale=gain_f32[:], bias=bias_col[:]
                 )
@@ -345,14 +370,6 @@ def tile_fp8_log_mel_d3_kernel(tc, P_bytes, P_scale, W, floor, gain, bias, out):
         quantize(0, 0)
         interleave_on_vector(0, 1, 0, HEAD[0])
 
-        early_units = [(c, 0) for c in range(LAST + 1, len(CHUNKS))]
-        late_units = [(c, 1) for c in range(len(CHUNKS) - LATE_CHUNKS, len(CHUNKS))]
-
-        def fetch_early(k):
-            fetch_from_tensor(*early_units[k])
-            if k + 2 < len(early_units):
-                interleave_on_tensor(*early_units[k + 2])
-
         for c in range(FIRST, LAST + 1):
             widen_on_vector(c, 1, vector_share(c)[1:] if c == FIRST_FULL else vector_share(c))
             if c >= FIRST_FULL:
@@ -370,17 +387,20 @@ def tile_fp8_log_mel_d3_kernel(tc, P_bytes, P_scale, W, floor, gain, bias, out):
             if c >= FIRST_FULL:
                 fetch_from_tensor(c, 1)
             if c == LAST:
-                interleave_on_tensor(*early_units[0])
-                interleave_on_tensor(*early_units[1])
+                for b in EARLY:
+                    bank_on_tensor(b, 0)
                 widen_on_scalar(TAIL_SPAN, 1, scalar_share(TAIL_SPAN))
-                fetch_early(0)
-                fetch_early(1)
+                widen_on_vector(TAIL_SPAN, 1, vector_share(TAIL_SPAN))
+                fetch_bank(EARLY[0], 0)
+                bank_on_tensor(LATE[0], 1)
+                fetch_bank(EARLY[1], 0)
+                for b in LATE[1:]:
+                    bank_on_tensor(b, 1)
                 nc.scalar.copy(out=gain_f32[:], in_=gain_col[:])
             if c > FIRST_FULL:
                 logarithm(c - 1)
             if c == LAST:
-                for k in range(2, len(early_units)):
-                    fetch_early(k)
+                fetch_bank(EARLY[2], 0)
 
             ready = c - FINISH_LAG
             if c == FIRST:
@@ -397,30 +417,30 @@ def tile_fp8_log_mel_d3_kernel(tc, P_bytes, P_scale, W, floor, gain, bias, out):
             quantize(c, 0)
 
         quantize(LAST, 1)
-        widen_on_vector(TAIL_SPAN, 1, vector_share(TAIL_SPAN))
         multiply(LAST)
-        for unit in late_units:
-            interleave_on_tensor(*unit)
-        for c in range(LAST + 1 - FINISH_LAG, LAST):
-            finish_on_scalar(c)
+        finish_on_scalar(LAST - 1)
+        for b in LATE:
+            fetch_bank(b, 1)
         logarithm(LAST)
-        for unit in late_units:
-            fetch_from_tensor(*unit)
-        finish_on_scalar(LAST)
+        finish_on_scalar(LAST, SCALAR_BANKS)
 
         def interleave_rest(c, g):
-            frames = CHUNKS[c] - (tensor_frames(c) if (c, g) in early_units + late_units else 0)
-            if frames:
-                interleave_on_vector(c, g, 0, frames)
+            if (c, g) not in grouped:
+                interleave_on_vector(c, g, 0, CHUNKS[c])
 
         tail_units = [(c, g) for c in range(LAST + 1, len(CHUNKS)) for g in range(PASSES)]
-        interleave_rest(*tail_units[0])
+        for unit in tail_units[:AHEAD]:
+            interleave_rest(*unit)
         for s, (c, g) in enumerate(tail_units):
-            if s + 1 < len(tail_units):
-                interleave_rest(*tail_units[s + 1])
+            if s + AHEAD < len(tail_units):
+                interleave_rest(*tail_units[s + AHEAD])
             quantize(c, g)
             if g == PASSES - 1:
                 multiply(c)
                 logarithm(c)
-        for c in range(LAST + 1, len(CHUNKS)):
+                if LAST + 1 < c <= LAST + 1 + TAIL_SCALAR:
+                    finish_on_scalar(c - 1)
+        for cols in banks(LAST)[SCALAR_BANKS:]:
+            finish_on_vector(logs[LAST][:, cols], chunk_start[LAST] + cols.start)
+        for c in range(LAST + 1 + TAIL_SCALAR, len(CHUNKS)):
             finish_on_vector(logs[c], chunk_start[c])

@@ -37,18 +37,21 @@ assert sum(CHUNKS) == T and sum(SPANS) == T
 
 TENSOR_FRAMES = 40
 POOL_FRAMES = FULL - TENSOR_FRAMES
-RAMP_POOL_FRAMES = 448
+RAMP_POOL_FRAMES = 480
 EARLY = [1, 2, 3]
-LATE = [1, 2]
+LATE = [2]
 TAIL_SCALAR = 1
-SCALAR_BANKS = 2
+BEFORE = 0
+SHIFT = 1
+FETCH_FIRST = 0
+SB = 2
 AHEAD = 2
 HEAD_PLANES = 2
 FIRST_PART = 256
 HEAD_LOADS = [(0, 0, 4, 0, FIRST_PART), (0, 0, 4, FIRST_PART, 512), (1, 0, 2, 0, 512), (1, 2, 4, 0, 512)]
 RAMP_PLANES = 2
 SPLIT_SPANS = [1, 2]
-VECTOR_FRAMES = 880
+VECTOR_FRAMES = 720
 FINISH_LAG = 2
 
 
@@ -328,8 +331,8 @@ def tile_fp8_log_mel_d3_kernel(tc, P_bytes, P_scale, W, floor, gain, bias, out):
             )
             store(values, start)
 
-        def finish_on_scalar(c, count=2):
-            for cols in banks(c)[:count]:
+        def finish_on_scalar(c, parts=None):
+            for cols in parts or banks(c):
                 nc.scalar.activation(
                     out=logs[c][:, cols], in_=logs[c][:, cols], func=ACT.Identity, scale=gain_f32[:], bias=bias_col[:]
                 )
@@ -391,16 +394,15 @@ def tile_fp8_log_mel_d3_kernel(tc, P_bytes, P_scale, W, floor, gain, bias, out):
                     bank_on_tensor(b, 0)
                 widen_on_scalar(TAIL_SPAN, 1, scalar_share(TAIL_SPAN))
                 widen_on_vector(TAIL_SPAN, 1, vector_share(TAIL_SPAN))
-                fetch_bank(EARLY[0], 0)
-                bank_on_tensor(LATE[0], 1)
-                fetch_bank(EARLY[1], 0)
-                for b in LATE[1:]:
-                    bank_on_tensor(b, 1)
                 nc.scalar.copy(out=gain_f32[:], in_=gain_col[:])
             if c > FIRST_FULL:
                 logarithm(c - 1)
             if c == LAST:
-                fetch_bank(EARLY[2], 0)
+                fetch_bank(EARLY[0], 0)
+                for b in LATE[:BEFORE]:
+                    bank_on_tensor(b, 1)
+                finish_on_scalar(LAST - 1)
+                fetch_bank(EARLY[1], 0)
 
             ready = c - FINISH_LAG
             if c == FIRST:
@@ -412,17 +414,25 @@ def tile_fp8_log_mel_d3_kernel(tc, P_bytes, P_scale, W, floor, gain, bias, out):
                     multiply(done)
             elif ready < FIRST_FULL:
                 finish_on_vector(head_logs[:], 0)
-            else:
+            elif c < LAST:
                 finish_on_vector(logs[ready], chunk_start[ready])
+            elif SHIFT < 2:
+                finish_on_vector(logs[ready][:, SHIFT * BANK :], chunk_start[ready] + SHIFT * BANK)
             quantize(c, 0)
 
         quantize(LAST, 1)
         multiply(LAST)
-        finish_on_scalar(LAST - 1)
-        for b in LATE:
-            fetch_bank(b, 1)
+        for b in LATE[BEFORE:]:
+            bank_on_tensor(b, 1)
+        fetch_bank(EARLY[2], 0)
+        if SHIFT:
+            finish_on_scalar(LAST - 2, banks(LAST - 2)[:SHIFT])
         logarithm(LAST)
-        finish_on_scalar(LAST, SCALAR_BANKS)
+        if not FETCH_FIRST:
+            finish_on_scalar(LAST, banks(LAST)[:1])
+        for b in LATE[BEFORE:]:
+            fetch_bank(b, 1)
+        finish_on_scalar(LAST, banks(LAST)[1 - FETCH_FIRST : SB])
 
         def interleave_rest(c, g):
             if (c, g) not in grouped:
@@ -440,7 +450,7 @@ def tile_fp8_log_mel_d3_kernel(tc, P_bytes, P_scale, W, floor, gain, bias, out):
                 logarithm(c)
                 if LAST + 1 < c <= LAST + 1 + TAIL_SCALAR:
                     finish_on_scalar(c - 1)
-        for cols in banks(LAST)[SCALAR_BANKS:]:
+        for cols in banks(LAST)[SB:]:
             finish_on_vector(logs[LAST][:, cols], chunk_start[LAST] + cols.start)
         for c in range(LAST + 1 + TAIL_SCALAR, len(CHUNKS)):
             finish_on_vector(logs[c], chunk_start[c])

from contextlib import ExitStack

import concourse.mybir as mybir
from concourse.masks import make_identity

F, T, N = 1024, 8192, 128
FLOPS = 2 * F * T * N

F32 = mybir.dt.float32
BF16 = mybir.dt.bfloat16
U32 = mybir.dt.uint32
U8 = mybir.dt.uint8
FP8 = mybir.dt.float8_e4m3fn
FP8X4 = mybir.dt.float8_e4m3fn_x4
ACT = mybir.ActivationFunctionType
ALU = mybir.AluOpType

P = 128
PACK = 4
PASSES = F // (P * PACK)
BANK = 512
BANK_FRAMES = 2 * BANK // PACK
FULL = 1024
VECTOR_RUN = 2
POOL_RUN = 2

HEAD = [512]
RAMP = 512
TAIL = [256, 256, 256, 128, 128]
CHUNKS = HEAD + [RAMP] + [FULL] * ((T - sum(HEAD) - RAMP - sum(TAIL)) // FULL) + TAIL
FIRST = len(HEAD)
FIRST_FULL = FIRST + 1
LAST = len(CHUNKS) - len(TAIL) - 1
SPANS = CHUNKS[: LAST + 1] + [sum(TAIL)]
TAIL_SPAN = LAST + 1
assert sum(CHUNKS) == T and sum(SPANS) == T

TENSOR_FRAMES = 40
POOL_FRAMES = FULL - TENSOR_FRAMES
RAMP_POOL_FRAMES = 480
EARLY = [1, 2, 3]
LATE = [2]
TAIL_SCALAR = 1
BEFORE = 0
SHIFT = 1
FETCH_FIRST = 0
SB = 2
AHEAD = 2
HEAD_PLANES = 2
FIRST_PART = 256
HEAD_LOADS = [(0, 0, 4, 0, FIRST_PART), (0, 0, 4, FIRST_PART, 512), (1, 0, 2, 0, 512), (1, 2, 4, 0, 512)]
RAMP_PLANES = 2
SPLIT_SPANS = [1, 2]
VECTOR_FRAMES = 720
FINISH_LAG = 2


def vector_share(span):
    if span == FIRST:
        return [(t, slice(0, SPANS[span])) for t in range(PACK - RAMP_PLANES, PACK)]
    if span <= FIRST_FULL:
        return [(t, slice(0, SPANS[span])) for t in range(PACK - HEAD_PLANES, PACK)]
    return [(PACK - 1, slice(0, VECTOR_FRAMES if span <= LAST else SPANS[span]))]


def scalar_share(span):
    if span == FIRST:
        return [(t, slice(0, SPANS[span])) for t in range(PACK - RAMP_PLANES)]
    if span <= FIRST_FULL:
        return [(t, slice(0, SPANS[span])) for t in range(PACK - HEAD_PLANES)]
    rest = [(PACK - 1, slice(VECTOR_FRAMES, FULL))] if span <= LAST else []
    return [(t, slice(0, SPANS[span])) for t in range(PACK - 1)] + rest


def tensor_frames(c):
    return TENSOR_FRAMES if c <= LAST else min(CHUNKS[c], BANK_FRAMES)


def pool_frames(c):
    return RAMP_POOL_FRAMES if c == FIRST else POOL_FRAMES


def tile_fp8_log_mel_d3_kernel(tc, P_bytes, P_scale, W, floor, gain, bias, out):
    nc = tc.nc
    chunk_start = [sum(CHUNKS[:c]) for c in range(len(CHUNKS))]

    with ExitStack() as ctx:
        keep = ctx.enter_context(tc.tile_pool(name="keep", bufs=1))
        work = ctx.enter_context(tc.tile_pool(name="work", bufs=4))
        psum_scale = ctx.enter_context(tc.psum_pool(name="psum_scale", bufs=1))
        psum_moved = ctx.enter_context(tc.psum_pool(name="psum_moved", bufs=3))
        psum_mel = ctx.enter_context(tc.psum_pool(name="psum_mel", bufs=4))
        ctx.enter_context(tc.manual_schedule())

        p_rows = P_bytes.rearrange("(g p t) n -> g p t n", p=P, t=PACK)
        raw = {}

        plane = {}

        def load_planes(span, g, t0, t1, n0, n1):
            start = chunk_start[span]
            tile = keep.tile([P, t1 - t0, n1 - n0], U8, name="p_bytes_%d_%d_%d_%d" % (span, g, t0, n0))
            nc.sync.dma_start(out=tile[:], in_=p_rows[g][:, t0:t1, start + n0 : start + n1])
            for t in range(t0, t1):
                plane.setdefault((span, g, t), []).append((n0, n1, tile[:, t - t0, :]))
            return tile

        def plane_bytes(span, g, t, frames):
            n0, n1, values = [part for part in plane[span, g, t] if part[0] <= frames.start < part[1]][0]
            return values[:, frames.start - n0 : frames.stop - n0].bitcast(FP8)

        def load(span, between=lambda: None):
            if span == 0:
                for g, t0, t1, n0, n1 in HEAD_LOADS:
                    load_planes(span, g, t0, t1, n0, n1)
            else:
                step = PACK // 2 if span in SPLIT_SPANS else PACK
                raw[span] = [(t, load_planes(span, 0, t, t + step, 0, SPANS[span])) for t in range(0, PACK, step)]
                between()
                load_planes(span, 1, 0, PACK, 0, SPANS[span])

        scale_tile = keep.tile([P, PASSES, 2 * PACK], F32)
        row_scale = scale_tile[:, :, :PACK]
        nc.scalar.dma_start(out=row_scale, in_=P_scale.rearrange("(g p t) o -> p g (t o)", p=P, t=PACK))
        for span in range(FIRST_FULL + 1):
            load(span)
        w_rows = keep.tile([P, F], BF16, align_bytes=64)
        load(FIRST_FULL + 1, lambda: nc.sync.dma_start(out=w_rows[:], in_=W))
        floor_col = keep.tile([P, 1], BF16)
        gain_col = keep.tile([P, 1], BF16)
        bias_col = keep.tile([P, 1], BF16)
        nc.sync.dma_start(out=floor_col[:], in_=floor.rearrange("(p o) -> p o", o=1))
        nc.sync.dma_start(out=gain_col[:], in_=gain.rearrange("(p o) -> p o", o=1))
        nc.sync.dma_start(out=bias_col[:], in_=bias.rearrange("(p o) -> p o", o=1))
        for span in range(FIRST_FULL + 2, len(SPANS)):
            load(span)

        one = keep.tile([P, 1], F32)
        warm = keep.tile([P, 1], F32)
        nc.vector.memset(one[:], 1.0)
        nc.scalar.activation(out=warm[:], in_=one[:], func=ACT.Ln)

        ident_f32 = keep.tile([P, P], F32)
        nc.vector.memset(ident_f32[:], 0.0)
        make_identity(nc, ident_f32[:], nomemset=True)
        ident_bf16 = keep.tile([P, P], BF16)

        repeats = P // (PACK * VECTOR_RUN)
        scale_rows = keep.tile([P, repeats, PACK, VECTOR_RUN], F32)
        scale_cols = keep.tile([P, P], F32)
        scale_turned = psum_moved.tile([P, P], F32, name="moved")
        scale_bank = psum_scale.tile([P, repeats, PACK, VECTOR_RUN], F32, name="scale_bank")

        def turn_scale():
            nc.vector.tensor_copy(
                out=scale_rows[:],
                in_=row_scale[:, 0, :].unsqueeze(1).unsqueeze(3).to_broadcast([P, repeats, PACK, VECTOR_RUN]),
            )
            nc.tensor.transpose(scale_turned[:], scale_rows[:].rearrange("p r t i -> p (r t i)"), ident_f32[:])

        def turn_scale_back():
            nc.scalar.copy(out=scale_cols[:], in_=scale_turned[:])
            nc.tensor.transpose(scale_bank[:].rearrange("p r t i -> p (r t i)"), scale_cols[:], ident_f32[:])

        w_codes = keep.tile([P, PASSES * N], U32, align_bytes=64)
        w_scales = keep.tile([P, PASSES * N], U8, align_bytes=64)
        w_grouped = keep.tile([P, PASSES * N * PACK], BF16, align_bytes=64)
        gain_f32 = keep.tile([P, 1], F32)

        def turn_w():
            pairs = w_rows[:].bitcast(F32)
            per_pass = P * PACK // 2
            turned = psum_moved.tile([P, PASSES, 2, N], F32, name="moved")
            for g in range(PASSES):
                for h in range(2):
                    nc.tensor.transpose(turned[:, g, h, :], pairs[:, per_pass * g + h : per_pass * (g + 1) : 2], ident_f32[:])
            nc.scalar.copy(
                out=w_grouped[:].bitcast(F32).rearrange("p (g m h) -> p g m h", g=PASSES, h=2),
                in_=turned[:].rearrange("p g h m -> p g m h"),
            )

        wide, grouped, moved, codes, scales, mel, logs = {}, {}, {}, {}, {}, {}, {}

        def wide_tile(span, g):
            if (span, g) not in wide:
                wide[span, g] = work.tile([P, PACK, SPANS[span]], BF16, name="wide", bufs=5)
            return wide[span, g]

        def widen_on_scalar(span, g, share):
            for t, frames in share:
                nc.scalar.activation(
                    out=wide_tile(span, g)[:, t, frames],
                    in_=plane_bytes(span, g, t, frames),
                    func=ACT.Copy,
                    scale=row_scale[:, g, t : t + 1],
                )

        def widen_on_vector(span, g, share):
            for t, frames in share:
                nc.vector.tensor_scalar(
                    out=wide_tile(span, g)[:, t, frames],
                    in0=plane_bytes(span, g, t, frames),
                    scalar1=row_scale[:, g, t : t + 1],
                    scalar2=None,
                    op0=ALU.mult,
                )

        def cast_first_pass(c):
            for t, tile in raw[c]:
                nc.scalar.copy(
                    out=wide_tile(c, 0)[:, t : t + tile.shape[1], :].rearrange("p t n -> p (t n)"),
                    in_=tile[:].rearrange("p t n -> p (t n)").bitcast(FP8),
                )

        def grouped_tile(c, g):
            if (c, g) not in grouped:
                if c <= LAST:
                    grouped[c, g] = work.tile([P, CHUNKS[c], PACK], BF16, name="grouped", align_bytes=64)
                else:
                    grouped[c, g] = keep.tile([P, CHUNKS[c], PACK], BF16, name="grouped_%d_%d" % (c, g), align_bytes=64)
            return grouped[c, g]

        def planes_of(c, g, n0, n1):
            span = min(c, TAIL_SPAN)
            first = chunk_start[c] - chunk_start[span]
            return wide[span, g][:, :, first + n0 : first + n1]

        def in_runs(c, g, n0, n1, run):
            return (
                grouped_tile(c, g)[:, n0:n1, :].rearrange("p (r i) t -> p r t i", i=run),
                planes_of(c, g, n0, n1).rearrange("p t (r i) -> p r t i", i=run),
            )

        def interleave_on_vector(c, g, n0, n1):
            target, source = in_runs(c, g, n0, n1, VECTOR_RUN)
            nc.vector.tensor_copy(out=target, in_=source)

        def scale_and_interleave(c):
            target, source = in_runs(c, 0, 0, CHUNKS[c], VECTOR_RUN)
            factor = scale_bank[:].rearrange("p r t i -> p (r t i)").unsqueeze(1).to_broadcast([P, CHUNKS[c] * PACK // P, P])
            nc.vector.tensor_tensor(out=target, in0=source, in1=factor, op=ALU.mult)

        def interleave_on_pool(c):
            target, source = in_runs(c, 1, 0, pool_frames(c), POOL_RUN)
            nc.gpsimd.tensor_scalar(out=target, in0=source, scalar1=1.0, scalar2=0.0, op0=ALU.mult, op1=ALU.add)

        def interleave_on_tensor(c, g):
            frames = tensor_frames(c)
            first = CHUNKS[c] - frames
            moved[c, g] = psum_moved.tile([P, frames * PACK], BF16, name="moved")
            for n0 in range(0, frames, BANK // PACK):
                n1 = min(n0 + BANK // PACK, frames)
                nc.tensor.matmul(
                    out=moved[c, g][:, n0 * PACK : n1 * PACK],
                    lhsT=ident_bf16[:],
                    rhs=planes_of(c, g, first + n0, first + n1).rearrange("p t n -> p n t"),
                    start=True,
                    stop=True,
                )

        def fetch_from_tensor(c, g):
            nc.scalar.copy(
                out=grouped_tile(c, g)[:, CHUNKS[c] - tensor_frames(c) :, :].rearrange("p n t -> p (n t)").bitcast(F32),
                in_=moved[c, g][:].bitcast(F32),
            )

        def bank_on_tensor(b, g):
            moved[TAIL_SPAN, b, g] = psum_moved.tile([P, BANK_FRAMES * PACK], BF16, name="moved")
            for n0 in range(0, BANK_FRAMES, BANK // PACK):
                first = b * BANK_FRAMES + n0
                nc.tensor.matmul(
                    out=moved[TAIL_SPAN, b, g][:, n0 * PACK : n0 * PACK + BANK],
                    lhsT=ident_bf16[:],
                    rhs=wide[TAIL_SPAN, g][:, :, first : first + BANK // PACK].rearrange("p t n -> p n t"),
                    start=True,
                    stop=True,
                )

        def fetch_bank(b, g):
            tile = keep.tile([P, BANK_FRAMES, PACK], BF16, name="bank_%d_%d" % (b, g), align_bytes=64)
            nc.scalar.copy(out=tile[:].rearrange("p n t -> p (n t)").bitcast(F32), in_=moved[TAIL_SPAN, b, g][:].bitcast(F32))
            for c in range(TAIL_SPAN, len(CHUNKS)):
                first = chunk_start[c] - chunk_start[TAIL_SPAN] - b * BANK_FRAMES
                if 0 <= first < BANK_FRAMES:
                    grouped[c, g] = tile[:, first : first + CHUNKS[c], :]

        def quantize(c, g):
            codes[c, g] = work.tile([P, CHUNKS[c]], U32, name="codes", align_bytes=64, bufs=7)
            scales[c, g] = work.tile([P, CHUNKS[c]], U8, name="scales", align_bytes=64, bufs=7)
            nc.vector.quantize_mx(
                out=codes[c, g][:].bitcast(FP8X4),
                scales=scales[c, g][:],
                in_=grouped[c, g][:].rearrange("p n t -> p (n t)"),
            )

        def banks(c):
            return [slice(n0, min(n0 + BANK, CHUNKS[c])) for n0 in range(0, CHUNKS[c], BANK)]

        def multiply(c, passes=range(PASSES)):
            if c not in mel:
                mel[c] = [psum_mel.tile([P, cols.stop - cols.start], F32, name="mel") for cols in banks(c)]
            for g in passes:
                for acc, cols in zip(mel[c], banks(c)):
                    nc.tensor.matmul_mx(
                        out=acc[:],
                        lhsT=w_codes[:, g * N : (g + 1) * N].bitcast(FP8X4),
                        lhsT_scale=w_scales[:, g * N : (g + 1) * N],
                        rhs=codes[c, g][:, cols].bitcast(FP8X4),
                        rhs_scale=scales[c, g][:, cols],
                        start=(g == 0),
                        stop=(g == PASSES - 1),
                    )

        head_logs = keep.tile([P, chunk_start[FIRST_FULL]], F32)

        def logarithm(c):
            if c < FIRST_FULL:
                logs[c] = head_logs[:, chunk_start[c] : chunk_start[c] + CHUNKS[c]]
            else:
                tile = keep.tile([P, CHUNKS[c]], F32, name="logs_%d" % c)
                logs[c] = tile[:]
            for acc, cols in zip(mel[c], banks(c)):
                nc.scalar.activation(out=logs[c][:, cols], in_=acc[:], func=ACT.Ln, bias=floor_col[:])

        def store(values, start):
            nc.sync.dma_start(out=out[:, start : start + values.shape[1]], in_=values)

        def finish_on_vector(values, start):
            nc.vector.tensor_scalar(
                out=values, in0=values, scalar1=gain_col[:], scalar2=bias_col[:], op0=ALU.mult, op1=ALU.add
            )
            store(values, start)

        def finish_on_scalar(c, parts=None):
            for cols in parts or banks(c):
                nc.scalar.activation(
                    out=logs[c][:, cols], in_=logs[c][:, cols], func=ACT.Identity, scale=gain_f32[:], bias=bias_col[:]
                )
                store(logs[c][:, cols], chunk_start[c] + cols.start)

        def prepare(c):
            cast_first_pass(c)
            if c == FIRST_FULL + 1:
                turn_w()
            if c == FIRST_FULL + 2:
                for done in range(FIRST_FULL):
                    logarithm(done)
            widen_on_scalar(c, 1, scalar_share(c))

        parts = [slice(0, FIRST_PART), slice(FIRST_PART, HEAD[0])]
        halves = [keep.tile([P, PACK, part.stop - part.start], BF16, name="half_%d" % part.start) for part in parts]
        for half, part in zip(halves, parts):
            for t in range(PACK - HEAD_PLANES):
                nc.scalar.activation(
                    out=half[:, t, :], in_=plane_bytes(0, 0, t, part), func=ACT.Copy, scale=row_scale[:, 0, t : t + 1]
                )
            for t in range(PACK - HEAD_PLANES, PACK):
                nc.vector.tensor_scalar(
                    out=half[:, t, :], in0=plane_bytes(0, 0, t, part), scalar1=row_scale[:, 0, t : t + 1], scalar2=None, op0=ALU.mult
                )
            if part.start == 0:
                turn_scale()
                nc.vector.tensor_copy(out=ident_bf16[:], in_=ident_f32[:])
        widen_on_scalar(0, 1, scalar_share(0))
        turn_scale_back()
        prepare(FIRST)
        for half, part in zip(halves, parts):
            nc.vector.tensor_copy(
                out=grouped_tile(0, 0)[:, part, :].rearrange("p (r i) t -> p r t i", i=VECTOR_RUN),
                in_=half[:].rearrange("p t (r i) -> p r t i", i=VECTOR_RUN),
            )
        widen_on_vector(0, 1, vector_share(0))
        quantize(0, 0)
        interleave_on_vector(0, 1, 0, HEAD[0])

        for c in range(FIRST, LAST + 1):
            widen_on_vector(c, 1, vector_share(c)[1:] if c == FIRST_FULL else vector_share(c))
            if c >= FIRST_FULL:
                interleave_on_tensor(c, 1)
            interleave_on_pool(c)
            quantize(c - 1, 1)
            if c > FIRST_FULL:
                multiply(c - 1)
            scale_and_interleave(c)

            if c < LAST:
                prepare(c + 1)
            else:
                widen_on_scalar(TAIL_SPAN, 0, [(t, slice(0, SPANS[TAIL_SPAN])) for t in range(PACK)])
            if c >= FIRST_FULL:
                fetch_from_tensor(c, 1)
            if c == LAST:
                for b in EARLY:
                    bank_on_tensor(b, 0)
                widen_on_scalar(TAIL_SPAN, 1, scalar_share(TAIL_SPAN))
                widen_on_vector(TAIL_SPAN, 1, vector_share(TAIL_SPAN))
                nc.scalar.copy(out=gain_f32[:], in_=gain_col[:])
            if c > FIRST_FULL:
                logarithm(c - 1)
            if c == LAST:
                fetch_bank(EARLY[0], 0)
                for b in LATE[:BEFORE]:
                    bank_on_tensor(b, 1)
                finish_on_scalar(LAST - 1)
                fetch_bank(EARLY[1], 0)

            ready = c - FINISH_LAG
            if c == FIRST:
                widen_on_vector(c + 1, 1, vector_share(c + 1)[:1])
                interleave_on_vector(c, 1, pool_frames(c), CHUNKS[c])
            elif c == FIRST_FULL:
                nc.vector.quantize_mx(out=w_codes[:].bitcast(FP8X4), scales=w_scales[:], in_=w_grouped[:])
                for done in range(FIRST_FULL):
                    multiply(done)
            elif ready < FIRST_FULL:
                finish_on_vector(head_logs[:], 0)
            elif c < LAST:
                finish_on_vector(logs[ready], chunk_start[ready])
            elif SHIFT < 2:
                finish_on_vector(logs[ready][:, SHIFT * BANK :], chunk_start[ready] + SHIFT * BANK)
            quantize(c, 0)

        quantize(LAST, 1)
        multiply(LAST)
        for b in LATE[BEFORE:]:
            bank_on_tensor(b, 1)
        fetch_bank(EARLY[2], 0)
        if SHIFT:
            finish_on_scalar(LAST - 2, banks(LAST - 2)[:SHIFT])
        logarithm(LAST)
        if not FETCH_FIRST:
            finish_on_scalar(LAST, banks(LAST)[:1])
        for b in LATE[BEFORE:]:
            fetch_bank(b, 1)
        finish_on_scalar(LAST, banks(LAST)[1 - FETCH_FIRST : SB])

        def interleave_rest(c, g):
            if (c, g) not in grouped:
                interleave_on_vector(c, g, 0, CHUNKS[c])

        tail_units = [(c, g) for c in range(LAST + 1, len(CHUNKS)) for g in range(PASSES)]
        for unit in tail_units[:AHEAD]:
            interleave_rest(*unit)
        for s, (c, g) in enumerate(tail_units):
            if s + AHEAD < len(tail_units):
                interleave_rest(*tail_units[s + AHEAD])
            quantize(c, g)
            if g == PASSES - 1:
                multiply(c)
                logarithm(c)
                if LAST + 1 < c <= LAST + 1 + TAIL_SCALAR:
                    finish_on_scalar(c - 1)
        for cols in banks(LAST)[SB:]:
            finish_on_vector(logs[LAST][:, cols], chunk_start[LAST] + cols.start)
        for c in range(LAST + 1 + TAIL_SCALAR, len(CHUNKS)):
            finish_on_vector(logs[c], chunk_start[c])
